import numpy as np
import ml_dtypes


def mxq(x, axis, fmt="e4m3"):
    dtype, down = {"e4m3": (ml_dtypes.float8_e4m3fn, 7), "e5m2": (ml_dtypes.float8_e5m2, 14)}[fmt]
    v = np.moveaxis(np.asarray(x, np.float32).astype(ml_dtypes.bfloat16).astype(np.float64), axis, -1)
    blocks = v.reshape(v.shape[:-1] + (-1, 32))
    amax = np.abs(blocks).max(-1, keepdims=True)
    byte = np.maximum(np.where(amax > 0, np.frexp(amax)[1] - 1 + 127, 0) - down, 1)
    scale = np.exp2(byte - 127.0)
    codes = (blocks / scale).astype(np.float32).astype(dtype).astype(np.float64)
    return np.moveaxis((codes * scale).reshape(v.shape), -1, axis)


WIDE = False


def mx_kscale(k):
    if not WIDE:
        return np.ones(k)
    levels = np.array([24, -24, 12, -12, 0])
    if k % 512:
        return np.exp2(np.random.permutation(np.resize(levels, k // 32))).repeat(32)
    a = np.empty((k // 512, 16))
    for p in range(k // 512):
        a[p, :8] = np.random.permutation(np.resize(levels, 8))
        for g in range(8):
            far = levels[np.abs(levels - a[p, g]) >= 10]
            a[p, g + 8] = far[np.random.randint(len(far))]
    return np.exp2(a.ravel()).repeat(32)


def f64(x):
    return np.asarray(x).astype(np.float64)


def striped8(idx):
    return np.concatenate([v.reshape(-1, 16).T for v in idx]).astype(np.uint16)


def unstriped8(offs):
    return np.stack([offs[16 * g:16 * g + 16].T.reshape(-1) for g in range(8)]).astype(np.int64)


E2M1 = np.array([0.0, 0.5, 1.0, 1.5, 2.0, 3.0, 4.0, 6.0, -0.0, -0.5, -1.0, -1.5, -2.0, -3.0, -4.0, -6.0])


def pack_weight(w, fmt):
    k, n = w.shape
    w = f64(np.asarray(w, np.float32).astype(ml_dtypes.bfloat16)).reshape(k // 32, 32, n)
    amax = np.abs(w).max(1)
    if fmt == "e4m3":
        byte = np.frexp(amax)[1] - 1 + 127 - 7
    else:
        mant, ex = np.frexp(amax / 6.0)
        byte = np.where(mant > 0.5, ex, ex - 1) + 127
    byte = np.clip(np.where(amax > 0, byte, 1), 1, 254)
    scaled = (w * np.exp2(127.0 - byte)[:, None, :]).reshape(k, n).astype(np.float32)
    by_word = np.ascontiguousarray(scaled.reshape(k // 512, 128, 4, n).transpose(0, 1, 3, 2))
    if fmt == "e4m3":
        words = by_word.astype(ml_dtypes.float8_e4m3fn).view(np.uint8)
    else:
        c = by_word.astype(ml_dtypes.float4_e2m1fn).view(np.uint8) & 0xF
        words = (c[..., 0::2] | (c[..., 1::2] << 4)).reshape(k // 512, 128, 2 * n)
    return np.ascontiguousarray(words), np.ascontiguousarray(byte.astype(np.uint8).reshape(k // 512, 16, n))


def unpack_weight(words, scales, fmt):
    g, _, n = scales.shape
    words = np.ascontiguousarray(words).reshape(g, 128, n, -1)
    if fmt == "e4m3":
        vals = words.view(ml_dtypes.float8_e4m3fn).astype(np.float64)
    else:
        nib = np.empty((g, 128, n, 4), np.uint8)
        nib[..., 0::2] = words & 0xF
        nib[..., 1::2] = words >> 4
        vals = E2M1[nib]
    vals = vals * np.repeat(np.exp2(scales.astype(np.float64) - 127.0), 8, axis=1)[..., None]
    return vals.transpose(0, 1, 3, 2).reshape(g * 512, n)


def gelu(f):
    return 0.5 * f * (1.0 + np.tanh(np.sqrt(2.0 / np.pi) * (f + 0.044715 * f**3)))


K, R, N, T, J = 1024, 1024, 512, 2048, 1024


def setup_inputs():
    n = np.random.standard_normal
    s = mx_kscale(K)[:, None]
    u = mx_kscale(R)[:, None]
    p_wg = pack_weight(n((K, R)) / np.sqrt(K) / s, "e4m3")
    p_wu = pack_weight(n((K, R)) / np.sqrt(K) / s * u.T, "e4m3")
    p_wd = pack_weight(n((R, N)) / np.sqrt(R) / u, "e2m1")
    return {
        "xT": (n((K, T)) * s).astype(np.float32),
        "wgt": np.repeat(np.random.uniform(0.5, 2.0, (8, J)), 16, axis=0).astype(np.float32),
        "wg_words": p_wg[0],
        "wg_scales": p_wg[1],
        "wu_words": p_wu[0],
        "wu_scales": p_wu[1],
        "wd_words": p_wd[0],
        "wd_scales": p_wd[1],
        "wgo": np.repeat(np.random.uniform(0.5, 2.0, (8, J)), 16, axis=0).astype(np.float32),
        "offs": striped8(np.stack([np.random.permutation(T)[:J] for _ in range(8)])),
        "offs2": striped8(np.stack([np.random.permutation(T)[:J] for _ in range(8)])),
    }


def reference(xT, wgt, wg_words, wg_scales, wu_words, wu_scales, wd_words, wd_scales, wgo, offs, offs2):
    idx = unstriped8(offs)
    idx2 = unstriped8(offs2)
    rows = np.arange(K)
    xg = f64(wgt)[rows // 4 % 128] * f64(xT)[rows[:, None], idx[rows % 512 // 64]]
    xT_ = mxq(xg, 0, "e4m3")
    wg_ = unpack_weight(wg_words, wg_scales, "e4m3")
    wu_ = unpack_weight(wu_words, wu_scales, "e4m3")
    ga = wg_.T @ xT_
    ub = wu_.T @ xT_
    h = gelu(ga) * ub
    h_ = mxq(h, 0, "e4m3")
    wd_ = unpack_weight(wd_words, wd_scales, "e2m1")
    y = wd_.T @ h_
    out = np.zeros((N, T))
    rows = np.arange(N)
    out[rows[:, None], idx2[rows % 128 // 16]] = f64(wgo)[rows % 128] * (y)
    return out

@@ -1,0 +1,207 @@
+from contextlib import ExitStack
+
+import concourse.mybir as mybir
+
+K, R, N, T, J = 1024, 1024, 512, 2048, 1024
+FLOPS = 2 * J * (2 * K * R + R * N)
+
+F32 = mybir.dt.float32
+BF16 = mybir.dt.bfloat16
+I32 = mybir.dt.int32
+U32 = mybir.dt.uint32
+U16 = mybir.dt.uint16
+U8 = mybir.dt.uint8
+FP8X4 = mybir.dt.float8_e4m3fn_x4
+FP4X4 = mybir.dt.float4_e2m1fn_x4
+MULT = mybir.AluOpType.mult
+GELU = mybir.ActivationFunctionType.Gelu_apprx_tanh
+
+P = 128
+PACK = 4
+HALF = 512
+TOK = 128
+PER_COL = 16
+
+
+def tile_list_gelu_scat_kernel(tc, xT, wgt, wg_words, wg_scales, wu_words, wu_scales, wd_words, wd_scales, wgo, offs, offs2, out):
+    nc = tc.nc
+    with ExitStack() as ctx:
+        keep = ctx.enter_context(tc.tile_pool(name="keep", bufs=1))
+        ring = ctx.enter_context(tc.tile_pool(name="ring", bufs=3))
+        stage = ctx.enter_context(tc.tile_pool(name="stage", bufs=4))
+        ps1 = ctx.enter_context(tc.psum_pool(name="ps1", bufs=3))
+        ps2 = ctx.enter_context(tc.psum_pool(name="ps2", bufs=2))
+
+        pick = keep.tile([P, J // PER_COL], U16, name="pick")
+        place = keep.tile([P, J // PER_COL], U16, name="place")
+        wgt_sb = [keep.tile([P, HALF], F32, name=f"wgt{h}") for h in range(2)]
+        wgo_sb = keep.tile([P, J], F32, name="wgo_sb")
+        x_sb = [[keep.tile([P, T], F32, name=f"x{a}{i}") for i in range(PACK)] for a in range(2)]
+        x_rows = xT.rearrange("(a p i) t -> a i p t", a=2, i=PACK)
+
+        warm = keep.tile([P, 8], F32, name="warm")
+        warm2 = keep.tile([P, 8], F32, name="warm2")
+        nc.gpsimd.memset(warm[:], 0.0)
+        nc.scalar.activation(warm2[:], warm[:], GELU)
+
+        win = [keep.tile([P, T], F32, name=f"win{n}") for n in range(N // P)]
+        sc_raw = keep.tile([P, R], U8, name="sc_raw", align_bytes=64)
+        wd_sc = keep.tile([P, 2, N], U8, name="wd_sc", align_bytes=64)
+        nc.vector.memset(sc_raw[:].bitcast(I32), 0)
+        nc.vector.memset(wd_sc[:].bitcast(I32), 0)
+        for n in range(N // P):
+            nc.vector.memset(win[n][:], 0.0)
+
+        nc.sync.dma_start(pick[:], offs)
+        nc.sync.dma_start(out=wgt_sb[0][:], in_=wgt[:, 0:HALF])
+        nc.sync.dma_start(out=x_sb[0][0][:], in_=x_rows[0, 0])
+        nc.sync.dma_start(out=wgt_sb[1][:], in_=wgt[:, HALF:J])
+        nc.sync.dma_start(out=x_sb[0][1][:], in_=x_rows[0, 1])
+        for m, scales in enumerate((wg_scales, wu_scales)):
+            for q in range(4):
+                lo = 32 * q + 8 * m
+                nc.scalar.dma_start(out=sc_raw[lo:lo + 8, :].bitcast(I32), in_=scales[:, 4 * q:4 * q + 4, :].bitcast(I32))
+        for a in range(2):
+            for i in range(PACK):
+                if PACK * a + i > 1:
+                    nc.sync.dma_start(out=x_sb[a][i][:], in_=x_rows[a, i])
+        w_raw = {}
+        for b in range(2):
+            for m, words in enumerate((wg_words, wu_words)):
+                w_raw[m, b] = keep.tile([P, 2, 512], I32, name=f"w_raw{m}{b}")
+                src = words.rearrange("a p r i -> p a (r i)")[:, :, 2048 * b:2048 * (b + 1)]
+                nc.sync.dma_start(out=w_raw[m, b][:], in_=src.bitcast(I32))
+        wd_sb = keep.tile([P, 2, 2 * N], U8, name="wd_sb", align_bytes=64)
+        nc.sync.dma_start(out=wd_sb[:].bitcast(I32), in_=wd_words.rearrange("a p c -> p a c").bitcast(I32))
+        for q in range(4):
+            nc.sync.dma_start(out=wd_sc[32 * q:32 * q + 4, :, :].bitcast(I32),
+                              in_=wd_scales[:, 4 * q:4 * q + 4, :].rearrange("a q n -> q a n").bitcast(I32))
+        nc.sync.dma_start(place[:], offs2)
+        nc.sync.dma_start(out=wgo_sb[:], in_=wgo)
+
+        g4 = {(a, h): stage.tile([P, PACK, HALF], F32, name=f"g4_{a}{h}", tag="stage") for h in range(2) for a in range(2)}
+        xb = {(a, h): keep.tile([P, HALF, PACK], BF16, name=f"xb_{a}{h}", align_bytes=64) for a in range(2) for h in range(2)}
+        xq = {(a, h): keep.tile([P, HALF], U32, name=f"xq_{a}{h}", align_bytes=64) for a in range(2) for h in range(2)}
+        xs = {(a, h): keep.tile([P, HALF], U8, name=f"xs_{a}{h}", align_bytes=64) for a in range(2) for h in range(2)}
+
+        def gather(a, i, h, c0, c1):
+            cols = pick[:, (HALF * h + c0) // PER_COL:(HALF * h + c1) // PER_COL]
+            nc.vector.tensor_tensor(g4[a, h][:, i, c0:c1], x_sb[a][i][:].indirect(cols), wgt_sb[h][:, c0:c1], MULT)
+
+        def interleave(a, h, c0, c1):
+            nc.scalar.copy(xb[a, h][:, c0:c1, :].rearrange("p (c e) i -> p c i e", e=4),
+                           g4[a, h][:, :, c0:c1].rearrange("p i (c e) -> p c i e", e=4))
+
+        def quantise_x(a, h, c0, c1):
+            nc.vector.quantize_mx(out=xq[a, h][:, c0:c1].bitcast(FP8X4), scales=xs[a, h][:, c0:c1],
+                                  in_=xb[a, h][:, c0:c1, :].rearrange("p c i -> p (c i)"))
+
+        sc_perm = keep.tile([P, R], U8, name="sc_perm", align_bytes=64)
+        w_perm = {}
+
+        def permute(m, b):
+            w_perm[m, b] = keep.tile([P, 2, PACK, P], I32, name=f"w_perm{m}{b}", align_bytes=64)
+            nc.vector.tensor_copy(out=w_perm[m, b][:].rearrange("p a t c -> p a c t"),
+                                  in_=w_raw[m, b][:].rearrange("p a (c t) -> p a c t", t=PACK))
+
+        hq = {(b, h): keep.tile([P, HALF], U32, name=f"hq_{b}{h}", align_bytes=64) for b in range(2) for h in range(2)}
+        hs = {(b, h): keep.tile([P, HALF], U8, name=f"hs_{b}{h}", align_bytes=64) for b in range(2) for h in range(2)}
+        hb = {(b, h): keep.tile([P, HALF, PACK], BF16, name=f"hb_{b}{h}", align_bytes=64) for b in range(2) for h in range(2)}
+
+        def first_product(m, b, h, c0):
+            bank = ps1.tile([P, PACK, TOK], F32, name=f"bank{m}")
+            for t in range(PACK):
+                for a in range(2):
+                    plane = 8 * m + 4 * a
+                    nc.tensor.matmul_mx(
+                        out=bank[:, t, :],
+                        lhsT=w_perm[m, b][:, a, t, :].bitcast(FP8X4),
+                        lhsT_scale=sc_perm[plane:, 512 * b + P * t:512 * b + P * (t + 1)],
+                        rhs=xq[a, h][:, c0:c0 + TOK].bitcast(FP8X4),
+                        rhs_scale=xs[a, h][:, c0:c0 + TOK],
+                        start=(a == 0), stop=(a == 1))
+            return bank
+
+        def hidden(b, h, c0):
+            ga = first_product(0, b, h, c0)
+            ub = first_product(1, b, h, c0)
+            act = ring.tile([P, TOK, PACK], F32, name="act")
+            nc.scalar.activation(act[:], ga[:].rearrange("p t c -> p c t"), GELU)
+            nc.vector.tensor_tensor(hb[b, h][:, c0:c0 + TOK, :], ub[:].rearrange("p t c -> p c t"), act[:], MULT)
+
+        def quantise_h(b, h, c0, c1):
+            nc.vector.quantize_mx(out=hq[b, h][:, c0:c1].bitcast(FP8X4), scales=hs[b, h][:, c0:c1],
+                                  in_=hb[b, h][:, c0:c1, :].rearrange("p c t -> p (c t)"))
+
+        def unit(h, u):
+            b, c0 = divmod(u * TOK, HALF)
+            hidden(b, h, c0)
+            if u % 2 == 1:
+                quantise_h(b, h, c0 - TOK, c0 + TOK)
+
+        y_sb = {}
+
+        def second_product(h, n):
+            if n == 0:
+                y_sb[h] = stage.tile([P, N // P, HALF], F32, name=f"y_{h}", tag="stage")
+            acc = ps2.tile([P, HALF], F32, name="acc")
+            for b in range(2):
+                nc.tensor.matmul_mx(
+                    out=acc[:],
+                    lhsT=wd_sb[:, b, 2 * P * n:2 * P * (n + 1)].bitcast(FP4X4),
+                    lhsT_scale=wd_sc[:, b, P * n:P * (n + 1)],
+                    rhs=hq[b, h][:].bitcast(FP8X4),
+                    rhs_scale=hs[b, h][:],
+                    start=(b == 0), stop=(b == 1))
+            nc.scalar.copy(y_sb[h][:, n, :], acc[:])
+
+        def scatter(h, n):
+            cols = place[:, HALF * h // PER_COL:HALF * (h + 1) // PER_COL]
+            nc.vector.tensor_tensor(win[n][:].indirect(cols), y_sb[h][:, n, :], wgo_sb[:, HALF * h:HALF * (h + 1)], MULT)
+            if h == 1:
+                nc.sync.dma_start(out=out[P * n:P * (n + 1), :], in_=win[n][:])
+
+        for i in range(PACK):
+            for h in range(2):
+                gather(0, i, h, 0, HALF)
+        for h in range(2):
+            interleave(0, h, 0, HALF)
+        for h in range(2):
+            gather(1, 0, h, 0, HALF)
+        nc.vector.tensor_copy(out=sc_perm[:].rearrange("p (b t c) -> p b c t", b=2, t=PACK),
+                              in_=sc_raw[:].rearrange("p (b c t) -> p b c t", b=2, t=PACK))
+        for i in range(1, PACK - 1):
+            for h in range(2):
+                gather(1, i, h, 0, HALF)
+            quantise_x(0, i - 1, 0, HALF)
+        for c0 in range(0, HALF, TOK):
+            gather(1, PACK - 1, 0, c0, c0 + TOK)
+            interleave(1, 0, c0, c0 + TOK)
+        permute(0, 0)
+        quantise_x(1, 0, 0, TOK)
+        permute(1, 0)
+        for c0 in range(TOK, HALF, TOK):
+            quantise_x(1, 0, c0, c0 + TOK)
+        for u in range(2):
+            unit(0, u)
+        permute(0, 1)
+        permute(1, 1)
+        for u in range(2, 8):
+            unit(0, u)
+        gather(1, PACK - 1, 1, 0, HALF)
+        interleave(1, 1, 0, HALF)
+        quantise_x(1, 1, 0, HALF)
+        unit(1, 0)
+        second_product(0, 0)
+        for u in range(1, 5):
+            unit(1, u)
+        second_product(0, 1)
+        for u in range(5, 8):
+            unit(1, u)
+        second_product(0, 2)
+        second_product(0, 3)
+        for n in range(N // P):
+            second_product(1, n)
+        for h in range(2):
+            for n in range(N // P):
+                scatter(h, n)

@@ -28,7 +28,6 @@ def tile_list_gelu_scat_kernel(tc, xT, wgt, wg_words, wg_scales, wu_words, wu_sc
     with ExitStack() as ctx:
         keep = ctx.enter_context(tc.tile_pool(name="keep", bufs=1))
         ring = ctx.enter_context(tc.tile_pool(name="ring", bufs=3))
-        stage = ctx.enter_context(tc.tile_pool(name="stage", bufs=4))
         ps1 = ctx.enter_context(tc.psum_pool(name="ps1", bufs=3))
         ps2 = ctx.enter_context(tc.psum_pool(name="ps2", bufs=2))
 
@@ -47,20 +46,22 @@ def tile_list_gelu_scat_kernel(tc, xT, wgt, wg_words, wg_scales, wu_words, wu_sc
         win = [keep.tile([P, T], F32, name=f"win{n}") for n in range(N // P)]
         sc_raw = keep.tile([P, R], U8, name="sc_raw", align_bytes=64)
         wd_sc = keep.tile([P, 2, N], U8, name="wd_sc", align_bytes=64)
-        nc.vector.memset(sc_raw[:].bitcast(I32), 0)
-        nc.vector.memset(wd_sc[:].bitcast(I32), 0)
         for n in range(N // P):
-            nc.vector.memset(win[n][:], 0.0)
+            nc.gpsimd.memset(win[n][:], 0.0)
+            if n == 1:
+                nc.gpsimd.memset(sc_raw[:].bitcast(I32), 0)
+                nc.gpsimd.memset(wd_sc[:].bitcast(I32), 0)
+                for m, scales in enumerate((wg_scales, wu_scales)):
+                    for q in range(4):
+                        lo = 32 * q + 8 * m
+                        nc.gpsimd.dma_start(out=sc_raw[lo:lo + 8, :].bitcast(I32), in_=scales[:, 4 * q:4 * q + 4, :].bitcast(I32))
 
-        nc.sync.dma_start(pick[:], offs)
-        nc.sync.dma_start(out=wgt_sb[0][:], in_=wgt[:, 0:HALF])
         nc.sync.dma_start(out=x_sb[0][0][:], in_=x_rows[0, 0])
+        nc.sync.dma_start(pick[:], offs)
+        nc.sync.dma_start(out=wgt_sb[0][:, 0:TOK], in_=wgt[:, 0:TOK])
+        nc.sync.dma_start(out=wgt_sb[0][:, TOK:HALF], in_=wgt[:, TOK:HALF])
         nc.sync.dma_start(out=wgt_sb[1][:], in_=wgt[:, HALF:J])
         nc.sync.dma_start(out=x_sb[0][1][:], in_=x_rows[0, 1])
-        for m, scales in enumerate((wg_scales, wu_scales)):
-            for q in range(4):
-                lo = 32 * q + 8 * m
-                nc.scalar.dma_start(out=sc_raw[lo:lo + 8, :].bitcast(I32), in_=scales[:, 4 * q:4 * q + 4, :].bitcast(I32))
         for a in range(2):
             for i in range(PACK):
                 if PACK * a + i > 1:
@@ -79,7 +80,7 @@ def tile_list_gelu_scat_kernel(tc, xT, wgt, wg_words, wg_scales, wu_words, wu_sc
         nc.sync.dma_start(place[:], offs2)
         nc.sync.dma_start(out=wgo_sb[:], in_=wgo)
 
-        g4 = {(a, h): stage.tile([P, PACK, HALF], F32, name=f"g4_{a}{h}", tag="stage") for h in range(2) for a in range(2)}
+        g4 = {(a, h): keep.tile([P, PACK, HALF], F32, name=f"g4_{a}{h}") for h in range(2) for a in range(2)}
         xb = {(a, h): keep.tile([P, HALF, PACK], BF16, name=f"xb_{a}{h}", align_bytes=64) for a in range(2) for h in range(2)}
         xq = {(a, h): keep.tile([P, HALF], U32, name=f"xq_{a}{h}", align_bytes=64) for a in range(2) for h in range(2)}
         xs = {(a, h): keep.tile([P, HALF], U8, name=f"xs_{a}{h}", align_bytes=64) for a in range(2) for h in range(2)}
@@ -122,28 +123,29 @@ def tile_list_gelu_scat_kernel(tc, xT, wgt, wg_words, wg_scales, wu_words, wu_sc
                         start=(a == 0), stop=(a == 1))
             return bank
 
-        def hidden(b, h, c0):
+        def hidden(b, h, c0, act):
             ga = first_product(0, b, h, c0)
             ub = first_product(1, b, h, c0)
-            act = ring.tile([P, TOK, PACK], F32, name="act")
-            nc.scalar.activation(act[:], ga[:].rearrange("p t c -> p c t"), GELU)
-            nc.vector.tensor_tensor(hb[b, h][:, c0:c0 + TOK, :], ub[:].rearrange("p t c -> p c t"), act[:], MULT)
+            act = act.rearrange("p (c t) -> p c t", t=PACK)
+            nc.scalar.activation(act, ga[:].rearrange("p t c -> p c t"), GELU)
+            nc.vector.tensor_tensor(hb[b, h][:, c0:c0 + TOK, :], ub[:].rearrange("p t c -> p c t"), act, MULT)
 
         def quantise_h(b, h, c0, c1):
             nc.vector.quantize_mx(out=hq[b, h][:, c0:c1].bitcast(FP8X4), scales=hs[b, h][:, c0:c1],
                                   in_=hb[b, h][:, c0:c1, :].rearrange("p c t -> p (c t)"))
 
-        def unit(h, u):
+        def unit(h, u, act=None):
             b, c0 = divmod(u * TOK, HALF)
-            hidden(b, h, c0)
-            if u % 2 == 1:
-                quantise_h(b, h, c0 - TOK, c0 + TOK)
+            if act is None:
+                act = ring.tile([P, TOK * PACK], F32, name="act")[:]
+            hidden(b, h, c0, act)
+            group = 2 * TOK if h == 0 else HALF
+            if (c0 + TOK) % group == 0:
+                quantise_h(b, h, c0 + TOK - group, c0 + TOK)
 
-        y_sb = {}
+        y_sb = [g4[0, h] for h in range(2)]
 
         def second_product(h, n):
-            if n == 0:
-                y_sb[h] = stage.tile([P, N // P, HALF], F32, name=f"y_{h}", tag="stage")
             acc = ps2.tile([P, HALF], F32, name="acc")
             for b in range(2):
                 nc.tensor.matmul_mx(
@@ -161,36 +163,40 @@ def tile_list_gelu_scat_kernel(tc, xT, wgt, wg_words, wg_scales, wu_words, wu_sc
             if h == 1:
                 nc.sync.dma_start(out=out[P * n:P * (n + 1), :], in_=win[n][:])
 
-        for i in range(PACK):
+        gather(0, 0, 0, 0, TOK)
+        gather(0, 0, 0, TOK, HALF)
+        gather(0, 0, 1, 0, HALF)
+        for i in range(1, PACK):
             for h in range(2):
                 gather(0, i, h, 0, HALF)
+        nc.vector.tensor_copy(out=sc_perm[:].rearrange("p (b t c) -> p b c t", b=2, t=PACK),
+                              in_=sc_raw[:].rearrange("p (b c t) -> p b c t", b=2, t=PACK))
         for h in range(2):
             interleave(0, h, 0, HALF)
         for h in range(2):
             gather(1, 0, h, 0, HALF)
-        nc.vector.tensor_copy(out=sc_perm[:].rearrange("p (b t c) -> p b c t", b=2, t=PACK),
-                              in_=sc_raw[:].rearrange("p (b c t) -> p b c t", b=2, t=PACK))
         for i in range(1, PACK - 1):
-            for h in range(2):
-                gather(1, i, h, 0, HALF)
+            gather(1, i, 0, 0, HALF)
             quantise_x(0, i - 1, 0, HALF)
-        for c0 in range(0, HALF, TOK):
-            gather(1, PACK - 1, 0, c0, c0 + TOK)
-            interleave(1, 0, c0, c0 + TOK)
+        for c0 in range(0, HALF, 2 * TOK):
+            gather(1, PACK - 1, 0, c0, c0 + 2 * TOK)
+            interleave(1, 0, c0, c0 + 2 * TOK)
         permute(0, 0)
-        quantise_x(1, 0, 0, TOK)
+        quantise_x(1, 0, 0, 2 * TOK)
         permute(1, 0)
-        for c0 in range(TOK, HALF, TOK):
-            quantise_x(1, 0, c0, c0 + TOK)
-        for u in range(2):
-            unit(0, u)
-        permute(0, 1)
-        permute(1, 1)
-        for u in range(2, 8):
-            unit(0, u)
-        gather(1, PACK - 1, 1, 0, HALF)
-        interleave(1, 1, 0, HALF)
-        quantise_x(1, 1, 0, HALF)
+        quantise_x(1, 0, 2 * TOK, HALF)
+        for u in range(8):
+            if u < PACK - 1:
+                unit(0, u, g4[1, 1][:, u + 1, :])
+                gather(1, u + 1, 1, 0, HALF)
+            else:
+                unit(0, u)
+            if u == 0:
+                permute(0, 1)
+                permute(1, 1)
+        for c0 in range(0, HALF, 2 * TOK):
+            interleave(1, 1, c0, c0 + 2 * TOK)
+            quantise_x(1, 1, c0, c0 + 2 * TOK)
         unit(1, 0)
         second_product(0, 0)
         for u in range(1, 5):

@@ -38,38 +38,44 @@ def tile_list_gelu_scat_kernel(tc, xT, wgt, wg_words, wg_scales, wu_words, wu_sc
         x_sb = [[keep.tile([P, T], F32, name=f"x{a}{i}") for i in range(PACK)] for a in range(2)]
         x_rows = xT.rearrange("(a p i) t -> a i p t", a=2, i=PACK)
 
+        sc_raw = keep.tile([P, R], U8, name="sc_raw", align_bytes=64)
+        nc.vector.memset(sc_raw[:].bitcast(I32), 0)
         warm = keep.tile([P, 8], F32, name="warm")
         warm2 = keep.tile([P, 8], F32, name="warm2")
         nc.gpsimd.memset(warm[:], 0.0)
         nc.scalar.activation(warm2[:], warm[:], GELU)
 
         win = [keep.tile([P, T], F32, name=f"win{n}") for n in range(N // P)]
-        sc_raw = keep.tile([P, R], U8, name="sc_raw", align_bytes=64)
         wd_sc = keep.tile([P, 2, N], U8, name="wd_sc", align_bytes=64)
+        nc.gpsimd.memset(wd_sc[:].bitcast(I32), 0)
         for n in range(N // P):
             nc.gpsimd.memset(win[n][:], 0.0)
-            if n == 1:
-                nc.gpsimd.memset(sc_raw[:].bitcast(I32), 0)
-                nc.gpsimd.memset(wd_sc[:].bitcast(I32), 0)
-                for m, scales in enumerate((wg_scales, wu_scales)):
-                    for q in range(4):
-                        lo = 32 * q + 8 * m
-                        nc.gpsimd.dma_start(out=sc_raw[lo:lo + 8, :].bitcast(I32), in_=scales[:, 4 * q:4 * q + 4, :].bitcast(I32))
 
-        nc.sync.dma_start(out=x_sb[0][0][:], in_=x_rows[0, 0])
+        def load_plane(plane):
+            a, i = divmod(plane, PACK)
+            nc.sync.dma_start(out=x_sb[a][i][:], in_=x_rows[a, i])
+
+        def load_scales(s):
+            m, q = divmod(s, 4)
+            lo = 32 * q + 8 * m
+            nc.sync.dma_start(out=sc_raw[lo:lo + 8, :].bitcast(I32),
+                              in_=(wg_scales, wu_scales)[m][:, 4 * q:4 * q + 4, :].bitcast(I32))
+
+        load_plane(0)
         nc.sync.dma_start(pick[:], offs)
         nc.sync.dma_start(out=wgt_sb[0][:, 0:TOK], in_=wgt[:, 0:TOK])
         nc.sync.dma_start(out=wgt_sb[0][:, TOK:HALF], in_=wgt[:, TOK:HALF])
         nc.sync.dma_start(out=wgt_sb[1][:], in_=wgt[:, HALF:J])
-        nc.sync.dma_start(out=x_sb[0][1][:], in_=x_rows[0, 1])
-        for a in range(2):
-            for i in range(PACK):
-                if PACK * a + i > 1:
-                    nc.sync.dma_start(out=x_sb[a][i][:], in_=x_rows[a, i])
+        for plane in range(1, 6):
+            load_plane(plane)
+        for plane in range(6, 8):
+            for s in range(4 * (plane - 6), 4 * (plane - 5)):
+                load_scales(s)
+            load_plane(plane)
         w_raw = {}
         for b in range(2):
             for m, words in enumerate((wg_words, wu_words)):
-                w_raw[m, b] = keep.tile([P, 2, 512], I32, name=f"w_raw{m}{b}")
+                w_raw[m, b] = keep.tile([P, 2, 512], I32, name=f"w_raw{m}{b}", align_bytes=64)
                 src = words.rearrange("a p r i -> p a (r i)")[:, :, 2048 * b:2048 * (b + 1)]
                 nc.sync.dma_start(out=w_raw[m, b][:], in_=src.bitcast(I32))
         wd_sb = keep.tile([P, 2, 2 * N], U8, name="wd_sb", align_bytes=64)
@@ -82,7 +88,13 @@ def tile_list_gelu_scat_kernel(tc, xT, wgt, wg_words, wg_scales, wu_words, wu_sc
 
         g4 = {(a, h): keep.tile([P, PACK, HALF], F32, name=f"g4_{a}{h}") for h in range(2) for a in range(2)}
         xb = {(a, h): keep.tile([P, HALF, PACK], BF16, name=f"xb_{a}{h}", align_bytes=64) for a in range(2) for h in range(2)}
-        xq = {(a, h): keep.tile([P, HALF], U32, name=f"xq_{a}{h}", align_bytes=64) for a in range(2) for h in range(2)}
+        xq = {(a, h): keep.tile([P, HALF], U32, name=f"xq_{a}{h}", align_bytes=64) for a in range(2) for h in range(2) if (a, h) != (1, 0)}
+
+        def x_codes(a, h, c0, c1):
+            if (a, h) == (1, 0):
+                return w_raw[c0 // (2 * TOK), 0][:, 0, c0:c1].bitcast(FP8X4)
+            return xq[a, h][:, c0:c1].bitcast(FP8X4)
+
         xs = {(a, h): keep.tile([P, HALF], U8, name=f"xs_{a}{h}", align_bytes=64) for a in range(2) for h in range(2)}
 
         def gather(a, i, h, c0, c1):
@@ -94,7 +106,7 @@ def tile_list_gelu_scat_kernel(tc, xT, wgt, wg_words, wg_scales, wu_words, wu_sc
                            g4[a, h][:, :, c0:c1].rearrange("p i (c e) -> p c i e", e=4))
 
         def quantise_x(a, h, c0, c1):
-            nc.vector.quantize_mx(out=xq[a, h][:, c0:c1].bitcast(FP8X4), scales=xs[a, h][:, c0:c1],
+            nc.vector.quantize_mx(out=x_codes(a, h, c0, c1), scales=xs[a, h][:, c0:c1],
                                   in_=xb[a, h][:, c0:c1, :].rearrange("p c i -> p (c i)"))
 
         sc_perm = keep.tile([P, R], U8, name="sc_perm", align_bytes=64)
@@ -118,7 +130,7 @@ def tile_list_gelu_scat_kernel(tc, xT, wgt, wg_words, wg_scales, wu_words, wu_sc
                         out=bank[:, t, :],
                         lhsT=w_perm[m, b][:, a, t, :].bitcast(FP8X4),
                         lhsT_scale=sc_perm[plane:, 512 * b + P * t:512 * b + P * (t + 1)],
-                        rhs=xq[a, h][:, c0:c0 + TOK].bitcast(FP8X4),
+                        rhs=x_codes(a, h, c0, c0 + TOK),
                         rhs_scale=xs[a, h][:, c0:c0 + TOK],
                         start=(a == 0), stop=(a == 1))
             return bank
@@ -169,8 +181,6 @@ def tile_list_gelu_scat_kernel(tc, xT, wgt, wg_words, wg_scales, wu_words, wu_sc
         for i in range(1, PACK):
             for h in range(2):
                 gather(0, i, h, 0, HALF)
-        nc.vector.tensor_copy(out=sc_perm[:].rearrange("p (b t c) -> p b c t", b=2, t=PACK),
-                              in_=sc_raw[:].rearrange("p (b c t) -> p b c t", b=2, t=PACK))
         for h in range(2):
             interleave(0, h, 0, HALF)
         for h in range(2):
@@ -178,6 +188,8 @@ def tile_list_gelu_scat_kernel(tc, xT, wgt, wg_words, wg_scales, wu_words, wu_sc
         for i in range(1, PACK - 1):
             gather(1, i, 0, 0, HALF)
             quantise_x(0, i - 1, 0, HALF)
+        nc.vector.tensor_copy(out=sc_perm[:].rearrange("p (b t c) -> p b c t", b=2, t=PACK),
+                              in_=sc_raw[:].rearrange("p (b c t) -> p b c t", b=2, t=PACK))
         for c0 in range(0, HALF, 2 * TOK):
             gather(1, PACK - 1, 0, c0, c0 + 2 * TOK)
             interleave(1, 0, c0, c0 + 2 * TOK)

@@ -45,11 +45,11 @@ def tile_list_gelu_scat_kernel(tc, xT, wgt, wg_words, wg_scales, wu_words, wu_sc
         nc.gpsimd.memset(warm[:], 0.0)
         nc.scalar.activation(warm2[:], warm[:], GELU)
 
-        win = [keep.tile([P, T], F32, name=f"win{n}") for n in range(N // P)]
+        win = [keep.tile([P, T], F32, name=f"win{n}") for n in range(3)]
         wd_sc = keep.tile([P, 2, N], U8, name="wd_sc", align_bytes=64)
-        nc.gpsimd.memset(wd_sc[:].bitcast(I32), 0)
-        for n in range(N // P):
-            nc.gpsimd.memset(win[n][:], 0.0)
+        nc.vector.memset(wd_sc[:].bitcast(I32), 0)
+        for n in range(3):
+            nc.vector.memset(win[n][:], 0.0)
 
         def load_plane(plane):
             a, i = divmod(plane, PACK)
@@ -151,9 +151,8 @@ def tile_list_gelu_scat_kernel(tc, xT, wgt, wg_words, wg_scales, wu_words, wu_sc
             if act is None:
                 act = ring.tile([P, TOK * PACK], F32, name="act")[:]
             hidden(b, h, c0, act)
-            group = 2 * TOK if h == 0 else HALF
-            if (c0 + TOK) % group == 0:
-                quantise_h(b, h, c0 + TOK - group, c0 + TOK)
+            if c0 + TOK == HALF:
+                quantise_h(b, h, 0, HALF)
 
         y_sb = [g4[0, h] for h in range(2)]
 
@@ -171,9 +170,9 @@ def tile_list_gelu_scat_kernel(tc, xT, wgt, wg_words, wg_scales, wu_words, wu_sc
 
         def scatter(h, n):
             cols = place[:, HALF * h // PER_COL:HALF * (h + 1) // PER_COL]
-            nc.vector.tensor_tensor(win[n][:].indirect(cols), y_sb[h][:, n, :], wgo_sb[:, HALF * h:HALF * (h + 1)], MULT)
+            nc.vector.tensor_tensor(win[n % 3][:].indirect(cols), y_sb[h][:, n, :], wgo_sb[:, HALF * h:HALF * (h + 1)], MULT)
             if h == 1:
-                nc.sync.dma_start(out=out[P * n:P * (n + 1), :], in_=win[n][:])
+                nc.sync.dma_start(out=out[P * n:P * (n + 1), :], in_=win[n % 3][:])
 
         gather(0, 0, 0, 0, TOK)
         gather(0, 0, 0, TOK, HALF)
@@ -217,9 +216,12 @@ def tile_list_gelu_scat_kernel(tc, xT, wgt, wg_words, wg_scales, wu_words, wu_sc
         for u in range(5, 8):
             unit(1, u)
         second_product(0, 2)
-        second_product(0, 3)
-        for n in range(N // P):
+        for n in range(3):
             second_product(1, n)
         for h in range(2):
-            for n in range(N // P):
+            second_product(h, 3)
+        for h in range(2):
+            for n in range(3):
                 scatter(h, n)
+        for h in range(2):
+            scatter(h, 3)

@@ -113,9 +113,9 @@ def tile_list_gelu_scat_kernel(tc, xT, wgt, wg_words, wg_scales, wu_words, wu_sc
         w_perm = {}
 
         def permute(m, b):
-            w_perm[m, b] = keep.tile([P, 2, PACK, P], I32, name=f"w_perm{m}{b}", align_bytes=64)
-            nc.vector.tensor_copy(out=w_perm[m, b][:].rearrange("p a t c -> p a c t"),
-                                  in_=w_raw[m, b][:].rearrange("p a (c t) -> p a c t", t=PACK))
+            w_perm[m, b] = keep.tile([P, PACK, 2, P], I32, name=f"w_perm{m}{b}", align_bytes=64)
+            nc.vector.tensor_copy(out=w_perm[m, b][:].rearrange("p t a (c e) -> p (a c) t e", e=4),
+                                  in_=w_raw[m, b][:].rearrange("p a (c e t) -> p (a c) t e", e=4, t=PACK))
 
         hq = {(b, h): keep.tile([P, HALF], U32, name=f"hq_{b}{h}", align_bytes=64) for b in range(2) for h in range(2)}
         hs = {(b, h): keep.tile([P, HALF], U8, name=f"hs_{b}{h}", align_bytes=64) for b in range(2) for h in range(2)}
@@ -128,7 +128,7 @@ def tile_list_gelu_scat_kernel(tc, xT, wgt, wg_words, wg_scales, wu_words, wu_sc
                     plane = 8 * m + 4 * a
                     nc.tensor.matmul_mx(
                         out=bank[:, t, :],
-                        lhsT=w_perm[m, b][:, a, t, :].bitcast(FP8X4),
+                        lhsT=w_perm[m, b][:, t, a, :].bitcast(FP8X4),
                         lhsT_scale=sc_perm[plane:, 512 * b + P * t:512 * b + P * (t + 1)],
                         rhs=x_codes(a, h, c0, c0 + TOK),
                         rhs_scale=xs[a, h][:, c0:c0 + TOK],
@@ -187,8 +187,8 @@ def tile_list_gelu_scat_kernel(tc, xT, wgt, wg_words, wg_scales, wu_words, wu_sc
         for i in range(1, PACK - 1):
             gather(1, i, 0, 0, HALF)
             quantise_x(0, i - 1, 0, HALF)
-        nc.vector.tensor_copy(out=sc_perm[:].rearrange("p (b t c) -> p b c t", b=2, t=PACK),
-                              in_=sc_raw[:].rearrange("p (b c t) -> p b c t", b=2, t=PACK))
+        nc.vector.tensor_copy(out=sc_perm[:].rearrange("p (b t c) -> p b t c", b=2, t=PACK),
+                              in_=sc_raw[:].rearrange("p (b c t) -> p b t c", b=2, t=PACK))
         for c0 in range(0, HALF, 2 * TOK):
             gather(1, PACK - 1, 0, c0, c0 + 2 * TOK)
             interleave(1, 0, c0, c0 + 2 * TOK)

@@ -1,6 +1,7 @@
 from contextlib import ExitStack
 
 import concourse.mybir as mybir
+from concourse.masks import make_identity
 
 K, R, N, T, J = 1024, 1024, 512, 2048, 1024
 FLOPS = 2 * J * (2 * K * R + R * N)
@@ -19,6 +20,7 @@ GELU = mybir.ActivationFunctionType.Gelu_apprx_tanh
 P = 128
 PACK = 4
 HALF = 512
+CHUNK = 256
 TOK = 128
 PER_COL = 16
 
@@ -27,9 +29,10 @@ def tile_list_gelu_scat_kernel(tc, xT, wgt, wg_words, wg_scales, wu_words, wu_sc
     nc = tc.nc
     with ExitStack() as ctx:
         keep = ctx.enter_context(tc.tile_pool(name="keep", bufs=1))
+        stage = ctx.enter_context(tc.tile_pool(name="stage", bufs=3))
         ring = ctx.enter_context(tc.tile_pool(name="ring", bufs=3))
         ps1 = ctx.enter_context(tc.psum_pool(name="ps1", bufs=3))
-        ps2 = ctx.enter_context(tc.psum_pool(name="ps2", bufs=2))
+        ps2 = ctx.enter_context(tc.psum_pool(name="ps2", bufs=1))
 
         pick = keep.tile([P, J // PER_COL], U16, name="pick")
         place = keep.tile([P, J // PER_COL], U16, name="place")
@@ -38,18 +41,15 @@ def tile_list_gelu_scat_kernel(tc, xT, wgt, wg_words, wg_scales, wu_words, wu_sc
         x_sb = [[keep.tile([P, T], F32, name=f"x{a}{i}") for i in range(PACK)] for a in range(2)]
         x_rows = xT.rearrange("(a p i) t -> a i p t", a=2, i=PACK)
 
-        sc_raw = keep.tile([P, R], U8, name="sc_raw", align_bytes=64)
-        nc.vector.memset(sc_raw[:].bitcast(I32), 0)
-        warm = keep.tile([P, 8], F32, name="warm")
-        warm2 = keep.tile([P, 8], F32, name="warm2")
-        nc.gpsimd.memset(warm[:], 0.0)
-        nc.scalar.activation(warm2[:], warm[:], GELU)
-
-        win = [keep.tile([P, T], F32, name=f"win{n}") for n in range(3)]
+        w_sc = keep.tile([P, 2, R], U8, name="w_sc", align_bytes=64)
+        nc.vector.memset(w_sc[:].rearrange("p a r -> p (a r)").bitcast(I32), 0)
         wd_sc = keep.tile([P, 2, N], U8, name="wd_sc", align_bytes=64)
-        nc.vector.memset(wd_sc[:].bitcast(I32), 0)
+        nc.vector.memset(wd_sc[:].rearrange("p a r -> p (a r)").bitcast(I32), 0)
+        win = [keep.tile([P, T], F32, name=f"win{n}") for n in range(3)]
         for n in range(3):
             nc.vector.memset(win[n][:], 0.0)
+        ident = keep.tile([P, P], F32, name="ident")
+        make_identity(nc, ident[:])
 
         def load_plane(plane):
             a, i = divmod(plane, PACK)
@@ -57,27 +57,26 @@ def tile_list_gelu_scat_kernel(tc, xT, wgt, wg_words, wg_scales, wu_words, wu_sc
 
         def load_scales(s):
             m, q = divmod(s, 4)
-            lo = 32 * q + 8 * m
-            nc.sync.dma_start(out=sc_raw[lo:lo + 8, :].bitcast(I32),
-                              in_=(wg_scales, wu_scales)[m][:, 4 * q:4 * q + 4, :].bitcast(I32))
+            lo = 32 * q + 4 * m
+            nc.sync.dma_start(out=w_sc[lo:lo + 4, :, :].bitcast(I32),
+                              in_=(wg_scales, wu_scales)[m][:, 4 * q:4 * q + 4, :].rearrange("a q r -> q a r").bitcast(I32))
 
         load_plane(0)
         nc.sync.dma_start(pick[:], offs)
-        nc.sync.dma_start(out=wgt_sb[0][:, 0:TOK], in_=wgt[:, 0:TOK])
-        nc.sync.dma_start(out=wgt_sb[0][:, TOK:HALF], in_=wgt[:, TOK:HALF])
-        nc.sync.dma_start(out=wgt_sb[1][:], in_=wgt[:, HALF:J])
+        for h in range(2):
+            nc.sync.dma_start(out=wgt_sb[h][:], in_=wgt[:, HALF * h:HALF * (h + 1)])
         for plane in range(1, 6):
             load_plane(plane)
         for plane in range(6, 8):
             for s in range(4 * (plane - 6), 4 * (plane - 5)):
                 load_scales(s)
             load_plane(plane)
-        w_raw = {}
+        w_sb = {}
         for b in range(2):
             for m, words in enumerate((wg_words, wu_words)):
-                w_raw[m, b] = keep.tile([P, 2, 512], I32, name=f"w_raw{m}{b}", align_bytes=64)
+                w_sb[m, b] = keep.tile([P, 2, HALF], I32, name=f"w_sb{m}{b}", align_bytes=64)
                 src = words.rearrange("a p r i -> p a (r i)")[:, :, 2048 * b:2048 * (b + 1)]
-                nc.sync.dma_start(out=w_raw[m, b][:], in_=src.bitcast(I32))
+                nc.sync.dma_start(out=w_sb[m, b][:], in_=src.bitcast(I32))
         wd_sb = keep.tile([P, 2, 2 * N], U8, name="wd_sb", align_bytes=64)
         nc.sync.dma_start(out=wd_sb[:].bitcast(I32), in_=wd_words.rearrange("a p c -> p a c").bitcast(I32))
         for q in range(4):
@@ -86,142 +85,128 @@ def tile_list_gelu_scat_kernel(tc, xT, wgt, wg_words, wg_scales, wu_words, wu_sc
         nc.sync.dma_start(place[:], offs2)
         nc.sync.dma_start(out=wgo_sb[:], in_=wgo)
 
-        g4 = {(a, h): keep.tile([P, PACK, HALF], F32, name=f"g4_{a}{h}") for h in range(2) for a in range(2)}
-        xb = {(a, h): keep.tile([P, HALF, PACK], BF16, name=f"xb_{a}{h}", align_bytes=64) for a in range(2) for h in range(2)}
-        xq = {(a, h): keep.tile([P, HALF], U32, name=f"xq_{a}{h}", align_bytes=64) for a in range(2) for h in range(2) if (a, h) != (1, 0)}
+        def gather(dst, a, i, c0, c1):
+            h = c0 // HALF
+            cols = pick[:, c0 // PER_COL:c1 // PER_COL]
+            nc.vector.tensor_tensor(dst, x_sb[a][i][:].indirect(cols), wgt_sb[h][:, c0 - HALF * h:c1 - HALF * h], MULT)
 
-        def x_codes(a, h, c0, c1):
-            if (a, h) == (1, 0):
-                return w_raw[c0 // (2 * TOK), 0][:, 0, c0:c1].bitcast(FP8X4)
-            return xq[a, h][:, c0:c1].bitcast(FP8X4)
+        xq, xs = {}, {}
 
-        xs = {(a, h): keep.tile([P, HALF], U8, name=f"xs_{a}{h}", align_bytes=64) for a in range(2) for h in range(2)}
+        def quantise_x(a, c0, src):
+            width = src.shape[2]
+            xb = keep.tile([P, width, PACK], BF16, name=f"xb{a}_{c0}", align_bytes=64)
+            nc.scalar.copy(xb[:].rearrange("p (c e) i -> p c i e", e=4), src.rearrange("p i (c e) -> p c i e", e=4))
+            codes = keep.tile([P, width], U32, name=f"xq{a}_{c0}", align_bytes=64)
+            scales = keep.tile([P, width], U8, name=f"xs{a}_{c0}", align_bytes=64)
+            nc.vector.quantize_mx(out=codes[:].bitcast(FP8X4), scales=scales[:], in_=xb[:].rearrange("p c i -> p (c i)"))
+            for t in range(width // TOK):
+                xq[a, c0 // TOK + t] = codes[:, TOK * t:TOK * (t + 1)].bitcast(FP8X4)
+                xs[a, c0 // TOK + t] = scales[:, TOK * t:TOK * (t + 1)]
 
-        def gather(a, i, h, c0, c1):
-            cols = pick[:, (HALF * h + c0) // PER_COL:(HALF * h + c1) // PER_COL]
-            nc.vector.tensor_tensor(g4[a, h][:, i, c0:c1], x_sb[a][i][:].indirect(cols), wgt_sb[h][:, c0:c1], MULT)
-
-        def interleave(a, h, c0, c1):
-            nc.scalar.copy(xb[a, h][:, c0:c1, :].rearrange("p (c e) i -> p c i e", e=4),
-                           g4[a, h][:, :, c0:c1].rearrange("p i (c e) -> p c i e", e=4))
-
-        def quantise_x(a, h, c0, c1):
-            nc.vector.quantize_mx(out=x_codes(a, h, c0, c1), scales=xs[a, h][:, c0:c1],
-                                  in_=xb[a, h][:, c0:c1, :].rearrange("p c i -> p (c i)"))
-
-        sc_perm = keep.tile([P, R], U8, name="sc_perm", align_bytes=64)
-        w_perm = {}
-
-        def permute(m, b):
-            w_perm[m, b] = keep.tile([P, PACK, 2, P], I32, name=f"w_perm{m}{b}", align_bytes=64)
-            nc.vector.tensor_copy(out=w_perm[m, b][:].rearrange("p t a (c e) -> p (a c) t e", e=4),
-                                  in_=w_raw[m, b][:].rearrange("p a (c e t) -> p (a c) t e", e=4, t=PACK))
-
-        hq = {(b, h): keep.tile([P, HALF], U32, name=f"hq_{b}{h}", align_bytes=64) for b in range(2) for h in range(2)}
-        hs = {(b, h): keep.tile([P, HALF], U8, name=f"hs_{b}{h}", align_bytes=64) for b in range(2) for h in range(2)}
-        hb = {(b, h): keep.tile([P, HALF, PACK], BF16, name=f"hb_{b}{h}", align_bytes=64) for b in range(2) for h in range(2)}
-
-        def first_product(m, b, h, c0):
-            bank = ps1.tile([P, PACK, TOK], F32, name=f"bank{m}")
-            for t in range(PACK):
-                for a in range(2):
-                    plane = 8 * m + 4 * a
-                    nc.tensor.matmul_mx(
-                        out=bank[:, t, :],
-                        lhsT=w_perm[m, b][:, t, a, :].bitcast(FP8X4),
-                        lhsT_scale=sc_perm[plane:, 512 * b + P * t:512 * b + P * (t + 1)],
-                        rhs=x_codes(a, h, c0, c0 + TOK),
-                        rhs_scale=xs[a, h][:, c0:c0 + TOK],
-                        start=(a == 0), stop=(a == 1))
-            return bank
-
-        def hidden(b, h, c0, act):
-            ga = first_product(0, b, h, c0)
-            ub = first_product(1, b, h, c0)
-            act = act.rearrange("p (c t) -> p c t", t=PACK)
-            nc.scalar.activation(act, ga[:].rearrange("p t c -> p c t"), GELU)
-            nc.vector.tensor_tensor(hb[b, h][:, c0:c0 + TOK, :], ub[:].rearrange("p t c -> p c t"), act, MULT)
-
-        def quantise_h(b, h, c0, c1):
-            nc.vector.quantize_mx(out=hq[b, h][:, c0:c1].bitcast(FP8X4), scales=hs[b, h][:, c0:c1],
-                                  in_=hb[b, h][:, c0:c1, :].rearrange("p c t -> p (c t)"))
-
-        def unit(h, u, act=None):
-            b, c0 = divmod(u * TOK, HALF)
-            if act is None:
-                act = ring.tile([P, TOK * PACK], F32, name="act")[:]
-            hidden(b, h, c0, act)
-            if c0 + TOK == HALF:
-                quantise_h(b, h, 0, HALF)
-
-        y_sb = [g4[0, h] for h in range(2)]
-
-        def second_product(h, n):
-            acc = ps2.tile([P, HALF], F32, name="acc")
-            for b in range(2):
-                nc.tensor.matmul_mx(
-                    out=acc[:],
-                    lhsT=wd_sb[:, b, 2 * P * n:2 * P * (n + 1)].bitcast(FP4X4),
-                    lhsT_scale=wd_sc[:, b, P * n:P * (n + 1)],
-                    rhs=hq[b, h][:].bitcast(FP8X4),
-                    rhs_scale=hs[b, h][:],
-                    start=(b == 0), stop=(b == 1))
-            nc.scalar.copy(y_sb[h][:, n, :], acc[:])
-
-        def scatter(h, n):
-            cols = place[:, HALF * h // PER_COL:HALF * (h + 1) // PER_COL]
-            nc.vector.tensor_tensor(win[n % 3][:].indirect(cols), y_sb[h][:, n, :], wgo_sb[:, HALF * h:HALF * (h + 1)], MULT)
-            if h == 1:
-                nc.sync.dma_start(out=out[P * n:P * (n + 1), :], in_=win[n % 3][:])
-
-        gather(0, 0, 0, 0, TOK)
-        gather(0, 0, 0, TOK, HALF)
-        gather(0, 0, 1, 0, HALF)
-        for i in range(1, PACK):
+        g0 = [keep.tile([P, PACK, HALF], F32, name=f"g0_{h}") for h in range(2)]
+        for i in range(PACK):
             for h in range(2):
-                gather(0, i, h, 0, HALF)
+                gather(g0[h][:, i, :], 0, i, HALF * h, HALF * (h + 1))
         for h in range(2):
-            interleave(0, h, 0, HALF)
-        for h in range(2):
-            gather(1, 0, h, 0, HALF)
-        for i in range(1, PACK - 1):
-            gather(1, i, 0, 0, HALF)
-            quantise_x(0, i - 1, 0, HALF)
-        nc.vector.tensor_copy(out=sc_perm[:].rearrange("p (b t c) -> p b t c", b=2, t=PACK),
-                              in_=sc_raw[:].rearrange("p (b c t) -> p b t c", b=2, t=PACK))
-        for c0 in range(0, HALF, 2 * TOK):
-            gather(1, PACK - 1, 0, c0, c0 + 2 * TOK)
-            interleave(1, 0, c0, c0 + 2 * TOK)
-        permute(0, 0)
-        quantise_x(1, 0, 0, 2 * TOK)
-        permute(1, 0)
-        quantise_x(1, 0, 2 * TOK, HALF)
-        for u in range(8):
-            if u < PACK - 1:
-                unit(0, u, g4[1, 1][:, u + 1, :])
-                gather(1, u + 1, 1, 0, HALF)
+            quantise_x(0, HALF * h, g0[h][:])
+
+        g1 = [stage.tile([P, PACK, CHUNK], F32, name="g1") for c in range(3)]
+        for i in range(PACK - 1):
+            for c in range(3):
+                gather(g1[c][:, i, :], 1, i, CHUNK * c, CHUNK * (c + 1))
+
+        def last_plane(c):
+            gather(g1[c][:, PACK - 1, :], 1, PACK - 1, CHUNK * c, CHUNK * (c + 1))
+            for t in range(2):
+                quantise_x(1, CHUNK * c + TOK * t, g1[c][:, :, TOK * t:TOK * (t + 1)])
+
+        for c in range(3):
+            last_plane(c)
+        g1.append(stage.tile([P, PACK, CHUNK], F32, name="g1"))
+        for i in range(2):
+            gather(g1[3][:, i, :], 1, i, CHUNK * 3, CHUNK * 4)
+
+        def last_chunk():
+            gather(g1[3][:, 2, :], 1, 2, CHUNK * 3, CHUNK * 4)
+            last_plane(3)
+            win.append(keep.tile([P, T], F32, name="win3", tag="x13"))
+            nc.vector.memset(win[3][:], 0.0)
+
+        y_sb = keep.tile([P, PACK, J], F32, name="y_sb")
+
+        def first_product(m, b, t):
+            bank = ps1.tile([P, HALF], F32, name=f"bank{m}")
+            for a in range(2):
+                nc.tensor.matmul_mx(
+                    out=bank[:],
+                    lhsT=xq[a, t], lhsT_scale=xs[a, t],
+                    rhs=w_sb[m, b][:, a, :].bitcast(FP8X4),
+                    rhs_scale=w_sc[4 * m:, a, HALF * b:HALF * (b + 1)],
+                    start=(a == 0), stop=(a == 1))
+            return bank[:].rearrange("p (q u e) -> p u q e", u=2, e=2)
+
+        def hidden(b, t):
+            ga = first_product(0, b, t)
+            ub = first_product(1, b, t)
+            if (b, t) == (0, 0):
+                act = g1[3][:, 2:4, :].rearrange("p u (q e) -> p u q e", e=2)
             else:
-                unit(0, u)
-            if u == 0:
-                permute(0, 1)
-                permute(1, 1)
-        for c0 in range(0, HALF, 2 * TOK):
-            interleave(1, 1, c0, c0 + 2 * TOK)
-            quantise_x(1, 1, c0, c0 + 2 * TOK)
-        unit(1, 0)
-        second_product(0, 0)
-        for u in range(1, 5):
-            unit(1, u)
-        second_product(0, 1)
-        for u in range(5, 8):
-            unit(1, u)
-        second_product(0, 2)
-        for n in range(3):
-            second_product(1, n)
-        for h in range(2):
-            second_product(h, 3)
-        for h in range(2):
-            for n in range(3):
-                scatter(h, n)
-        for h in range(2):
-            scatter(h, 3)
+                act = ring.tile([P, 2, P, 2], F32, name="act")[:]
+            nc.scalar.activation(act, ga, GELU)
+            hid = ring.tile([P, 2, P, 2], BF16, name=f"hid{b}")
+            nc.vector.tensor_tensor(hid[:], ub, act, MULT)
+            return hid[:].rearrange("p u q e -> p (u q e)").bitcast(F32)
+
+        hq, hs = {}, {}
+
+        def turn(t, hid):
+            turned = ps2.tile([P, 2, 2, TOK], F32, name="turned")
+            for b in range(2):
+                for u in range(2):
+                    nc.tensor.transpose(turned[:, b, u, :], hid[b][:, P * u:P * (u + 1)], ident[:])
+            hb = ring.tile([P, 2 * TOK * PACK], BF16, name="hb", align_bytes=64)
+            nc.scalar.copy(hb[:].bitcast(F32).rearrange("p (b c u) -> p b c u", b=2, u=2), turned[:].rearrange("p b u c -> p b c u"))
+            hq[t] = ring.tile([P, 2 * TOK], U32, name="hq", align_bytes=64)
+            hs[t] = ring.tile([P, 2 * TOK], U8, name="hs", align_bytes=64)
+            nc.vector.quantize_mx(out=hq[t][:].bitcast(FP8X4), scales=hs[t][:], in_=hb[:])
+
+        def second_product(t, n0):
+            acc = ps2.tile([P, 2, TOK], F32, name="acc")
+            for n in range(n0, n0 + 2):
+                for b in range(2):
+                    nc.tensor.matmul_mx(
+                        out=acc[:, n - n0, :],
+                        lhsT=wd_sb[:, b, 2 * P * n:2 * P * (n + 1)].bitcast(FP4X4),
+                        lhsT_scale=wd_sc[:, b, P * n:P * (n + 1)],
+                        rhs=hq[t][:, TOK * b:TOK * (b + 1)].bitcast(FP8X4),
+                        rhs_scale=hs[t][:, TOK * b:TOK * (b + 1)],
+                        start=(b == 0), stop=(b == 1))
+            nc.scalar.copy(y_sb[:, n0:n0 + 2, TOK * t:TOK * (t + 1)], acc[:])
+            for n in range(n0, n0 + 2):
+                if t + 1 in cuts[n]:
+                    scatter(n, cuts[n][cuts[n].index(t + 1) - 1], t + 1)
+
+        def scatter(n, t0, t1):
+            c0, c1 = TOK * t0, TOK * t1
+            cols = place[:, c0 // PER_COL:c1 // PER_COL]
+            nc.vector.tensor_tensor(win[n][:].indirect(cols), y_sb[:, n, c0:c1], wgo_sb[:, c0:c1], MULT)
+            if c1 == J:
+                nc.sync.dma_start(out=out[P * n:P * (n + 1), :], in_=win[n][:])
+
+        tiles = J // TOK
+        every = list(range(tiles + 1))
+        cuts = [every, every, every, [0, 2, tiles]]
+        hid = {}
+        for t in range(tiles + 2):
+            if t < tiles:
+                hid[t, 0] = hidden(0, t)
+            if t == 0:
+                last_chunk()
+            if t >= 2:
+                second_product(t - 2, 0)
+            if 1 <= t <= tiles:
+                turn(t - 1, [hid[t - 1, b] for b in range(2)])
+            if t < tiles:
+                hid[t, 1] = hidden(1, t)
+            if t >= 2:
+                second_product(t - 2, 2)

@@ -22,6 +22,7 @@ PACK = 4
 HALF = 512
 CHUNK = 256
 TOK = 128
+EARLY = 768
 PER_COL = 16
 
 
@@ -29,14 +30,13 @@ def tile_list_gelu_scat_kernel(tc, xT, wgt, wg_words, wg_scales, wu_words, wu_sc
     nc = tc.nc
     with ExitStack() as ctx:
         keep = ctx.enter_context(tc.tile_pool(name="keep", bufs=1))
-        stage = ctx.enter_context(tc.tile_pool(name="stage", bufs=3))
         ring = ctx.enter_context(tc.tile_pool(name="ring", bufs=3))
         ps1 = ctx.enter_context(tc.psum_pool(name="ps1", bufs=3))
         ps2 = ctx.enter_context(tc.psum_pool(name="ps2", bufs=1))
 
         pick = keep.tile([P, J // PER_COL], U16, name="pick")
         place = keep.tile([P, J // PER_COL], U16, name="place")
-        wgt_sb = [keep.tile([P, HALF], F32, name=f"wgt{h}") for h in range(2)]
+        wgt_sb = keep.tile([P, J], F32, name="wgt_sb")
         wgo_sb = keep.tile([P, J], F32, name="wgo_sb")
         x_sb = [[keep.tile([P, T], F32, name=f"x{a}{i}") for i in range(PACK)] for a in range(2)]
         x_rows = xT.rearrange("(a p i) t -> a i p t", a=2, i=PACK)
@@ -45,9 +45,13 @@ def tile_list_gelu_scat_kernel(tc, xT, wgt, wg_words, wg_scales, wu_words, wu_sc
         nc.vector.memset(w_sc[:].rearrange("p a r -> p (a r)").bitcast(I32), 0)
         wd_sc = keep.tile([P, 2, N], U8, name="wd_sc", align_bytes=64)
         nc.vector.memset(wd_sc[:].rearrange("p a r -> p (a r)").bitcast(I32), 0)
-        win = [keep.tile([P, T], F32, name=f"win{n}") for n in range(3)]
-        for n in range(3):
+        win = [keep.tile([P, T], F32, name=f"win{n}") for n in range(PACK)]
+        for n in range(PACK):
             nc.vector.memset(win[n][:], 0.0)
+        warm = keep.tile([P, 8], F32, name="warm")
+        warm2 = keep.tile([P, 8], F32, name="warm2")
+        nc.gpsimd.memset(warm[:], 0.0)
+        nc.scalar.activation(warm2[:], warm[:], GELU)
         ident = keep.tile([P, P], F32, name="ident")
         make_identity(nc, ident[:])
 
@@ -64,7 +68,7 @@ def tile_list_gelu_scat_kernel(tc, xT, wgt, wg_words, wg_scales, wu_words, wu_sc
         load_plane(0)
         nc.sync.dma_start(pick[:], offs)
         for h in range(2):
-            nc.sync.dma_start(out=wgt_sb[h][:], in_=wgt[:, HALF * h:HALF * (h + 1)])
+            nc.sync.dma_start(out=wgt_sb[:, HALF * h:HALF * (h + 1)], in_=wgt[:, HALF * h:HALF * (h + 1)])
         for plane in range(1, 6):
             load_plane(plane)
         for plane in range(6, 8):
@@ -86,15 +90,14 @@ def tile_list_gelu_scat_kernel(tc, xT, wgt, wg_words, wg_scales, wu_words, wu_sc
         nc.sync.dma_start(out=wgo_sb[:], in_=wgo)
 
         def gather(dst, a, i, c0, c1):
-            h = c0 // HALF
             cols = pick[:, c0 // PER_COL:c1 // PER_COL]
-            nc.vector.tensor_tensor(dst, x_sb[a][i][:].indirect(cols), wgt_sb[h][:, c0 - HALF * h:c1 - HALF * h], MULT)
+            nc.vector.tensor_tensor(dst, x_sb[a][i][:].indirect(cols), wgt_sb[:, c0:c1], MULT)
 
         xq, xs = {}, {}
 
-        def quantise_x(a, c0, src):
+        def quantise_x(a, c0, src, tag=None):
             width = src.shape[2]
-            xb = keep.tile([P, width, PACK], BF16, name=f"xb{a}_{c0}", align_bytes=64)
+            xb = keep.tile([P, width, PACK], BF16, name=f"xb{a}_{c0}", tag=tag or f"xb{a}_{c0}", align_bytes=64)
             nc.scalar.copy(xb[:].rearrange("p (c e) i -> p c i e", e=4), src.rearrange("p i (c e) -> p c i e", e=4))
             codes = keep.tile([P, width], U32, name=f"xq{a}_{c0}", align_bytes=64)
             scales = keep.tile([P, width], U8, name=f"xs{a}_{c0}", align_bytes=64)
@@ -103,34 +106,28 @@ def tile_list_gelu_scat_kernel(tc, xT, wgt, wg_words, wg_scales, wu_words, wu_sc
                 xq[a, c0 // TOK + t] = codes[:, TOK * t:TOK * (t + 1)].bitcast(FP8X4)
                 xs[a, c0 // TOK + t] = scales[:, TOK * t:TOK * (t + 1)]
 
-        g0 = [keep.tile([P, PACK, HALF], F32, name=f"g0_{h}") for h in range(2)]
-        for i in range(PACK):
-            for h in range(2):
-                gather(g0[h][:, i, :], 0, i, HALF * h, HALF * (h + 1))
+        g0 = keep.tile([P, PACK, J], F32, name="g0")
         for h in range(2):
-            quantise_x(0, HALF * h, g0[h][:])
+            gather(g0[:, 0, HALF * h:HALF * (h + 1)], 0, 0, HALF * h, HALF * (h + 1))
+        for i in range(1, PACK):
+            gather(g0[:, i, :], 0, i, 0, J)
+        for h in range(2):
+            quantise_x(0, HALF * h, g0[:, :, HALF * h:HALF * (h + 1)])
 
-        g1 = [stage.tile([P, PACK, CHUNK], F32, name="g1") for c in range(3)]
+        g1 = keep.tile([P, PACK, EARLY], F32, name="g1")
         for i in range(PACK - 1):
-            for c in range(3):
-                gather(g1[c][:, i, :], 1, i, CHUNK * c, CHUNK * (c + 1))
-
-        def last_plane(c):
-            gather(g1[c][:, PACK - 1, :], 1, PACK - 1, CHUNK * c, CHUNK * (c + 1))
-            for t in range(2):
-                quantise_x(1, CHUNK * c + TOK * t, g1[c][:, :, TOK * t:TOK * (t + 1)])
-
-        for c in range(3):
-            last_plane(c)
-        g1.append(stage.tile([P, PACK, CHUNK], F32, name="g1"))
+            gather(g1[:, i, :], 1, i, 0, EARLY)
+        gather(g1[:, PACK - 1, 0:TOK], 1, PACK - 1, 0, TOK)
+        quantise_x(1, 0, g1[:, :, 0:TOK], "late")
+        gather(g1[:, PACK - 1, TOK:EARLY], 1, PACK - 1, TOK, EARLY)
+        quantise_x(1, TOK, g1[:, :, TOK:CHUNK])
+        late = keep.tile([P, PACK, CHUNK], F32, name="late", align_bytes=64)
         for i in range(2):
-            gather(g1[3][:, i, :], 1, i, CHUNK * 3, CHUNK * 4)
+            gather(late[:, i, :], 1, i, EARLY, J)
 
-        def last_chunk():
-            gather(g1[3][:, 2, :], 1, 2, CHUNK * 3, CHUNK * 4)
-            last_plane(3)
-            win.append(keep.tile([P, T], F32, name="win3", tag="x13"))
-            nc.vector.memset(win[3][:], 0.0)
+        def quantise_chunk(c):
+            src = g1[:, :, CHUNK * c:CHUNK * (c + 1)] if CHUNK * c < EARLY else late[:]
+            quantise_x(1, CHUNK * c, src)
 
         y_sb = keep.tile([P, PACK, J], F32, name="y_sb")
 
@@ -148,8 +145,8 @@ def tile_list_gelu_scat_kernel(tc, xT, wgt, wg_words, wg_scales, wu_words, wu_sc
         def hidden(b, t):
             ga = first_product(0, b, t)
             ub = first_product(1, b, t)
-            if (b, t) == (0, 0):
-                act = g1[3][:, 2:4, :].rearrange("p u (q e) -> p u q e", e=2)
+            if (b, t) == (1, 0):
+                act = late[:, 2:4, :].rearrange("p u (q e) -> p u q e", e=2)
             else:
                 act = ring.tile([P, 2, P, 2], F32, name="act")[:]
             nc.scalar.activation(act, ga, GELU)
@@ -161,7 +158,7 @@ def tile_list_gelu_scat_kernel(tc, xT, wgt, wg_words, wg_scales, wu_words, wu_sc
 
         def turn(t, hid):
             turned = ps2.tile([P, 2, 2, TOK], F32, name="turned")
-            for b in range(2):
+            for b in (1, 0):
                 for u in range(2):
                     nc.tensor.transpose(turned[:, b, u, :], hid[b][:, P * u:P * (u + 1)], ident[:])
             hb = ring.tile([P, 2 * TOK * PACK], BF16, name="hb", align_bytes=64)
@@ -195,18 +192,23 @@ def tile_list_gelu_scat_kernel(tc, xT, wgt, wg_words, wg_scales, wu_words, wu_sc
 
         tiles = J // TOK
         every = list(range(tiles + 1))
-        cuts = [every, every, every, [0, 2, tiles]]
+        cuts = [every[0::2], [0] + every[1::2] + [tiles], every[:5] + every[6:], [0, 2, tiles]]
         hid = {}
         for t in range(tiles + 2):
             if t < tiles:
                 hid[t, 0] = hidden(0, t)
-            if t == 0:
-                last_chunk()
+            if t == tiles:
+                turn(t - 1, [hid[t - 1, b] for b in range(2)])
             if t >= 2:
                 second_product(t - 2, 0)
-            if 1 <= t <= tiles:
+            if 1 <= t < tiles:
                 turn(t - 1, [hid[t - 1, b] for b in range(2)])
             if t < tiles:
                 hid[t, 1] = hidden(1, t)
+            if t == 0:
+                for i in range(2, PACK):
+                    gather(late[:, i, :], 1, i, EARLY, J)
             if t >= 2:
                 second_product(t - 2, 2)
+            if t % 2 == 1 and t + 1 < tiles:
+                quantise_chunk((t + 1) // 2)

@@ -22,7 +22,7 @@ PACK = 4
 HALF = 512
 CHUNK = 256
 TOK = 128
-EARLY = 768
+SPARE = 1
 PER_COL = 16
 
 
@@ -38,32 +38,27 @@ def tile_list_gelu_scat_kernel(tc, xT, wgt, wg_words, wg_scales, wu_words, wu_sc
         place = keep.tile([P, J // PER_COL], U16, name="place")
         wgt_sb = keep.tile([P, J], F32, name="wgt_sb")
         wgo_sb = keep.tile([P, J], F32, name="wgo_sb")
-        x_sb = [[keep.tile([P, T], F32, name=f"x{a}{i}") for i in range(PACK)] for a in range(2)]
+        x_sb = [[keep.tile([P, T], F32, name=f"x{a}{i}", align_bytes=64) for i in range(PACK)] for a in range(2)]
         x_rows = xT.rearrange("(a p i) t -> a i p t", a=2, i=PACK)
 
+        ident = keep.tile([P, P], F32, name="ident")
+        make_identity(nc, ident[:])
         w_sc = keep.tile([P, 2, R], U8, name="w_sc", align_bytes=64)
         nc.vector.memset(w_sc[:].rearrange("p a r -> p (a r)").bitcast(I32), 0)
         wd_sc = keep.tile([P, 2, N], U8, name="wd_sc", align_bytes=64)
         nc.vector.memset(wd_sc[:].rearrange("p a r -> p (a r)").bitcast(I32), 0)
-        win = [keep.tile([P, T], F32, name=f"win{n}") for n in range(PACK)]
-        for n in range(PACK):
-            nc.vector.memset(win[n][:], 0.0)
-        warm = keep.tile([P, 8], F32, name="warm")
-        warm2 = keep.tile([P, 8], F32, name="warm2")
-        nc.gpsimd.memset(warm[:], 0.0)
-        nc.scalar.activation(warm2[:], warm[:], GELU)
-        ident = keep.tile([P, P], F32, name="ident")
-        make_identity(nc, ident[:])
+        win = [keep.tile([P, T], F32, name=f"win{n}") for n in range(3)]
+        for n in range(3):
+            nc.vector.memset(win[n][:].bitcast(I32), 0)
 
         def load_plane(plane):
             a, i = divmod(plane, PACK)
             nc.sync.dma_start(out=x_sb[a][i][:], in_=x_rows[a, i])
 
         def load_scales(s):
-            m, q = divmod(s, 4)
-            lo = 32 * q + 4 * m
-            nc.sync.dma_start(out=w_sc[lo:lo + 4, :, :].bitcast(I32),
-                              in_=(wg_scales, wu_scales)[m][:, 4 * q:4 * q + 4, :].rearrange("a q r -> q a r").bitcast(I32))
+            row, m = divmod(s, 2)
+            nc.sync.dma_start(out=w_sc[4 * m + row:P:32, :, :].bitcast(I32),
+                              in_=(wg_scales, wu_scales)[m][:, row:16:4, :].rearrange("a q r -> q a r").bitcast(I32))
 
         load_plane(0)
         nc.sync.dma_start(pick[:], offs)
@@ -83,11 +78,14 @@ def tile_list_gelu_scat_kernel(tc, xT, wgt, wg_words, wg_scales, wu_words, wu_sc
                 nc.sync.dma_start(out=w_sb[m, b][:], in_=src.bitcast(I32))
         wd_sb = keep.tile([P, 2, 2 * N], U8, name="wd_sb", align_bytes=64)
         nc.sync.dma_start(out=wd_sb[:].bitcast(I32), in_=wd_words.rearrange("a p c -> p a c").bitcast(I32))
-        for q in range(4):
-            nc.sync.dma_start(out=wd_sc[32 * q:32 * q + 4, :, :].bitcast(I32),
-                              in_=wd_scales[:, 4 * q:4 * q + 4, :].rearrange("a q n -> q a n").bitcast(I32))
+        for row in range(4):
+            nc.sync.dma_start(out=wd_sc[row:P:32, :, :].bitcast(I32),
+                              in_=wd_scales[:, row:16:4, :].rearrange("a q n -> q a n").bitcast(I32))
         nc.sync.dma_start(place[:], offs2)
         nc.sync.dma_start(out=wgo_sb[:], in_=wgo)
+
+        warm = keep.tile([P, 8], F32, name="warm")
+        nc.scalar.activation(warm[:], win[0][:, 0:8], GELU)
 
         def gather(dst, a, i, c0, c1):
             cols = pick[:, c0 // PER_COL:c1 // PER_COL]
@@ -95,11 +93,12 @@ def tile_list_gelu_scat_kernel(tc, xT, wgt, wg_words, wg_scales, wu_words, wu_sc
 
         xq, xs = {}, {}
 
-        def quantise_x(a, c0, src, tag=None):
+        def quantise_x(a, c0, src, tag=None, xb=None, xtag=None):
             width = src.shape[2]
-            xb = keep.tile([P, width, PACK], BF16, name=f"xb{a}_{c0}", tag=tag or f"xb{a}_{c0}", align_bytes=64)
+            if xb is None:
+                xb = keep.tile([P, width, PACK], BF16, name=f"xb{a}_{c0}", tag=xtag or f"xb{a}_{c0}", align_bytes=64)
             nc.scalar.copy(xb[:].rearrange("p (c e) i -> p c i e", e=4), src.rearrange("p i (c e) -> p c i e", e=4))
-            codes = keep.tile([P, width], U32, name=f"xq{a}_{c0}", align_bytes=64)
+            codes = keep.tile([P, width], U32, name=f"xq{a}_{c0}", tag=tag or f"xq{a}_{c0}", align_bytes=64)
             scales = keep.tile([P, width], U8, name=f"xs{a}_{c0}", align_bytes=64)
             nc.vector.quantize_mx(out=codes[:].bitcast(FP8X4), scales=scales[:], in_=xb[:].rearrange("p c i -> p (c i)"))
             for t in range(width // TOK):
@@ -111,23 +110,21 @@ def tile_list_gelu_scat_kernel(tc, xT, wgt, wg_words, wg_scales, wu_words, wu_sc
             gather(g0[:, 0, HALF * h:HALF * (h + 1)], 0, 0, HALF * h, HALF * (h + 1))
         for i in range(1, PACK):
             gather(g0[:, i, :], 0, i, 0, J)
-        for h in range(2):
-            quantise_x(0, HALF * h, g0[:, :, HALF * h:HALF * (h + 1)])
-
-        g1 = keep.tile([P, PACK, EARLY], F32, name="g1")
-        for i in range(PACK - 1):
-            gather(g1[:, i, :], 1, i, 0, EARLY)
-        gather(g1[:, PACK - 1, 0:TOK], 1, PACK - 1, 0, TOK)
-        quantise_x(1, 0, g1[:, :, 0:TOK], "late")
-        gather(g1[:, PACK - 1, TOK:EARLY], 1, PACK - 1, TOK, EARLY)
-        quantise_x(1, TOK, g1[:, :, TOK:CHUNK])
-        late = keep.tile([P, PACK, CHUNK], F32, name="late", align_bytes=64)
+        g1 = [keep.tile([P, PACK, HALF], F32, name=f"g1_{h}", align_bytes=64) for h in range(2)]
         for i in range(2):
-            gather(late[:, i, :], 1, i, EARLY, J)
+            for h in range(2):
+                gather(g1[h][:, i, :], 1, i, HALF * h, HALF * (h + 1))
+        quantise_x(0, 0, g0[:, :, 0:HALF], "x11")
+        gather(g1[0][:, 2, :], 1, 2, 0, HALF)
+        gather(g1[0][:, 3, 0:TOK], 1, 3, 0, TOK)
+        quantise_x(1, 0, g1[0][:, :, 0:TOK], None, g1[1][:, 3, 0:CHUNK].bitcast(BF16).rearrange("p (c i) -> p c i", i=PACK))
+        gather(g1[0][:, 3, TOK:HALF], 1, 3, TOK, HALF)
+        quantise_x(1, TOK, g1[0][:, :, TOK:CHUNK])
+        gather(g1[1][:, 3, :], 1, 3, HALF, J)
 
         def quantise_chunk(c):
-            src = g1[:, :, CHUNK * c:CHUNK * (c + 1)] if CHUNK * c < EARLY else late[:]
-            quantise_x(1, CHUNK * c, src)
+            h, c0 = divmod(CHUNK * c, HALF)
+            quantise_x(1, CHUNK * c, g1[h][:, :, c0:c0 + CHUNK], None, None, f"codes{c}")
 
         y_sb = keep.tile([P, PACK, J], F32, name="y_sb")
 
@@ -146,11 +143,16 @@ def tile_list_gelu_scat_kernel(tc, xT, wgt, wg_words, wg_scales, wu_words, wu_sc
             ga = first_product(0, b, t)
             ub = first_product(1, b, t)
             if (b, t) == (1, 0):
-                act = late[:, 2:4, :].rearrange("p u (q e) -> p u q e", e=2)
+                act = g1[1][:, 2, :].rearrange("p (u q e) -> p u q e", u=2, e=2)
+            elif b == 0 and t < 2:
+                act = keep.tile([P, 2, P, 2], F32, name=f"act{t}", tag=f"codes{t}", align_bytes=64)[:]
             else:
                 act = ring.tile([P, 2, P, 2], F32, name="act")[:]
             nc.scalar.activation(act, ga, GELU)
-            hid = ring.tile([P, 2, P, 2], BF16, name=f"hid{b}")
+            if b == 0 and t in (1, 3):
+                hid = keep.tile([P, 2, P, 2], BF16, name=f"hid{t}", tag=f"codes{(t + 3) // 2}", align_bytes=64)
+            else:
+                hid = ring.tile([P, 2, P, 2], BF16, name=f"hid{b}")
             nc.vector.tensor_tensor(hid[:], ub, act, MULT)
             return hid[:].rearrange("p u q e -> p (u q e)").bitcast(F32)
 
@@ -161,15 +163,24 @@ def tile_list_gelu_scat_kernel(tc, xT, wgt, wg_words, wg_scales, wu_words, wu_sc
             for b in (1, 0):
                 for u in range(2):
                     nc.tensor.transpose(turned[:, b, u, :], hid[b][:, P * u:P * (u + 1)], ident[:])
-            hb = ring.tile([P, 2 * TOK * PACK], BF16, name="hb", align_bytes=64)
+            if t == 0:
+                hb = keep.tile([P, 2 * TOK * PACK], BF16, name="hb0", tag="win3", align_bytes=64)
+            else:
+                hb = ring.tile([P, 2 * TOK * PACK], BF16, name="hb", align_bytes=64)
             nc.scalar.copy(hb[:].bitcast(F32).rearrange("p (b c u) -> p b c u", b=2, u=2), turned[:].rearrange("p b u c -> p b c u"))
-            hq[t] = ring.tile([P, 2 * TOK], U32, name="hq", align_bytes=64)
-            hs[t] = ring.tile([P, 2 * TOK], U8, name="hs", align_bytes=64)
+            hq[t] = keep.tile([P, 2 * TOK], U32, name=f"hq{t}", align_bytes=64)
+            hs[t] = keep.tile([P, 2 * TOK], U8, name=f"hs{t}", align_bytes=64)
             nc.vector.quantize_mx(out=hq[t][:].bitcast(FP8X4), scales=hs[t][:], in_=hb[:])
+            if t == 0:
+                win.append(keep.tile([P, T], F32, name="win3", align_bytes=64))
+                nc.vector.memset(win[3][:].bitcast(I32), 0)
 
-        def second_product(t, n0):
-            acc = ps2.tile([P, 2, TOK], F32, name="acc")
-            for n in range(n0, n0 + 2):
+        def second_product(t, n0, n1, drain=False):
+            if drain:
+                acc = ps1.tile([P, n1 - n0, TOK], F32, name=f"bank{n0 // 2}")
+            else:
+                acc = ps2.tile([P, n1 - n0, TOK], F32, name="acc")
+            for n in range(n0, n1):
                 for b in range(2):
                     nc.tensor.matmul_mx(
                         out=acc[:, n - n0, :],
@@ -178,8 +189,8 @@ def tile_list_gelu_scat_kernel(tc, xT, wgt, wg_words, wg_scales, wu_words, wu_sc
                         rhs=hq[t][:, TOK * b:TOK * (b + 1)].bitcast(FP8X4),
                         rhs_scale=hs[t][:, TOK * b:TOK * (b + 1)],
                         start=(b == 0), stop=(b == 1))
-            nc.scalar.copy(y_sb[:, n0:n0 + 2, TOK * t:TOK * (t + 1)], acc[:])
-            for n in range(n0, n0 + 2):
+            nc.scalar.copy(y_sb[:, n0:n1, TOK * t:TOK * (t + 1)], acc[:])
+            for n in range(n0, n1):
                 if t + 1 in cuts[n]:
                     scatter(n, cuts[n][cuts[n].index(t + 1) - 1], t + 1)
 
@@ -192,7 +203,7 @@ def tile_list_gelu_scat_kernel(tc, xT, wgt, wg_words, wg_scales, wu_words, wu_sc
 
         tiles = J // TOK
         every = list(range(tiles + 1))
-        cuts = [every[0::2], [0] + every[1::2] + [tiles], every[:5] + every[6:], [0, 2, tiles]]
+        cuts = [[0] + every[1::2] + [tiles], every[0::2], every, [0, 1, 2, tiles]]
         hid = {}
         for t in range(tiles + 2):
             if t < tiles:
@@ -200,15 +211,19 @@ def tile_list_gelu_scat_kernel(tc, xT, wgt, wg_words, wg_scales, wu_words, wu_sc
             if t == tiles:
                 turn(t - 1, [hid[t - 1, b] for b in range(2)])
             if t >= 2:
-                second_product(t - 2, 0)
+                second_product(t - 2, 0, 2, t > tiles)
             if 1 <= t < tiles:
                 turn(t - 1, [hid[t - 1, b] for b in range(2)])
             if t < tiles:
                 hid[t, 1] = hidden(1, t)
             if t == 0:
-                for i in range(2, PACK):
-                    gather(late[:, i, :], 1, i, EARLY, J)
+                quantise_x(0, HALF, g0[:, :, HALF:J], "codes0")
+                gather(g1[1][:, 2, :], 1, 2, HALF, J)
             if t >= 2:
-                second_product(t - 2, 2)
-            if t % 2 == 1 and t + 1 < tiles:
-                quantise_chunk((t + 1) // 2)
+                second_product(t - 2, 2, 3 if t - 2 == SPARE else 4, t > tiles)
+            if t == tiles - 1:
+                second_product(SPARE, 3, 4)
+            if t == 1:
+                quantise_chunk(1)
+            if t in (2, 4):
+                quantise_chunk(t // 2 + 1)

@@ -22,7 +22,8 @@ PACK = 4
 HALF = 512
 CHUNK = 256
 TOK = 128
-SPARE = 1
+SPARE = 2
+BUFS = {"bank0": 3, "bank1": 3, "acc": 1}
 PER_COL = 16
 
 
@@ -31,8 +32,7 @@ def tile_list_gelu_scat_kernel(tc, xT, wgt, wg_words, wg_scales, wu_words, wu_sc
     with ExitStack() as ctx:
         keep = ctx.enter_context(tc.tile_pool(name="keep", bufs=1))
         ring = ctx.enter_context(tc.tile_pool(name="ring", bufs=3))
-        ps1 = ctx.enter_context(tc.psum_pool(name="ps1", bufs=3))
-        ps2 = ctx.enter_context(tc.psum_pool(name="ps2", bufs=1))
+        psum = ctx.enter_context(tc.psum_pool(name="psum", bufs=1))
 
         pick = keep.tile([P, J // PER_COL], U16, name="pick")
         place = keep.tile([P, J // PER_COL], U16, name="place")
@@ -47,23 +47,23 @@ def tile_list_gelu_scat_kernel(tc, xT, wgt, wg_words, wg_scales, wu_words, wu_sc
         nc.vector.memset(w_sc[:].rearrange("p a r -> p (a r)").bitcast(I32), 0)
         wd_sc = keep.tile([P, 2, N], U8, name="wd_sc", align_bytes=64)
         nc.vector.memset(wd_sc[:].rearrange("p a r -> p (a r)").bitcast(I32), 0)
-        win = [keep.tile([P, T], F32, name=f"win{n}") for n in range(3)]
-        for n in range(3):
-            nc.vector.memset(win[n][:].bitcast(I32), 0)
+        win = [keep.tile([P, T], F32, name=f"win{n}") for n in range(PACK)]
+        for n in range(PACK):
+            nc.vector.memset(win[n][:], 0.0)
 
         def load_plane(plane):
             a, i = divmod(plane, PACK)
             nc.sync.dma_start(out=x_sb[a][i][:], in_=x_rows[a, i])
 
         def load_scales(s):
-            row, m = divmod(s, 2)
-            nc.sync.dma_start(out=w_sc[4 * m + row:P:32, :, :].bitcast(I32),
-                              in_=(wg_scales, wu_scales)[m][:, row:16:4, :].rearrange("a q r -> q a r").bitcast(I32))
+            m, q = divmod(s, 4)
+            lo = 32 * q + 4 * m
+            nc.sync.dma_start(out=w_sc[lo:lo + 4, :, :].bitcast(I32),
+                              in_=(wg_scales, wu_scales)[m][:, 4 * q:4 * q + 4, :].rearrange("a q r -> q a r").bitcast(I32))
 
         load_plane(0)
         nc.sync.dma_start(pick[:], offs)
-        for h in range(2):
-            nc.sync.dma_start(out=wgt_sb[:, HALF * h:HALF * (h + 1)], in_=wgt[:, HALF * h:HALF * (h + 1)])
+        nc.sync.dma_start(out=wgt_sb[:], in_=wgt)
         for plane in range(1, 6):
             load_plane(plane)
         for plane in range(6, 8):
@@ -78,9 +78,9 @@ def tile_list_gelu_scat_kernel(tc, xT, wgt, wg_words, wg_scales, wu_words, wu_sc
                 nc.sync.dma_start(out=w_sb[m, b][:], in_=src.bitcast(I32))
         wd_sb = keep.tile([P, 2, 2 * N], U8, name="wd_sb", align_bytes=64)
         nc.sync.dma_start(out=wd_sb[:].bitcast(I32), in_=wd_words.rearrange("a p c -> p a c").bitcast(I32))
-        for row in range(4):
-            nc.sync.dma_start(out=wd_sc[row:P:32, :, :].bitcast(I32),
-                              in_=wd_scales[:, row:16:4, :].rearrange("a q n -> q a n").bitcast(I32))
+        for q in range(4):
+            nc.sync.dma_start(out=wd_sc[32 * q:32 * q + 4, :, :].bitcast(I32),
+                              in_=wd_scales[:, 4 * q:4 * q + 4, :].rearrange("a q n -> q a n").bitcast(I32))
         nc.sync.dma_start(place[:], offs2)
         nc.sync.dma_start(out=wgo_sb[:], in_=wgo)
 
@@ -106,9 +106,7 @@ def tile_list_gelu_scat_kernel(tc, xT, wgt, wg_words, wg_scales, wu_words, wu_sc
                 xs[a, c0 // TOK + t] = scales[:, TOK * t:TOK * (t + 1)]
 
         g0 = keep.tile([P, PACK, J], F32, name="g0")
-        for h in range(2):
-            gather(g0[:, 0, HALF * h:HALF * (h + 1)], 0, 0, HALF * h, HALF * (h + 1))
-        for i in range(1, PACK):
+        for i in range(PACK):
             gather(g0[:, i, :], 0, i, 0, J)
         g1 = [keep.tile([P, PACK, HALF], F32, name=f"g1_{h}", align_bytes=64) for h in range(2)]
         for i in range(2):
@@ -129,7 +127,7 @@ def tile_list_gelu_scat_kernel(tc, xT, wgt, wg_words, wg_scales, wu_words, wu_sc
         y_sb = keep.tile([P, PACK, J], F32, name="y_sb")
 
         def first_product(m, b, t):
-            bank = ps1.tile([P, HALF], F32, name=f"bank{m}")
+            bank = psum.tile([P, HALF], F32, name=f"bank{m}", bufs=BUFS[f"bank{m}"])
             for a in range(2):
                 nc.tensor.matmul_mx(
                     out=bank[:],
@@ -159,40 +157,32 @@ def tile_list_gelu_scat_kernel(tc, xT, wgt, wg_words, wg_scales, wu_words, wu_sc
         hq, hs = {}, {}
 
         def turn(t, hid):
-            turned = ps2.tile([P, 2, 2, TOK], F32, name="turned")
+            turned = psum.tile([P, 2, 2, TOK], F32, name="turned")
             for b in (1, 0):
                 for u in range(2):
                     nc.tensor.transpose(turned[:, b, u, :], hid[b][:, P * u:P * (u + 1)], ident[:])
-            if t == 0:
-                hb = keep.tile([P, 2 * TOK * PACK], BF16, name="hb0", tag="win3", align_bytes=64)
-            else:
-                hb = ring.tile([P, 2 * TOK * PACK], BF16, name="hb", align_bytes=64)
+            hb = ring.tile([P, 2 * TOK * PACK], BF16, name="hb", align_bytes=64)
             nc.scalar.copy(hb[:].bitcast(F32).rearrange("p (b c u) -> p b c u", b=2, u=2), turned[:].rearrange("p b u c -> p b c u"))
             hq[t] = keep.tile([P, 2 * TOK], U32, name=f"hq{t}", align_bytes=64)
             hs[t] = keep.tile([P, 2 * TOK], U8, name=f"hs{t}", align_bytes=64)
             nc.vector.quantize_mx(out=hq[t][:].bitcast(FP8X4), scales=hs[t][:], in_=hb[:])
-            if t == 0:
-                win.append(keep.tile([P, T], F32, name="win3", align_bytes=64))
-                nc.vector.memset(win[3][:].bitcast(I32), 0)
 
-        def second_product(t, n0, n1, drain=False):
-            if drain:
-                acc = ps1.tile([P, n1 - n0, TOK], F32, name=f"bank{n0 // 2}")
-            else:
-                acc = ps2.tile([P, n1 - n0, TOK], F32, name="acc")
+        def second_product(t0, t1, n0, n1, pool, tag):
+            acc = pool.tile([P, n1 - n0, (t1 - t0) * TOK], F32, name=tag, bufs=BUFS[tag])
             for n in range(n0, n1):
-                for b in range(2):
-                    nc.tensor.matmul_mx(
-                        out=acc[:, n - n0, :],
-                        lhsT=wd_sb[:, b, 2 * P * n:2 * P * (n + 1)].bitcast(FP4X4),
-                        lhsT_scale=wd_sc[:, b, P * n:P * (n + 1)],
-                        rhs=hq[t][:, TOK * b:TOK * (b + 1)].bitcast(FP8X4),
-                        rhs_scale=hs[t][:, TOK * b:TOK * (b + 1)],
-                        start=(b == 0), stop=(b == 1))
-            nc.scalar.copy(y_sb[:, n0:n1, TOK * t:TOK * (t + 1)], acc[:])
+                for t in range(t0, t1):
+                    for b in range(2):
+                        nc.tensor.matmul_mx(
+                            out=acc[:, n - n0, TOK * (t - t0):TOK * (t - t0 + 1)],
+                            lhsT=wd_sb[:, b, 2 * P * n:2 * P * (n + 1)].bitcast(FP4X4),
+                            lhsT_scale=wd_sc[:, b, P * n:P * (n + 1)],
+                            rhs=hq[t][:, TOK * b:TOK * (b + 1)].bitcast(FP8X4),
+                            rhs_scale=hs[t][:, TOK * b:TOK * (b + 1)],
+                            start=(b == 0), stop=(b == 1))
+            nc.scalar.copy(y_sb[:, n0:n1, TOK * t0:TOK * t1], acc[:])
             for n in range(n0, n1):
-                if t + 1 in cuts[n]:
-                    scatter(n, cuts[n][cuts[n].index(t + 1) - 1], t + 1)
+                if t1 in cuts[n]:
+                    scatter(n, cuts[n][cuts[n].index(t1) - 1], t1)
 
         def scatter(n, t0, t1):
             c0, c1 = TOK * t0, TOK * t1
@@ -202,16 +192,17 @@ def tile_list_gelu_scat_kernel(tc, xT, wgt, wg_words, wg_scales, wu_words, wu_sc
                 nc.sync.dma_start(out=out[P * n:P * (n + 1), :], in_=win[n][:])
 
         tiles = J // TOK
+        last = tiles - 1
         every = list(range(tiles + 1))
-        cuts = [[0] + every[1::2] + [tiles], every[0::2], every, [0, 1, 2, tiles]]
+        cuts = [[0] + every[1::2] + [tiles], every[0::2], every, every[:SPARE + 2] + [tiles]]
         hid = {}
-        for t in range(tiles + 2):
+        for t in range(tiles + 1):
             if t < tiles:
                 hid[t, 0] = hidden(0, t)
-            if t == tiles:
-                turn(t - 1, [hid[t - 1, b] for b in range(2)])
+            else:
+                turn(last, [hid[last, b] for b in range(2)])
             if t >= 2:
-                second_product(t - 2, 0, 2, t > tiles)
+                second_product(t - 2, t - 1, 0, 2, psum, "acc")
             if 1 <= t < tiles:
                 turn(t - 1, [hid[t - 1, b] for b in range(2)])
             if t < tiles:
@@ -220,10 +211,13 @@ def tile_list_gelu_scat_kernel(tc, xT, wgt, wg_words, wg_scales, wu_words, wu_sc
                 quantise_x(0, HALF, g0[:, :, HALF:J], "codes0")
                 gather(g1[1][:, 2, :], 1, 2, HALF, J)
             if t >= 2:
-                second_product(t - 2, 2, 3 if t - 2 == SPARE else 4, t > tiles)
-            if t == tiles - 1:
-                second_product(SPARE, 3, 4)
+                second_product(t - 2, t - 1, 2, 4 if t - 2 < SPARE else 3, psum, "acc")
+            if t == last:
+                second_product(SPARE, SPARE + 1, 3, 4, psum, "acc")
             if t == 1:
                 quantise_chunk(1)
             if t in (2, 4):
                 quantise_chunk(t // 2 + 1)
+        second_product(SPARE + 1, last, 3, 4, psum, "bank1")
+        second_product(last, tiles, 0, 2, psum, "bank0")
+        second_product(last, tiles, 2, 4, psum, "bank1")

@@ -22,7 +22,7 @@ PACK = 4
 HALF = 512
 CHUNK = 256
 TOK = 128
-SPARE = 2
+SPARE = 1
 BUFS = {"bank0": 3, "bank1": 3, "acc": 1}
 PER_COL = 16
 
@@ -138,8 +138,12 @@ def tile_list_gelu_scat_kernel(tc, xT, wgt, wg_words, wg_scales, wu_words, wu_sc
             return bank[:].rearrange("p (q u e) -> p u q e", u=2, e=2)
 
         def hidden(b, t):
-            ga = first_product(0, b, t)
-            ub = first_product(1, b, t)
+            if t == 0:
+                ga = first_product(0, b, t)
+                ub = first_product(1, b, t)
+            else:
+                ub = first_product(1, b, t)
+                ga = first_product(0, b, t)
             if (b, t) == (1, 0):
                 act = g1[1][:, 2, :].rearrange("p (u q e) -> p u q e", u=2, e=2)
             elif b == 0 and t < 2:
@@ -218,6 +222,7 @@ def tile_list_gelu_scat_kernel(tc, xT, wgt, wg_words, wg_scales, wu_words, wu_sc
                 quantise_chunk(1)
             if t in (2, 4):
                 quantise_chunk(t // 2 + 1)
-        second_product(SPARE + 1, last, 3, 4, psum, "bank1")
+        second_product(SPARE + 1, last - 1, 3, 4, psum, "bank1")
+        second_product(last - 1, last, 3, 4, psum, "bank0")
         second_product(last, tiles, 0, 2, psum, "bank0")
         second_product(last, tiles, 2, 4, psum, "bank1")

@@ -22,9 +22,16 @@ PACK = 4
 HALF = 512
 CHUNK = 256
 TOK = 128
-SPARE = 1
-BUFS = {"bank0": 3, "bank1": 3, "acc": 1}
 PER_COL = 16
+BUFS = {"bank0": 3, "bank1": 3, "acc": 1, "turned": 1}
+SLOTS = {
+    2: [(2, 0, 1), (3, 0, 1)],
+    3: [(0, 1, 2), (1, 1, 2), (2, 1, 2)],
+    4: [(3, 1, 3), (0, 2, 3)],
+    5: [(1, 2, 4), (2, 2, 3)],
+    6: [(0, 3, 5), (2, 3, 4)],
+    7: [(1, 4, 6), (2, 4, 6)],
+}
 
 
 def tile_list_gelu_scat_kernel(tc, xT, wgt, wg_words, wg_scales, wu_words, wu_scales, wd_words, wd_scales, wgo, offs, offs2, out):
@@ -48,8 +55,10 @@ def tile_list_gelu_scat_kernel(tc, xT, wgt, wg_words, wg_scales, wu_words, wu_sc
         wd_sc = keep.tile([P, 2, N], U8, name="wd_sc", align_bytes=64)
         nc.vector.memset(wd_sc[:].rearrange("p a r -> p (a r)").bitcast(I32), 0)
         win = [keep.tile([P, T], F32, name=f"win{n}") for n in range(PACK)]
-        for n in range(PACK):
-            nc.vector.memset(win[n][:], 0.0)
+        for n in range(2):
+            nc.vector.memset(win[n][:, 0:T - 1], 0.0)
+            nc.vector.memset(win[n][:, T - 1:T], 0.0)
+            nc.gpsimd.memset(win[2 + n][:], 0.0)
 
         def load_plane(plane):
             a, i = divmod(plane, PACK)
@@ -66,16 +75,26 @@ def tile_list_gelu_scat_kernel(tc, xT, wgt, wg_words, wg_scales, wu_words, wu_sc
         nc.sync.dma_start(out=wgt_sb[:], in_=wgt)
         for plane in range(1, 6):
             load_plane(plane)
-        for plane in range(6, 8):
-            for s in range(4 * (plane - 6), 4 * (plane - 5)):
-                load_scales(s)
-            load_plane(plane)
         w_sb = {}
-        for b in range(2):
-            for m, words in enumerate((wg_words, wu_words)):
-                w_sb[m, b] = keep.tile([P, 2, HALF], I32, name=f"w_sb{m}{b}", align_bytes=64)
-                src = words.rearrange("a p r i -> p a (r i)")[:, :, 2048 * b:2048 * (b + 1)]
-                nc.sync.dma_start(out=w_sb[m, b][:], in_=src.bitcast(I32))
+
+        def load_weights(m, a, b0, b1):
+            piece = keep.tile([P, (b1 - b0) * HALF], I32, name=f"w_sb{m}{a}{b0}", align_bytes=64)
+            src = (wg_words, wu_words)[m][a].rearrange("p r i -> p (r i)")[:, 2048 * b0:2048 * b1]
+            nc.sync.dma_start(out=piece[:], in_=src.bitcast(I32))
+            for b in range(b0, b1):
+                w_sb[m, b, a] = piece[:, HALF * (b - b0):HALF * (b - b0 + 1)].bitcast(FP8X4)
+
+        for s in range(4):
+            load_scales(s)
+        load_plane(6)
+        for s in range(4, 8):
+            load_scales(s)
+        load_weights(0, 0, 0, 2)
+        load_plane(7)
+        load_weights(1, 0, 0, 2)
+        load_weights(0, 1, 0, 2)
+        load_weights(1, 1, 0, 1)
+        load_weights(1, 1, 1, 2)
         wd_sb = keep.tile([P, 2, 2 * N], U8, name="wd_sb", align_bytes=64)
         nc.sync.dma_start(out=wd_sb[:].bitcast(I32), in_=wd_words.rearrange("a p c -> p a c").bitcast(I32))
         for q in range(4):
@@ -87,142 +106,156 @@ def tile_list_gelu_scat_kernel(tc, xT, wgt, wg_words, wg_scales, wu_words, wu_sc
         warm = keep.tile([P, 8], F32, name="warm")
         nc.scalar.activation(warm[:], win[0][:, 0:8], GELU)
 
-        def gather(dst, a, i, c0, c1):
+        g0 = keep.tile([P, PACK, J], F32, name="g0")
+        g1 = keep.tile([P, PACK, J], F32, name="g1", align_bytes=64)
+
+        def staged(a, c0, c1):
+            return (g0, g1)[a][:, :, c0:c1]
+
+        def gather(a, i, c0, c1):
             cols = pick[:, c0 // PER_COL:c1 // PER_COL]
-            nc.vector.tensor_tensor(dst, x_sb[a][i][:].indirect(cols), wgt_sb[:, c0:c1], MULT)
+            nc.vector.tensor_tensor(staged(a, c0, c1)[:, i, :], x_sb[a][i][:].indirect(cols), wgt_sb[:, c0:c1], MULT)
 
         xq, xs = {}, {}
 
-        def quantise_x(a, c0, src, tag=None, xb=None, xtag=None):
-            width = src.shape[2]
-            if xb is None:
-                xb = keep.tile([P, width, PACK], BF16, name=f"xb{a}_{c0}", tag=xtag or f"xb{a}_{c0}", align_bytes=64)
-            nc.scalar.copy(xb[:].rearrange("p (c e) i -> p c i e", e=4), src.rearrange("p i (c e) -> p c i e", e=4))
-            codes = keep.tile([P, width], U32, name=f"xq{a}_{c0}", tag=tag or f"xq{a}_{c0}", align_bytes=64)
+        def quantise_x(a, c0, c1, codes_tag, xb_tag, weave=nc.scalar.copy):
+            width = c1 - c0
+            if xb_tag is None:
+                xb = g1[:, 3, J - 2 * width:J].bitcast(BF16).rearrange("p (c i) -> p c i", i=PACK)
+            else:
+                xb = keep.tile([P, width, PACK], BF16, name=f"xb{a}_{c0}", tag=xb_tag, align_bytes=64)[:]
+            weave(xb.rearrange("p (c e) i -> p c i e", e=4), staged(a, c0, c1).rearrange("p i (c e) -> p c i e", e=4))
+            codes = keep.tile([P, width], U32, name=f"xq{a}_{c0}", tag=codes_tag, align_bytes=64)
             scales = keep.tile([P, width], U8, name=f"xs{a}_{c0}", align_bytes=64)
-            nc.vector.quantize_mx(out=codes[:].bitcast(FP8X4), scales=scales[:], in_=xb[:].rearrange("p c i -> p (c i)"))
+            nc.vector.quantize_mx(out=codes[:].bitcast(FP8X4), scales=scales[:], in_=xb.rearrange("p c i -> p (c i)"))
             for t in range(width // TOK):
                 xq[a, c0 // TOK + t] = codes[:, TOK * t:TOK * (t + 1)].bitcast(FP8X4)
                 xs[a, c0 // TOK + t] = scales[:, TOK * t:TOK * (t + 1)]
+            return codes
 
-        g0 = keep.tile([P, PACK, J], F32, name="g0")
-        for i in range(PACK):
-            gather(g0[:, i, :], 0, i, 0, J)
-        g1 = [keep.tile([P, PACK, HALF], F32, name=f"g1_{h}", align_bytes=64) for h in range(2)]
-        for i in range(2):
-            for h in range(2):
-                gather(g1[h][:, i, :], 1, i, HALF * h, HALF * (h + 1))
-        quantise_x(0, 0, g0[:, :, 0:HALF], "x11")
-        gather(g1[0][:, 2, :], 1, 2, 0, HALF)
-        gather(g1[0][:, 3, 0:TOK], 1, 3, 0, TOK)
-        quantise_x(1, 0, g1[0][:, :, 0:TOK], None, g1[1][:, 3, 0:CHUNK].bitcast(BF16).rearrange("p (c i) -> p c i", i=PACK))
-        gather(g1[0][:, 3, TOK:HALF], 1, 3, TOK, HALF)
-        quantise_x(1, TOK, g1[0][:, :, TOK:CHUNK])
-        gather(g1[1][:, 3, :], 1, 3, HALF, J)
+        for i in range(3):
+            gather(0, i, 0, J)
+        gather(0, 3, 0, HALF)
+        gather(0, 3, HALF, J)
+        gather(1, 0, 0, J)
+        quantise_x(0, 0, HALF, "x10", "xb00")
+        gather(1, 1, 0, J)
+        gather(1, 2, 0, J)
+        gather(1, 3, 0, TOK)
+        quantise_x(1, 0, TOK, "xq10", "xb10")
+        gather(1, 3, TOK, 3 * TOK)
+        gather(1, 3, 3 * TOK, 5 * TOK)
+        quantise_x(1, TOK, 2 * TOK, "xq11", None)
+        gather(1, 3, 5 * TOK, J)
+        quantise_x(1, 2 * TOK, 3 * TOK, "xq15", "xb15")
 
-        def quantise_chunk(c):
-            h, c0 = divmod(CHUNK * c, HALF)
-            quantise_x(1, CHUNK * c, g1[h][:, :, c0:c0 + CHUNK], None, None, f"codes{c}")
+        banks = {}
 
-        y_sb = keep.tile([P, PACK, J], F32, name="y_sb")
+        def first_pass(m, b, t, a):
+            if a == 0:
+                tag = f"bank{(m + (2 * t + b) // 3) % 2}"
+                banks[m, b, t] = psum.tile([P, HALF], F32, name=tag, bufs=BUFS[tag])
+            nc.tensor.matmul_mx(
+                out=banks[m, b, t][:],
+                lhsT=xq[a, t], lhsT_scale=xs[a, t],
+                rhs=w_sb[m, b, a],
+                rhs_scale=w_sc[4 * m:, a, HALF * b:HALF * (b + 1)],
+                start=(a == 0), stop=(a == 1))
 
-        def first_product(m, b, t):
-            bank = psum.tile([P, HALF], F32, name=f"bank{m}", bufs=BUFS[f"bank{m}"])
-            for a in range(2):
-                nc.tensor.matmul_mx(
-                    out=bank[:],
-                    lhsT=xq[a, t], lhsT_scale=xs[a, t],
-                    rhs=w_sb[m, b][:, a, :].bitcast(FP8X4),
-                    rhs_scale=w_sc[4 * m:, a, HALF * b:HALF * (b + 1)],
-                    start=(a == 0), stop=(a == 1))
-            return bank[:].rearrange("p (q u e) -> p u q e", u=2, e=2)
+        hid = {}
 
         def hidden(b, t):
-            if t == 0:
-                ga = first_product(0, b, t)
-                ub = first_product(1, b, t)
-            else:
-                ub = first_product(1, b, t)
-                ga = first_product(0, b, t)
-            if (b, t) == (1, 0):
-                act = g1[1][:, 2, :].rearrange("p (u q e) -> p u q e", u=2, e=2)
-            elif b == 0 and t < 2:
-                act = keep.tile([P, 2, P, 2], F32, name=f"act{t}", tag=f"codes{t}", align_bytes=64)[:]
-            else:
-                act = ring.tile([P, 2, P, 2], F32, name="act")[:]
+            for m in ((0, 1) if 2 * t + b < 3 else (1, 0)):
+                for a in range(2):
+                    if a == 1 or (m, b, t) not in banks:
+                        first_pass(m, b, t, a)
+            ga, ub = (banks[m, b, t][:].rearrange("p (q u e) -> p u q e", u=2, e=2) for m in range(2))
+            act = ring.tile([P, 2, P, 2], F32, name="act")[:]
             nc.scalar.activation(act, ga, GELU)
-            if b == 0 and t in (1, 3):
-                hid = keep.tile([P, 2, P, 2], BF16, name=f"hid{t}", tag=f"codes{(t + 3) // 2}", align_bytes=64)
-            else:
-                hid = ring.tile([P, 2, P, 2], BF16, name=f"hid{b}")
-            nc.vector.tensor_tensor(hid[:], ub, act, MULT)
-            return hid[:].rearrange("p u q e -> p (u q e)").bitcast(F32)
+            words = ring.tile([P, 2, P, 2], BF16, name=f"hid{b}")
+            nc.vector.tensor_tensor(words[:], ub, act, MULT)
+            hid[t, b] = words[:].rearrange("p u q e -> p (u q e)").bitcast(F32)
 
         hq, hs = {}, {}
 
-        def turn(t, hid):
-            turned = psum.tile([P, 2, 2, TOK], F32, name="turned")
-            for b in (1, 0):
+        def turn(t, b0, b1, tag="turned", hb_tag=None):
+            nb = b1 - b0
+            turned = psum.tile([P, nb, 2, TOK], F32, name=tag, bufs=BUFS[tag])
+            for b in range(b1 - 1, b0 - 1, -1):
                 for u in range(2):
-                    nc.tensor.transpose(turned[:, b, u, :], hid[b][:, P * u:P * (u + 1)], ident[:])
-            hb = ring.tile([P, 2 * TOK * PACK], BF16, name="hb", align_bytes=64)
-            nc.scalar.copy(hb[:].bitcast(F32).rearrange("p (b c u) -> p b c u", b=2, u=2), turned[:].rearrange("p b u c -> p b c u"))
-            hq[t] = keep.tile([P, 2 * TOK], U32, name=f"hq{t}", align_bytes=64)
-            hs[t] = keep.tile([P, 2 * TOK], U8, name=f"hs{t}", align_bytes=64)
-            nc.vector.quantize_mx(out=hq[t][:].bitcast(FP8X4), scales=hs[t][:], in_=hb[:])
+                    nc.tensor.transpose(turned[:, b - b0, u, :], hid[t, b][:, P * u:P * (u + 1)], ident[:])
+            if hb_tag is None:
+                hb = ring.tile([P, nb * TOK * PACK], BF16, name="hb", align_bytes=64)[:]
+            else:
+                hb = keep.tile([P, nb * TOK * PACK], BF16, name=f"hb{t}", tag=hb_tag, align_bytes=64)[:]
+            nc.scalar.copy(hb.bitcast(F32).rearrange("p (b c u) -> p b c u", b=nb, u=2), turned[:].rearrange("p b u c -> p b c u"))
+            codes = keep.tile([P, nb * TOK], U32, name=f"hq{t}_{b0}", align_bytes=64)
+            scales = keep.tile([P, nb * TOK], U8, name=f"hs{t}_{b0}", align_bytes=64)
+            nc.vector.quantize_mx(out=codes[:].bitcast(FP8X4), scales=scales[:], in_=hb)
+            for b in range(b0, b1):
+                hq[t, b] = codes[:, TOK * (b - b0):TOK * (b - b0 + 1)].bitcast(FP8X4)
+                hs[t, b] = scales[:, TOK * (b - b0):TOK * (b - b0 + 1)]
 
-        def second_product(t0, t1, n0, n1, pool, tag):
-            acc = pool.tile([P, n1 - n0, (t1 - t0) * TOK], F32, name=tag, bufs=BUFS[tag])
-            for n in range(n0, n1):
-                for t in range(t0, t1):
-                    for b in range(2):
-                        nc.tensor.matmul_mx(
-                            out=acc[:, n - n0, TOK * (t - t0):TOK * (t - t0 + 1)],
-                            lhsT=wd_sb[:, b, 2 * P * n:2 * P * (n + 1)].bitcast(FP4X4),
-                            lhsT_scale=wd_sc[:, b, P * n:P * (n + 1)],
-                            rhs=hq[t][:, TOK * b:TOK * (b + 1)].bitcast(FP8X4),
-                            rhs_scale=hs[t][:, TOK * b:TOK * (b + 1)],
-                            start=(b == 0), stop=(b == 1))
-            nc.scalar.copy(y_sb[:, n0:n1, TOK * t0:TOK * t1], acc[:])
-            for n in range(n0, n1):
-                if t1 in cuts[n]:
-                    scatter(n, cuts[n][cuts[n].index(t1) - 1], t1)
+        def multiply(units, tag, y):
+            acc = psum.tile([P, len(units) * TOK], F32, name=tag, bufs=BUFS[tag])
+            for k, (n, t) in enumerate(units):
+                for b in range(2):
+                    nc.tensor.matmul_mx(
+                        out=acc[:, TOK * k:TOK * (k + 1)],
+                        lhsT=wd_sb[:, b, 2 * P * n:2 * P * (n + 1)].bitcast(FP4X4),
+                        lhsT_scale=wd_sc[:, b, P * n:P * (n + 1)],
+                        rhs=hq[t, b], rhs_scale=hs[t, b],
+                        start=(b == 0), stop=(b == 1))
+            nc.scalar.copy(y, acc[:])
 
-        def scatter(n, t0, t1):
+        def scatter(n, t0, t1, y):
             c0, c1 = TOK * t0, TOK * t1
             cols = place[:, c0 // PER_COL:c1 // PER_COL]
-            nc.vector.tensor_tensor(win[n][:].indirect(cols), y_sb[:, n, c0:c1], wgo_sb[:, c0:c1], MULT)
+            nc.vector.tensor_tensor(win[n][:].indirect(cols), y, wgo_sb[:, c0:c1], MULT)
             if c1 == J:
                 nc.sync.dma_start(out=out[P * n:P * (n + 1), :], in_=win[n][:])
 
+        def second_product(pieces, tag):
+            units = [(n, t) for n, t0, t1 in pieces for t in range(t0, t1)]
+            y = ring.tile([P, len(units) * TOK], F32, name="y", bufs=4)
+            multiply(units, tag, y[:])
+            k = 0
+            for n, t0, t1 in pieces:
+                scatter(n, t0, t1, y[:, k:k + TOK * (t1 - t0)])
+                k = k + TOK * (t1 - t0)
+            return y
+
+        for m in range(2):
+            for b, t in ((0, 0), (1, 0), (0, 1)):
+                first_pass(m, b, t, 0)
+        hidden(0, 0)
+        hidden(1, 0)
+        turn(0, 0, 1, "turned", "late0")
+        turn(0, 1, 2, "bank1", "late1")
+        quantise_x(1, 3 * TOK, 5 * TOK, "xq12", "late0", nc.vector.tensor_copy)
+        quantise_x(0, HALF, J, "late1", "xb01")
+        hidden(0, 1)
+        hidden(1, 1)
+        second_product([(0, 0, 1)], "turned")
+        hidden(0, 2)
+        turn(1, 0, 2)
+        second_product([(1, 0, 1)], "acc")
         tiles = J // TOK
-        last = tiles - 1
-        every = list(range(tiles + 1))
-        cuts = [[0] + every[1::2] + [tiles], every[0::2], every, every[:SPARE + 2] + [tiles]]
-        hid = {}
-        for t in range(tiles + 1):
-            if t < tiles:
-                hid[t, 0] = hidden(0, t)
-            else:
-                turn(last, [hid[last, b] for b in range(2)])
-            if t >= 2:
-                second_product(t - 2, t - 1, 0, 2, psum, "acc")
-            if 1 <= t < tiles:
-                turn(t - 1, [hid[t - 1, b] for b in range(2)])
-            if t < tiles:
-                hid[t, 1] = hidden(1, t)
-            if t == 0:
-                quantise_x(0, HALF, g0[:, :, HALF:J], "codes0")
-                gather(g1[1][:, 2, :], 1, 2, HALF, J)
-            if t >= 2:
-                second_product(t - 2, t - 1, 2, 4 if t - 2 < SPARE else 3, psum, "acc")
-            if t == last:
-                second_product(SPARE, SPARE + 1, 3, 4, psum, "acc")
-            if t == 1:
-                quantise_chunk(1)
-            if t in (2, 4):
-                quantise_chunk(t // 2 + 1)
-        second_product(SPARE + 1, last - 1, 3, 4, psum, "bank1")
-        second_product(last - 1, last, 3, 4, psum, "bank0")
-        second_product(last, tiles, 0, 2, psum, "bank0")
-        second_product(last, tiles, 2, 4, psum, "bank1")
+        for t in range(2, tiles):
+            hidden(1, t)
+            second_product(SLOTS[t], "acc")
+            if t == 2:
+                quantise_x(1, 5 * TOK, 7 * TOK, "xq13", "hq0_0")
+            if t == 4:
+                quantise_x(1, 7 * TOK, J, "xq14", "hq1_0")
+            if t + 1 < tiles:
+                hidden(0, t + 1)
+            turn(t, 0, 2)
+        second_product([(0, 5, 7), (1, 6, 7)], "turned")
+        second_product([(0, 7, 8)], "acc")
+        second_product([(1, 7, 8)], "bank1")
+        second_product([(2, 6, 8)], "bank0")
+        y_last = keep.tile([P, 5 * TOK], F32, name="y_last")
+        multiply([(3, t) for t in range(3, 7)], "bank1", y_last[:, 0:HALF])
+        multiply([(3, 7)], "bank0", y_last[:, HALF:5 * TOK])
+        scatter(3, 3, 8, y_last[:])

@@ -26,11 +26,11 @@ PER_COL = 16
 BUFS = {"bank0": 3, "bank1": 3, "acc": 1, "turned": 1}
 SLOTS = {
     2: [(2, 0, 1), (3, 0, 1)],
-    3: [(0, 1, 2), (1, 1, 2), (2, 1, 2)],
-    4: [(3, 1, 3), (0, 2, 3)],
-    5: [(1, 2, 4), (2, 2, 3)],
-    6: [(0, 3, 5), (2, 3, 4)],
-    7: [(1, 4, 6), (2, 4, 6)],
+    3: [(1, 1, 2), (2, 1, 2), (3, 1, 2)],
+    4: [(0, 1, 3), (1, 2, 3)],
+    5: [(2, 2, 4), (3, 2, 4)],
+    6: [(0, 3, 5), (1, 3, 5)],
+    7: [(3, 4, 6)],
 }
 
 
@@ -55,20 +55,17 @@ def tile_list_gelu_scat_kernel(tc, xT, wgt, wg_words, wg_scales, wu_words, wu_sc
         wd_sc = keep.tile([P, 2, N], U8, name="wd_sc", align_bytes=64)
         nc.vector.memset(wd_sc[:].rearrange("p a r -> p (a r)").bitcast(I32), 0)
         win = [keep.tile([P, T], F32, name=f"win{n}") for n in range(PACK)]
-        for n in range(2):
-            nc.vector.memset(win[n][:, 0:T - 1], 0.0)
-            nc.vector.memset(win[n][:, T - 1:T], 0.0)
-            nc.gpsimd.memset(win[2 + n][:], 0.0)
+        for n in range(PACK):
+            nc.vector.memset(win[n][:], 0.0)
 
         def load_plane(plane):
             a, i = divmod(plane, PACK)
             nc.sync.dma_start(out=x_sb[a][i][:], in_=x_rows[a, i])
 
         def load_scales(s):
-            m, q = divmod(s, 4)
-            lo = 32 * q + 4 * m
-            nc.sync.dma_start(out=w_sc[lo:lo + 4, :, :].bitcast(I32),
-                              in_=(wg_scales, wu_scales)[m][:, 4 * q:4 * q + 4, :].rearrange("a q r -> q a r").bitcast(I32))
+            row, m = divmod(s, 2)
+            nc.sync.dma_start(out=w_sc[4 * m + row:P:32, :, :].bitcast(I32),
+                              in_=(wg_scales, wu_scales)[m][:, row:16:4, :].rearrange("a q r -> q a r").bitcast(I32))
 
         load_plane(0)
         nc.sync.dma_start(pick[:], offs)
@@ -172,8 +169,18 @@ def tile_list_gelu_scat_kernel(tc, xT, wgt, wg_words, wg_scales, wu_words, wu_sc
             ga, ub = (banks[m, b, t][:].rearrange("p (q u e) -> p u q e", u=2, e=2) for m in range(2))
             act = ring.tile([P, 2, P, 2], F32, name="act")[:]
             nc.scalar.activation(act, ga, GELU)
-            words = ring.tile([P, 2, P, 2], BF16, name=f"hid{b}")
-            nc.vector.tensor_tensor(words[:], ub, act, MULT)
+            if b == 0 and t >= 4:
+                words = keep.tile([P, 2, P, 2], BF16, name=f"hid0_{t}", tag=f"hb_{t - 2}", align_bytes=64)
+            elif b == 1 and t in (2, 3, 4, 7):
+                words = keep.tile([P, 2, P, 2], BF16, name=f"hid1_{t}", tag=f"after_turn{t}", align_bytes=64)
+            else:
+                words = ring.tile([P, 2, P, 2], BF16, name=f"hid{b}")
+            if t >= 4:
+                up = ring.tile([P, 2, P, 2], F32, name="up")
+                nc.scalar.copy(up[:], ub)
+                nc.gpsimd.tensor_tensor(words[:], up[:], act, MULT)
+            else:
+                nc.vector.tensor_tensor(words[:], act, ub, MULT)
             hid[t, b] = words[:].rearrange("p u q e -> p (u q e)").bitcast(F32)
 
         hq, hs = {}, {}
@@ -181,11 +188,11 @@ def tile_list_gelu_scat_kernel(tc, xT, wgt, wg_words, wg_scales, wu_words, wu_sc
         def turn(t, b0, b1, tag="turned", hb_tag=None):
             nb = b1 - b0
             turned = psum.tile([P, nb, 2, TOK], F32, name=tag, bufs=BUFS[tag])
-            for b in range(b1 - 1, b0 - 1, -1):
+            for b in range(b0, b1):
                 for u in range(2):
                     nc.tensor.transpose(turned[:, b - b0, u, :], hid[t, b][:, P * u:P * (u + 1)], ident[:])
             if hb_tag is None:
-                hb = ring.tile([P, nb * TOK * PACK], BF16, name="hb", align_bytes=64)[:]
+                hb = ring.tile([P, nb * TOK * PACK], BF16, name="hb", bufs=1, align_bytes=64)[:]
             else:
                 hb = keep.tile([P, nb * TOK * PACK], BF16, name=f"hb{t}", tag=hb_tag, align_bytes=64)[:]
             nc.scalar.copy(hb.bitcast(F32).rearrange("p (b c u) -> p b c u", b=nb, u=2), turned[:].rearrange("p b u c -> p b c u"))
@@ -196,9 +203,9 @@ def tile_list_gelu_scat_kernel(tc, xT, wgt, wg_words, wg_scales, wu_words, wu_sc
                 hq[t, b] = codes[:, TOK * (b - b0):TOK * (b - b0 + 1)].bitcast(FP8X4)
                 hs[t, b] = scales[:, TOK * (b - b0):TOK * (b - b0 + 1)]
 
-        def multiply(units, tag, y):
+        def multiply(units, tag, y, pieces=None):
             acc = psum.tile([P, len(units) * TOK], F32, name=tag, bufs=BUFS[tag])
-            for k, (n, t) in enumerate(units):
+            for k, (n, t) in reversed(list(enumerate(units))):
                 for b in range(2):
                     nc.tensor.matmul_mx(
                         out=acc[:, TOK * k:TOK * (k + 1)],
@@ -206,22 +213,35 @@ def tile_list_gelu_scat_kernel(tc, xT, wgt, wg_words, wg_scales, wu_words, wu_sc
                         lhsT_scale=wd_sc[:, b, P * n:P * (n + 1)],
                         rhs=hq[t, b], rhs_scale=hs[t, b],
                         start=(b == 0), stop=(b == 1))
-            nc.scalar.copy(y, acc[:])
+            if pieces is None:
+                nc.scalar.copy(y, acc[:])
+            else:
+                k = 0
+                for n, t0, t1 in pieces:
+                    width = TOK * (t1 - t0)
+                    nc.vector.tensor_tensor(y[:, k:k + width], wgo_sb[:, TOK * t0:TOK * t1], acc[:, k:k + width], MULT)
+                    k = k + width
 
-        def scatter(n, t0, t1, y):
+        def scatter(n, t0, t1, y, fused=True):
             c0, c1 = TOK * t0, TOK * t1
             cols = place[:, c0 // PER_COL:c1 // PER_COL]
-            nc.vector.tensor_tensor(win[n][:].indirect(cols), y, wgo_sb[:, c0:c1], MULT)
+            if fused:
+                nc.vector.tensor_tensor(win[n][:].indirect(cols), y, wgo_sb[:, c0:c1], MULT)
+            else:
+                nc.vector.tensor_copy(win[n][:].indirect(cols), y)
             if c1 == J:
                 nc.sync.dma_start(out=out[P * n:P * (n + 1), :], in_=win[n][:])
 
-        def second_product(pieces, tag):
+        def second_product(pieces, tag, y_tag=None, fused=True):
             units = [(n, t) for n, t0, t1 in pieces for t in range(t0, t1)]
-            y = ring.tile([P, len(units) * TOK], F32, name="y", bufs=4)
-            multiply(units, tag, y[:])
+            if y_tag is None:
+                y = ring.tile([P, len(units) * TOK], F32, name="y", bufs=4)
+            else:
+                y = keep.tile([P, len(units) * TOK], F32, name="y_held", tag=y_tag, align_bytes=64)
+            multiply(units, tag, y[:], None if fused else pieces)
             k = 0
             for n, t0, t1 in pieces:
-                scatter(n, t0, t1, y[:, k:k + TOK * (t1 - t0)])
+                scatter(n, t0, t1, y[:, k:k + TOK * (t1 - t0)], fused)
                 k = k + TOK * (t1 - t0)
             return y
 
@@ -238,24 +258,21 @@ def tile_list_gelu_scat_kernel(tc, xT, wgt, wg_words, wg_scales, wu_words, wu_sc
         hidden(1, 1)
         second_product([(0, 0, 1)], "turned")
         hidden(0, 2)
-        turn(1, 0, 2)
+        turn(1, 0, 2, "turned", "hb_1")
         second_product([(1, 0, 1)], "acc")
         tiles = J // TOK
         for t in range(2, tiles):
             hidden(1, t)
-            second_product(SLOTS[t], "acc")
-            if t == 2:
-                quantise_x(1, 5 * TOK, 7 * TOK, "xq13", "hq0_0")
-            if t == 4:
-                quantise_x(1, 7 * TOK, J, "xq14", "hq1_0")
+            if t > 2:
+                turn(t - 1, 0, 2, ("turned", "acc")[t % 2], f"hb_{t - 1}")
+            second_product(SLOTS[t], ("turned", "acc")[t % 2], None, not 3 <= t < 7)
+            if 3 <= t <= 5:
+                quantise_x(1, TOK * (t + 2), TOK * (t + 3), f"xq1_late{t}", f"after_turn{t - 1}")
             if t + 1 < tiles:
                 hidden(0, t + 1)
-            turn(t, 0, 2)
-        second_product([(0, 5, 7), (1, 6, 7)], "turned")
-        second_product([(0, 7, 8)], "acc")
-        second_product([(1, 7, 8)], "bank1")
-        second_product([(2, 6, 8)], "bank0")
-        y_last = keep.tile([P, 5 * TOK], F32, name="y_last")
-        multiply([(3, t) for t in range(3, 7)], "bank1", y_last[:, 0:HALF])
-        multiply([(3, 7)], "bank0", y_last[:, HALF:5 * TOK])
-        scatter(3, 3, 8, y_last[:])
+        turn(tiles - 1, 0, 2)
+        second_product([(0, 5, 7)], "acc", "after_turn7")
+        second_product([(3, 6, 8)], "turned")
+        second_product([(0, 7, 8)], "bank0")
+        second_product([(1, 5, 8)], "bank1")
+        second_product([(2, 4, 8)], "bank0")

@@ -51,12 +51,12 @@ def tile_list_gelu_scat_kernel(tc, xT, wgt, wg_words, wg_scales, wu_words, wu_sc
         ident = keep.tile([P, P], F32, name="ident")
         make_identity(nc, ident[:])
         w_sc = keep.tile([P, 2, R], U8, name="w_sc", align_bytes=64)
-        nc.vector.memset(w_sc[:].rearrange("p a r -> p (a r)").bitcast(I32), 0)
+        nc.gpsimd.memset(w_sc[:].rearrange("p a r -> p (a r)").bitcast(I32), 0)
         wd_sc = keep.tile([P, 2, N], U8, name="wd_sc", align_bytes=64)
-        nc.vector.memset(wd_sc[:].rearrange("p a r -> p (a r)").bitcast(I32), 0)
+        nc.gpsimd.memset(wd_sc[:].rearrange("p a r -> p (a r)").bitcast(I32), 0)
         win = [keep.tile([P, T], F32, name=f"win{n}") for n in range(PACK)]
         for n in range(PACK):
-            nc.vector.memset(win[n][:], 0.0)
+            nc.gpsimd.memset(win[n][:], 0.0)
 
         def load_plane(plane):
             a, i = divmod(plane, PACK)
@@ -101,7 +101,7 @@ def tile_list_gelu_scat_kernel(tc, xT, wgt, wg_words, wg_scales, wu_words, wu_sc
         nc.sync.dma_start(out=wgo_sb[:], in_=wgo)
 
         warm = keep.tile([P, 8], F32, name="warm")
-        nc.scalar.activation(warm[:], win[0][:, 0:8], GELU)
+        nc.scalar.activation(warm[:], ident[:, 0:8], GELU)
 
         g0 = keep.tile([P, PACK, J], F32, name="g0")
         g1 = keep.tile([P, PACK, J], F32, name="g1", align_bytes=64)

@@ -169,13 +169,13 @@ def tile_list_gelu_scat_kernel(tc, xT, wgt, wg_words, wg_scales, wu_words, wu_sc
             ga, ub = (banks[m, b, t][:].rearrange("p (q u e) -> p u q e", u=2, e=2) for m in range(2))
             act = ring.tile([P, 2, P, 2], F32, name="act")[:]
             nc.scalar.activation(act, ga, GELU)
-            if b == 0 and t >= 4:
+            if b == 0 and 4 <= t < 7:
                 words = keep.tile([P, 2, P, 2], BF16, name=f"hid0_{t}", tag=f"hb_{t - 2}", align_bytes=64)
             elif b == 1 and t in (2, 3, 4, 7):
                 words = keep.tile([P, 2, P, 2], BF16, name=f"hid1_{t}", tag=f"after_turn{t}", align_bytes=64)
             else:
                 words = ring.tile([P, 2, P, 2], BF16, name=f"hid{b}")
-            if t >= 4:
+            if 4 <= t < 7:
                 up = ring.tile([P, 2, P, 2], F32, name="up")
                 nc.scalar.copy(up[:], ub)
                 nc.gpsimd.tensor_tensor(words[:], up[:], act, MULT)
@@ -265,7 +265,7 @@ def tile_list_gelu_scat_kernel(tc, xT, wgt, wg_words, wg_scales, wu_words, wu_sc
             hidden(1, t)
             if t > 2:
                 turn(t - 1, 0, 2, ("turned", "acc")[t % 2], f"hb_{t - 1}")
-            second_product(SLOTS[t], ("turned", "acc")[t % 2], None, not 3 <= t < 7)
+            second_product(SLOTS[t], ("turned", "acc")[t % 2], None, not 3 <= t < 6)
             if 3 <= t <= 5:
                 quantise_x(1, TOK * (t + 2), TOK * (t + 3), f"xq1_late{t}", f"after_turn{t - 1}")
             if t + 1 < tiles:

@@ -25,7 +25,7 @@ TOK = 128
 PER_COL = 16
 BUFS = {"bank0": 3, "bank1": 3, "acc": 1, "turned": 1}
 SLOTS = {
-    2: [(2, 0, 1), (3, 0, 1)],
+    2: [(1, 0, 1), (2, 0, 1), (3, 0, 1)],
     3: [(1, 1, 2), (2, 1, 2), (3, 1, 2)],
     4: [(0, 1, 3), (1, 2, 3)],
     5: [(2, 2, 4), (3, 2, 4)],
@@ -130,13 +130,11 @@ def tile_list_gelu_scat_kernel(tc, xT, wgt, wg_words, wg_scales, wu_words, wu_sc
                 xs[a, c0 // TOK + t] = scales[:, TOK * t:TOK * (t + 1)]
             return codes
 
-        for i in range(3):
+        for i in range(PACK):
             gather(0, i, 0, J)
-        gather(0, 3, 0, HALF)
-        gather(0, 3, HALF, J)
         gather(1, 0, 0, J)
-        quantise_x(0, 0, HALF, "x10", "xb00")
         gather(1, 1, 0, J)
+        quantise_x(0, 0, HALF, "x11", "xb00")
         gather(1, 2, 0, J)
         gather(1, 3, 0, TOK)
         quantise_x(1, 0, TOK, "xq10", "xb10")
@@ -150,7 +148,7 @@ def tile_list_gelu_scat_kernel(tc, xT, wgt, wg_words, wg_scales, wu_words, wu_sc
 
         def first_pass(m, b, t, a):
             if a == 0:
-                tag = f"bank{(m + (2 * t + b) // 3) % 2}"
+                tag = ("acc", "turned")[m] if (b, t) == (1, 1) else f"bank{(m + (2 * t + b) // 3) % 2}"
                 banks[m, b, t] = psum.tile([P, HALF], F32, name=tag, bufs=BUFS[tag])
             nc.tensor.matmul_mx(
                 out=banks[m, b, t][:],
@@ -162,20 +160,20 @@ def tile_list_gelu_scat_kernel(tc, xT, wgt, wg_words, wg_scales, wu_words, wu_sc
         hid = {}
 
         def hidden(b, t):
-            for m in ((0, 1) if 2 * t + b < 3 else (1, 0)):
+            for m in ((0, 1) if t < 2 else (1, 0)):
                 for a in range(2):
                     if a == 1 or (m, b, t) not in banks:
                         first_pass(m, b, t, a)
             ga, ub = (banks[m, b, t][:].rearrange("p (q u e) -> p u q e", u=2, e=2) for m in range(2))
             act = ring.tile([P, 2, P, 2], F32, name="act")[:]
             nc.scalar.activation(act, ga, GELU)
-            if b == 0 and 4 <= t < 7:
+            if b == 0 and 3 <= t < 7:
                 words = keep.tile([P, 2, P, 2], BF16, name=f"hid0_{t}", tag=f"hb_{t - 2}", align_bytes=64)
             elif b == 1 and t in (2, 3, 4, 7):
                 words = keep.tile([P, 2, P, 2], BF16, name=f"hid1_{t}", tag=f"after_turn{t}", align_bytes=64)
             else:
                 words = ring.tile([P, 2, P, 2], BF16, name=f"hid{b}")
-            if 4 <= t < 7:
+            if 3 <= t < 7:
                 up = ring.tile([P, 2, P, 2], F32, name="up")
                 nc.scalar.copy(up[:], ub)
                 nc.gpsimd.tensor_tensor(words[:], up[:], act, MULT)
@@ -246,11 +244,11 @@ def tile_list_gelu_scat_kernel(tc, xT, wgt, wg_words, wg_scales, wu_words, wu_sc
             return y
 
         for m in range(2):
-            for b, t in ((0, 0), (1, 0), (0, 1)):
+            for b, t in ((0, 0), (1, 0), (0, 1), (1, 1)):
                 first_pass(m, b, t, 0)
         hidden(0, 0)
         hidden(1, 0)
-        turn(0, 0, 1, "turned", "late0")
+        turn(0, 0, 1, "bank0", "late0")
         turn(0, 1, 2, "bank1", "late1")
         quantise_x(1, 3 * TOK, 5 * TOK, "xq12", "late0", nc.vector.tensor_copy)
         quantise_x(0, HALF, J, "late1", "xb01")
@@ -259,13 +257,12 @@ def tile_list_gelu_scat_kernel(tc, xT, wgt, wg_words, wg_scales, wu_words, wu_sc
         second_product([(0, 0, 1)], "turned")
         hidden(0, 2)
         turn(1, 0, 2, "turned", "hb_1")
-        second_product([(1, 0, 1)], "acc")
         tiles = J // TOK
         for t in range(2, tiles):
             hidden(1, t)
             if t > 2:
                 turn(t - 1, 0, 2, ("turned", "acc")[t % 2], f"hb_{t - 1}")
-            second_product(SLOTS[t], ("turned", "acc")[t % 2], None, not 3 <= t < 6)
+            second_product(SLOTS[t], ("turned", "acc")[t % 2], None, not 2 <= t < 6)
             if 3 <= t <= 5:
                 quantise_x(1, TOK * (t + 2), TOK * (t + 3), f"xq1_late{t}", f"after_turn{t - 1}")
             if t + 1 < tiles:

@@ -1,7 +1,6 @@
 from contextlib import ExitStack
 
 import concourse.mybir as mybir
-from concourse.masks import make_identity
 
 K, R, N, T, J = 1024, 1024, 512, 2048, 1024
 FLOPS = 2 * J * (2 * K * R + R * N)
@@ -20,25 +19,31 @@ GELU = mybir.ActivationFunctionType.Gelu_apprx_tanh
 P = 128
 PACK = 4
 HALF = 512
-CHUNK = 256
 TOK = 128
+TILES = J // TOK
 PER_COL = 16
-BUFS = {"bank0": 3, "bank1": 3, "acc": 1, "turned": 1}
-SLOTS = {
-    2: [(1, 0, 1), (2, 0, 1), (3, 0, 1)],
-    3: [(1, 1, 2), (2, 1, 2), (3, 1, 2)],
-    4: [(0, 1, 3), (1, 2, 3)],
-    5: [(2, 2, 4), (3, 2, 4)],
-    6: [(0, 3, 5), (1, 3, 5)],
-    7: [(3, 4, 6)],
+OLD = {
+    1: [(3, 0, 1)],
+    2: [(2, 1, 2), (3, 1, 2)],
+    3: [(0, 2, 3), (1, 2, 3), (2, 2, 3)],
+    4: [(0, 3, 4), (3, 2, 4)],
+    5: [(1, 3, 4), (2, 3, 5)],
+    6: [(3, 4, 5), (0, 4, 6)],
+    7: [(1, 4, 5)],
 }
+NEW = {
+    0: [(0, 0, 1), (1, 0, 1), (2, 0, 1)],
+    1: [(0, 1, 2), (1, 1, 2)],
+}
+LEAD = 3
+UP_TAGS = ("x00", "x01", "x02", "x03", "x10", "x12", "x13", "up7")
+LAST = [(0, 6, 8), (1, 5, 8), (2, 5, 8), (3, 5, 8)]
 
 
 def tile_list_gelu_scat_kernel(tc, xT, wgt, wg_words, wg_scales, wu_words, wu_scales, wd_words, wd_scales, wgo, offs, offs2, out):
     nc = tc.nc
     with ExitStack() as ctx:
         keep = ctx.enter_context(tc.tile_pool(name="keep", bufs=1))
-        ring = ctx.enter_context(tc.tile_pool(name="ring", bufs=3))
         psum = ctx.enter_context(tc.psum_pool(name="psum", bufs=1))
 
         pick = keep.tile([P, J // PER_COL], U16, name="pick")
@@ -48,10 +53,8 @@ def tile_list_gelu_scat_kernel(tc, xT, wgt, wg_words, wg_scales, wu_words, wu_sc
         x_sb = [[keep.tile([P, T], F32, name=f"x{a}{i}", align_bytes=64) for i in range(PACK)] for a in range(2)]
         x_rows = xT.rearrange("(a p i) t -> a i p t", a=2, i=PACK)
 
-        ident = keep.tile([P, P], F32, name="ident")
-        make_identity(nc, ident[:])
-        w_sc = keep.tile([P, 2, R], U8, name="w_sc", align_bytes=64)
-        nc.gpsimd.memset(w_sc[:].rearrange("p a r -> p (a r)").bitcast(I32), 0)
+        sc_raw = keep.tile([P, R], U8, name="sc_raw", align_bytes=64)
+        nc.gpsimd.memset(sc_raw[:].bitcast(I32), 0)
         wd_sc = keep.tile([P, 2, N], U8, name="wd_sc", align_bytes=64)
         nc.gpsimd.memset(wd_sc[:].rearrange("p a r -> p (a r)").bitcast(I32), 0)
         win = [keep.tile([P, T], F32, name=f"win{n}") for n in range(PACK)]
@@ -62,148 +65,165 @@ def tile_list_gelu_scat_kernel(tc, xT, wgt, wg_words, wg_scales, wu_words, wu_sc
             a, i = divmod(plane, PACK)
             nc.sync.dma_start(out=x_sb[a][i][:], in_=x_rows[a, i])
 
-        def load_scales(s):
-            row, m = divmod(s, 2)
-            nc.sync.dma_start(out=w_sc[4 * m + row:P:32, :, :].bitcast(I32),
-                              in_=(wg_scales, wu_scales)[m][:, row:16:4, :].rearrange("a q r -> q a r").bitcast(I32))
+        def load_scales(m):
+            for q in range(4):
+                row = 32 * q + 8 * m
+                nc.sync.dma_start(out=sc_raw[row:row + 8, :].bitcast(I32),
+                                  in_=(wg_scales, wu_scales)[m][:, 4 * q:4 * q + 4, :].bitcast(I32))
+
+        w_raw, w_sb = {}, {}
+
+        def load_weights(m, a, b0, b1):
+            piece = keep.tile([P, (b1 - b0) * HALF], I32, name=f"w_raw{m}{a}{b0}", align_bytes=64)
+            src = (wg_words, wu_words)[m][a].rearrange("p r i -> p (r i)")[:, 2048 * b0:2048 * b1]
+            nc.sync.dma_start(out=piece[:], in_=src.bitcast(I32))
+            w_raw[m, a, b0] = piece
 
         load_plane(0)
         nc.sync.dma_start(pick[:], offs)
         nc.sync.dma_start(out=wgt_sb[:], in_=wgt)
         for plane in range(1, 6):
             load_plane(plane)
-        w_sb = {}
-
-        def load_weights(m, a, b0, b1):
-            piece = keep.tile([P, (b1 - b0) * HALF], I32, name=f"w_sb{m}{a}{b0}", align_bytes=64)
-            src = (wg_words, wu_words)[m][a].rearrange("p r i -> p (r i)")[:, 2048 * b0:2048 * b1]
-            nc.sync.dma_start(out=piece[:], in_=src.bitcast(I32))
-            for b in range(b0, b1):
-                w_sb[m, b, a] = piece[:, HALF * (b - b0):HALF * (b - b0 + 1)].bitcast(FP8X4)
-
-        for s in range(4):
-            load_scales(s)
-        load_plane(6)
-        for s in range(4, 8):
-            load_scales(s)
+        load_scales(0)
         load_weights(0, 0, 0, 2)
-        load_plane(7)
+        load_scales(1)
+        load_plane(6)
         load_weights(1, 0, 0, 2)
-        load_weights(0, 1, 0, 2)
-        load_weights(1, 1, 0, 1)
-        load_weights(1, 1, 1, 2)
+        load_plane(7)
+        for b in range(2):
+            for m in range(2):
+                load_weights(m, 1, b, b + 1)
         wd_sb = keep.tile([P, 2, 2 * N], U8, name="wd_sb", align_bytes=64)
         nc.sync.dma_start(out=wd_sb[:].bitcast(I32), in_=wd_words.rearrange("a p c -> p a c").bitcast(I32))
         for q in range(4):
             nc.sync.dma_start(out=wd_sc[32 * q:32 * q + 4, :, :].bitcast(I32),
                               in_=wd_scales[:, 4 * q:4 * q + 4, :].rearrange("a q n -> q a n").bitcast(I32))
-        nc.sync.dma_start(place[:], offs2)
         nc.sync.dma_start(out=wgo_sb[:], in_=wgo)
+        nc.sync.dma_start(place[:], offs2)
 
         warm = keep.tile([P, 8], F32, name="warm")
-        nc.scalar.activation(warm[:], ident[:, 0:8], GELU)
+        nc.scalar.activation(warm[:], wgt_sb[:, 0:8], GELU)
 
         g0 = keep.tile([P, PACK, J], F32, name="g0")
         g1 = keep.tile([P, PACK, J], F32, name="g1", align_bytes=64)
 
-        def staged(a, c0, c1):
-            return (g0, g1)[a][:, :, c0:c1]
-
         def gather(a, i, c0, c1):
             cols = pick[:, c0 // PER_COL:c1 // PER_COL]
-            nc.vector.tensor_tensor(staged(a, c0, c1)[:, i, :], x_sb[a][i][:].indirect(cols), wgt_sb[:, c0:c1], MULT)
+            nc.vector.tensor_tensor((g0, g1)[a][:, i, c0:c1], x_sb[a][i][:].indirect(cols), wgt_sb[:, c0:c1], MULT)
 
-        xq, xs = {}, {}
-
-        def quantise_x(a, c0, c1, codes_tag, xb_tag, weave=nc.scalar.copy):
-            width = c1 - c0
-            if xb_tag is None:
-                xb = g1[:, 3, J - 2 * width:J].bitcast(BF16).rearrange("p (c i) -> p c i", i=PACK)
+        def deal_weights(m, a, b0, b1, on_vector):
+            dealt = keep.tile([P, (b1 - b0) * HALF], I32, name=f"w_sb{m}{a}{b0}", align_bytes=64)
+            dst = dealt[:].rearrange("p (b i q) -> p b q i", i=PACK, q=P)
+            src = w_raw[m, a, b0][:].rearrange("p (b q i) -> p b q i", i=PACK, q=P)
+            if on_vector:
+                nc.vector.tensor_copy(dst, src)
             else:
-                xb = keep.tile([P, width, PACK], BF16, name=f"xb{a}_{c0}", tag=xb_tag, align_bytes=64)[:]
-            weave(xb.rearrange("p (c e) i -> p c i e", e=4), staged(a, c0, c1).rearrange("p i (c e) -> p c i e", e=4))
-            codes = keep.tile([P, width], U32, name=f"xq{a}_{c0}", tag=codes_tag, align_bytes=64)
-            scales = keep.tile([P, width], U8, name=f"xs{a}_{c0}", align_bytes=64)
-            nc.vector.quantize_mx(out=codes[:].bitcast(FP8X4), scales=scales[:], in_=xb.rearrange("p c i -> p (c i)"))
+                nc.scalar.copy(dst.bitcast(U32), src.bitcast(U32))
+            for b in range(b0, b1):
+                for i in range(PACK):
+                    c = HALF * (b - b0) + P * i
+                    w_sb[m, a, b, i] = dealt[:, c:c + P].bitcast(FP8X4)
+
+        xb, xq, xs = {}, {}, {}
+
+        def weave(a, c0, c1, tag, copy, step=HALF):
+            xb[a, c0] = keep.tile([P, c1 - c0, PACK], BF16, name=f"xb{a}_{c0}", tag=tag, align_bytes=64)[:]
+            for c in range(c0, c1, step):
+                end = min(c1, c + step)
+                copy(xb[a, c0][:, c - c0:end - c0, :].rearrange("p (c e) i -> p c i e", e=4),
+                     (g0, g1)[a][:, :, c:end].rearrange("p i (c e) -> p c i e", e=4))
+
+        def quantise_x(a, c0, c1, tag):
+            width = c1 - c0
+            codes = keep.tile([P, width], U32, name=f"xq{a}_{c0}", tag=tag, align_bytes=64)[:]
+            scales = keep.tile([P, width], U8, name=f"xs{a}_{c0 // TOK}", align_bytes=64)
+            nc.vector.quantize_mx(out=codes.bitcast(FP8X4), scales=scales[:], in_=xb[a, c0].rearrange("p c i -> p (c i)"))
             for t in range(width // TOK):
                 xq[a, c0 // TOK + t] = codes[:, TOK * t:TOK * (t + 1)].bitcast(FP8X4)
                 xs[a, c0 // TOK + t] = scales[:, TOK * t:TOK * (t + 1)]
-            return codes
 
         for i in range(PACK):
             gather(0, i, 0, J)
+        weave(0, 0, HALF, "xb00", nc.scalar.copy)
+        weave(0, HALF, J, "xb01", nc.scalar.copy)
         gather(1, 0, 0, J)
         gather(1, 1, 0, J)
-        quantise_x(0, 0, HALF, "x11", "xb00")
+        w_sc = keep.tile([P, R], U8, name="w_sc", align_bytes=64)
+        nc.vector.tensor_copy(w_sc[:].rearrange("p (b i q) -> p b q i", i=PACK, q=P),
+                              sc_raw[:].rearrange("p (b q i) -> p b q i", i=PACK, q=P))
+        quantise_x(0, 0, HALF, "x11")
+        quantise_x(0, HALF, J, "xq01")
+        deal_weights(0, 0, 0, 2, False)
         gather(1, 2, 0, J)
-        gather(1, 3, 0, TOK)
-        quantise_x(1, 0, TOK, "xq10", "xb10")
-        gather(1, 3, TOK, 3 * TOK)
-        gather(1, 3, 3 * TOK, 5 * TOK)
-        quantise_x(1, TOK, 2 * TOK, "xq11", None)
-        gather(1, 3, 5 * TOK, J)
-        quantise_x(1, 2 * TOK, 3 * TOK, "xq15", "xb15")
+        deal_weights(1, 0, 0, 2, False)
 
         banks = {}
+        ring = []
 
         def first_pass(m, b, t, a):
             if a == 0:
-                tag = ("acc", "turned")[m] if (b, t) == (1, 1) else f"bank{(m + (2 * t + b) // 3) % 2}"
-                banks[m, b, t] = psum.tile([P, HALF], F32, name=tag, bufs=BUFS[tag])
-            nc.tensor.matmul_mx(
-                out=banks[m, b, t][:],
-                lhsT=xq[a, t], lhsT_scale=xs[a, t],
-                rhs=w_sb[m, b, a],
-                rhs_scale=w_sc[4 * m:, a, HALF * b:HALF * (b + 1)],
-                start=(a == 0), stop=(a == 1))
+                if (b, t) == (1, 1):
+                    tag = f"acc{m}"
+                else:
+                    tag = f"bank{len(ring) % 6}"
+                    ring.append(tag)
+                banks[m, b, t] = psum.tile([P, PACK, TOK], F32, name=tag)
+            row = 8 * m + 4 * a
+            for i in range(PACK):
+                c = HALF * b + P * i
+                nc.tensor.matmul_mx(
+                    out=banks[m, b, t][:, i, :],
+                    lhsT=w_sb[m, a, b, i], lhsT_scale=w_sc[row:, c:c + P],
+                    rhs=xq[a, t], rhs_scale=xs[a, t],
+                    start=(a == 0 and i == 0), stop=(a == 1 and i == PACK - 1))
 
-        hid = {}
+        def first_layer(m, b, t):
+            if (m, b, t) not in banks:
+                first_pass(m, b, t, 0)
+            first_pass(m, b, t, 1)
+            return banks[m, b, t][:].rearrange("p i c -> p c i")
 
-        def hidden(b, t):
-            for m in ((0, 1) if t < 2 else (1, 0)):
-                for a in range(2):
-                    if a == 1 or (m, b, t) not in banks:
-                        first_pass(m, b, t, a)
-            ga, ub = (banks[m, b, t][:].rearrange("p (q u e) -> p u q e", u=2, e=2) for m in range(2))
-            act = ring.tile([P, 2, P, 2], F32, name="act")[:]
-            nc.scalar.activation(act, ga, GELU)
-            if b == 0 and 3 <= t < 7:
-                words = keep.tile([P, 2, P, 2], BF16, name=f"hid0_{t}", tag=f"hb_{t - 2}", align_bytes=64)
-            elif b == 1 and t in (2, 3, 4, 7):
-                words = keep.tile([P, 2, P, 2], BF16, name=f"hid1_{t}", tag=f"after_turn{t}", align_bytes=64)
-            else:
-                words = ring.tile([P, 2, P, 2], BF16, name=f"hid{b}")
-            if 3 <= t < 7:
-                up = ring.tile([P, 2, P, 2], F32, name="up")
-                nc.scalar.copy(up[:], ub)
-                nc.gpsimd.tensor_tensor(words[:], up[:], act, MULT)
-            else:
-                nc.vector.tensor_tensor(words[:], act, ub, MULT)
-            hid[t, b] = words[:].rearrange("p u q e -> p (u q e)").bitcast(F32)
+        for t, b in ((0, 0), (0, 1), (1, 0), (1, 1)):
+            for m in range(2):
+                first_pass(m, b, t, 0)
+
+        gather(1, 3, 0, TOK)
+        weave(1, 0, TOK, "xb10", nc.scalar.copy)
+        gather(1, 3, TOK, HALF)
+        deal_weights(0, 1, 0, 1, False)
+        deal_weights(1, 1, 0, 1, True)
+        quantise_x(1, 0, TOK, "xq10")
+        deal_weights(0, 1, 1, 2, True)
+        weave(1, TOK, 2 * TOK, "xb10", nc.vector.tensor_copy)
+        deal_weights(1, 1, 1, 2, True)
+        quantise_x(1, TOK, 2 * TOK, "xq11")
+        weave(1, 2 * TOK, 3 * TOK, "xb12", nc.scalar.copy)
+        quantise_x(1, 2 * TOK, 3 * TOK, "xq12")
+        weave(1, 3 * TOK, 4 * TOK, "xb10", nc.vector.tensor_copy)
+
+        acts, ups = {}, {}
+
+        def new_set(t):
+            acts[t] = keep.tile([P, R], F32, name=f"act{t}", tag=f"act{t % 5}", align_bytes=64)
+            ups[t] = keep.tile([P, R], F32, name=f"up{t}", tag=UP_TAGS[t], align_bytes=64)
+
+        def by_word(ap):
+            return ap.rearrange("p (c i) -> p c i", i=PACK)
 
         hq, hs = {}, {}
 
-        def turn(t, b0, b1, tag="turned", hb_tag=None):
-            nb = b1 - b0
-            turned = psum.tile([P, nb, 2, TOK], F32, name=tag, bufs=BUFS[tag])
-            for b in range(b0, b1):
-                for u in range(2):
-                    nc.tensor.transpose(turned[:, b - b0, u, :], hid[t, b][:, P * u:P * (u + 1)], ident[:])
-            if hb_tag is None:
-                hb = ring.tile([P, nb * TOK * PACK], BF16, name="hb", bufs=1, align_bytes=64)[:]
-            else:
-                hb = keep.tile([P, nb * TOK * PACK], BF16, name=f"hb{t}", tag=hb_tag, align_bytes=64)[:]
-            nc.scalar.copy(hb.bitcast(F32).rearrange("p (b c u) -> p b c u", b=nb, u=2), turned[:].rearrange("p b u c -> p b c u"))
-            codes = keep.tile([P, nb * TOK], U32, name=f"hq{t}_{b0}", align_bytes=64)
-            scales = keep.tile([P, nb * TOK], U8, name=f"hs{t}_{b0}", align_bytes=64)
-            nc.vector.quantize_mx(out=codes[:].bitcast(FP8X4), scales=scales[:], in_=hb)
-            for b in range(b0, b1):
-                hq[t, b] = codes[:, TOK * (b - b0):TOK * (b - b0 + 1)].bitcast(FP8X4)
-                hs[t, b] = scales[:, TOK * (b - b0):TOK * (b - b0 + 1)]
+        def quantise_h(t, hb, tag):
+            codes = keep.tile([P, 2 * TOK], U32, name=f"hq{t}", tag=tag, align_bytes=64)
+            scales = keep.tile([P, 2 * TOK], U8, name=f"hs{t}", align_bytes=64)
+            nc.vector.quantize_mx(out=codes[:].bitcast(FP8X4), scales=scales[:], in_=hb[:])
+            for b in range(2):
+                hq[t, b] = codes[:, TOK * b:TOK * (b + 1)].bitcast(FP8X4)
+                hs[t, b] = scales[:, TOK * b:TOK * (b + 1)]
 
-        def multiply(units, tag, y, pieces=None):
-            acc = psum.tile([P, len(units) * TOK], F32, name=tag, bufs=BUFS[tag])
-            for k, (n, t) in reversed(list(enumerate(units))):
+        def second_layer(pieces, tag):
+            units = [(n, t) for n, t0, t1 in pieces for t in range(t0, t1)]
+            acc = psum.tile([P, len(units) * TOK], F32, name=tag)
+            for k, (n, t) in enumerate(units):
                 for b in range(2):
                     nc.tensor.matmul_mx(
                         out=acc[:, TOK * k:TOK * (k + 1)],
@@ -211,65 +231,89 @@ def tile_list_gelu_scat_kernel(tc, xT, wgt, wg_words, wg_scales, wu_words, wu_sc
                         lhsT_scale=wd_sc[:, b, P * n:P * (n + 1)],
                         rhs=hq[t, b], rhs_scale=hs[t, b],
                         start=(b == 0), stop=(b == 1))
-            if pieces is None:
-                nc.scalar.copy(y, acc[:])
-            else:
-                k = 0
-                for n, t0, t1 in pieces:
-                    width = TOK * (t1 - t0)
-                    nc.vector.tensor_tensor(y[:, k:k + width], wgo_sb[:, TOK * t0:TOK * t1], acc[:, k:k + width], MULT)
-                    k = k + width
+            return acc
 
-        def scatter(n, t0, t1, y, fused=True):
-            c0, c1 = TOK * t0, TOK * t1
-            cols = place[:, c0 // PER_COL:c1 // PER_COL]
-            if fused:
-                nc.vector.tensor_tensor(win[n][:].indirect(cols), y, wgo_sb[:, c0:c1], MULT)
-            else:
-                nc.vector.tensor_copy(win[n][:].indirect(cols), y)
-            if c1 == J:
-                nc.sync.dma_start(out=out[P * n:P * (n + 1), :], in_=win[n][:])
+        accs = []
 
-        def second_product(pieces, tag, y_tag=None, fused=True):
-            units = [(n, t) for n, t0, t1 in pieces for t in range(t0, t1)]
-            if y_tag is None:
-                y = ring.tile([P, len(units) * TOK], F32, name="y", bufs=4)
-            else:
-                y = keep.tile([P, len(units) * TOK], F32, name="y_held", tag=y_tag, align_bytes=64)
-            multiply(units, tag, y[:], None if fused else pieces)
+        def weigh(pieces, ys):
+            accs.append(second_layer(pieces, f"acc{len(accs) % 2}"))
+            acc = accs[-1]
             k = 0
-            for n, t0, t1 in pieces:
-                scatter(n, t0, t1, y[:, k:k + TOK * (t1 - t0)], fused)
-                k = k + TOK * (t1 - t0)
-            return y
+            rest = pieces[1:]
+            spans = [(t0, t1) for n, t0, t1 in rest]
+            groups = [pieces[0][1:] + (1,)] + [span + (spans.count(span),) for span in sorted(set(spans), key=spans.index)]
+            for (t0, t1, count), y in zip(groups, ys):
+                width = TOK * (t1 - t0)
+                cols = slice(k, k + count * width)
+                nc.vector.tensor_tensor(
+                    y[:, 0:count * width].rearrange("p (n c) -> p n c", n=count),
+                    wgo_sb[:, TOK * t0:TOK * t1].unsqueeze(1).to_broadcast([P, count, width]),
+                    acc[:, cols].rearrange("p (n c) -> p n c", n=count), MULT)
+                k = k + count * width
 
+        def scatter_weighed(pieces, ys):
+            k = 0
+            for at, (n, t0, t1) in enumerate(pieces):
+                cols = place[:, TOK * t0 // PER_COL:TOK * t1 // PER_COL]
+                nc.vector.tensor_copy(win[n][:].indirect(cols), ys[min(at, 1)][:, k:k + TOK * (t1 - t0)])
+                k = (k + TOK * (t1 - t0)) * min(at, 1)
+
+        def hidden(t, b):
+            if b == 0:
+                new_set(t)
+            nc.scalar.activation(by_word(acts[t][:, HALF * b:HALF * (b + 1)]), first_layer(0, b, t), GELU)
+            nc.scalar.copy(by_word(ups[t][:, HALF * b:HALF * (b + 1)]), first_layer(1, b, t))
+
+        act_first = keep.tile([P, HALF], F32, name="act_first", align_bytes=64)
+        hb = keep.tile([P, R], BF16, name="hb", align_bytes=64)
+        for b in range(2):
+            act = (act_first[:], g1[:, 3, HALF:J])[b]
+            nc.scalar.activation(by_word(act), first_layer(0, b, 0), GELU)
+            nc.vector.tensor_tensor(by_word(hb[:, HALF * b:HALF * (b + 1)]), by_word(act), first_layer(1, b, 0), MULT)
+        new_set(1)
         for m in range(2):
-            for b, t in ((0, 0), (1, 0), (0, 1), (1, 1)):
-                first_pass(m, b, t, 0)
-        hidden(0, 0)
-        hidden(1, 0)
-        turn(0, 0, 1, "bank0", "late0")
-        turn(0, 1, 2, "bank1", "late1")
-        quantise_x(1, 3 * TOK, 5 * TOK, "xq12", "late0", nc.vector.tensor_copy)
-        quantise_x(0, HALF, J, "late1", "xb01")
-        hidden(0, 1)
-        hidden(1, 1)
-        second_product([(0, 0, 1)], "turned")
-        hidden(0, 2)
-        turn(1, 0, 2, "turned", "hb_1")
-        tiles = J // TOK
-        for t in range(2, tiles):
-            hidden(1, t)
-            if t > 2:
-                turn(t - 1, 0, 2, ("turned", "acc")[t % 2], f"hb_{t - 1}")
-            second_product(SLOTS[t], ("turned", "acc")[t % 2], None, not 2 <= t < 6)
-            if 3 <= t <= 5:
-                quantise_x(1, TOK * (t + 2), TOK * (t + 3), f"xq1_late{t}", f"after_turn{t - 1}")
-            if t + 1 < tiles:
-                hidden(0, t + 1)
-        turn(tiles - 1, 0, 2)
-        second_product([(0, 5, 7)], "acc", "after_turn7")
-        second_product([(3, 6, 8)], "turned")
-        second_product([(0, 7, 8)], "bank0")
-        second_product([(1, 5, 8)], "bank1")
-        second_product([(2, 4, 8)], "bank0")
+            for b in range(2):
+                first_pass(m, b, 1, 1)
+        for b in range(2):
+            nc.scalar.activation(by_word(acts[1][:, HALF * b:HALF * (b + 1)]), banks[0, b, 1][:].rearrange("p i c -> p c i"), GELU)
+        for b in range(2):
+            nc.scalar.copy(by_word(ups[1][:, HALF * b:HALF * (b + 1)]), banks[1, b, 1][:].rearrange("p i c -> p c i"))
+        quantise_x(1, 3 * TOK, 4 * TOK, "act_first")
+        quantise_h(0, hb, "hq0")
+        gather(1, 3, HALF, J)
+        y_new = [keep.tile([P, HALF], F32, name=tag, align_bytes=64)[:] for tag in ("fresh0", "x00")]
+        holds = ["fresh0", "x00"]
+        weigh(NEW[0], y_new)
+        scatter_weighed(NEW[0], y_new)
+        hidden(2, 0)
+
+        for t in range(1, TILES):
+            late = t + LEAD
+            if late < TILES:
+                weave(1, TOK * late, TOK * (late + 1), f"xs1_{t}", nc.scalar.copy)
+            if t + 1 < TILES:
+                hidden(t + 1, 1)
+            hb = keep.tile([P, R], BF16, name="hb", align_bytes=64)
+            nc.gpsimd.tensor_tensor(hb[:], ups[t][:], acts[t][:], MULT)
+            if late < TILES:
+                quantise_x(1, TOK * late, TOK * (late + 1), holds.pop(0))
+            quantise_h(t, hb, holds[0])
+            y_old = (keep.tile([P, TOK], F32, name=f"first{t}", tag=f"act{t % 5}", align_bytes=64)[:], ups[t][:])
+            holds = [f"act{t % 5}", UP_TAGS[t]]
+            weigh(OLD[t], y_old)
+            scatter_weighed(OLD[t], y_old)
+            if t + 2 < TILES:
+                hidden(t + 2, 0)
+            if t in NEW:
+                holds = ["fresh1", "fresh2"]
+                y_new = [keep.tile([P, TOK], F32, name=tag, align_bytes=64)[:] for tag in holds]
+                weigh(NEW[t], y_new)
+                scatter_weighed(NEW[t], y_new)
+
+        for n, t0, t1 in LAST:
+            acc = second_layer([(n, t0, t1)], f"bank{(n + 4) % 6}")
+            y = g0[:, n, 0:TOK * (t1 - t0)]
+            nc.scalar.copy(y, acc[:])
+            cols = place[:, TOK * t0 // PER_COL:TOK * t1 // PER_COL]
+            nc.vector.tensor_tensor(win[n][:].indirect(cols), y, wgo_sb[:, TOK * t0:TOK * t1], MULT)
+            nc.sync.dma_start(out=out[P * n:P * (n + 1), :], in_=win[n][:])

@@ -22,22 +22,10 @@ HALF = 512
 TOK = 128
 TILES = J // TOK
 PER_COL = 16
-OLD = {
-    1: [(3, 0, 1)],
-    2: [(2, 1, 2), (3, 1, 2)],
-    3: [(0, 2, 3), (1, 2, 3), (2, 2, 3)],
-    4: [(0, 3, 4), (3, 2, 4)],
-    5: [(1, 3, 4), (2, 3, 5)],
-    6: [(3, 4, 5), (0, 4, 6)],
-    7: [(1, 4, 5)],
-}
-NEW = {
-    0: [(0, 0, 1), (1, 0, 1), (2, 0, 1)],
-    1: [(0, 1, 2), (1, 1, 2)],
-}
-LEAD = 3
-UP_TAGS = ("x00", "x01", "x02", "x03", "x10", "x12", "x13", "up7")
-LAST = [(0, 6, 8), (1, 5, 8), (2, 5, 8), (3, 5, 8)]
+EARLY = 5 * TOK
+ACT_TAGS = {2: "act0", 3: "act1", 4: "act2", 5: "x13", 6: "act1", 7: "act2"}
+UP_TAGS = {2: "x00", 3: "x01", 4: "x02", 5: "x03", 6: "x10", 7: "x12"}
+LAST = [(0, 7, 8), (1, 5, 8), (2, 5, 8), (3, 5, 8)]
 
 
 def tile_list_gelu_scat_kernel(tc, xT, wgt, wg_words, wg_scales, wu_words, wu_scales, wd_words, wd_scales, wgo, offs, offs2, out):
@@ -105,7 +93,8 @@ def tile_list_gelu_scat_kernel(tc, xT, wgt, wg_words, wg_scales, wu_words, wu_sc
         nc.scalar.activation(warm[:], wgt_sb[:, 0:8], GELU)
 
         g0 = keep.tile([P, PACK, J], F32, name="g0")
-        g1 = keep.tile([P, PACK, J], F32, name="g1", align_bytes=64)
+        g1_flat = keep.tile([P, PACK * J + TOK], F32, name="g1", align_bytes=64)
+        g1 = g1_flat[:, 0:PACK * J].rearrange("p (i j) -> p i j", i=PACK)
 
         def gather(a, i, c0, c1):
             cols = pick[:, c0 // PER_COL:c1 // PER_COL]
@@ -126,33 +115,31 @@ def tile_list_gelu_scat_kernel(tc, xT, wgt, wg_words, wg_scales, wu_words, wu_sc
 
         xb, xq, xs = {}, {}, {}
 
-        def weave(a, c0, c1, tag, copy, step=HALF):
-            xb[a, c0] = keep.tile([P, c1 - c0, PACK], BF16, name=f"xb{a}_{c0}", tag=tag, align_bytes=64)[:]
-            for c in range(c0, c1, step):
-                end = min(c1, c + step)
-                copy(xb[a, c0][:, c - c0:end - c0, :].rearrange("p (c e) i -> p c i e", e=4),
-                     (g0, g1)[a][:, :, c:end].rearrange("p i (c e) -> p c i e", e=4))
+        def weave(a, t0, t1, tag, copy):
+            xb[a, t0] = keep.tile([P, TOK * (t1 - t0), PACK], BF16, name=f"xb{a}_{t0}", tag=tag, align_bytes=64)[:]
+            copy(xb[a, t0].rearrange("p (c e) i -> p c i e", e=4),
+                 (g0, g1)[a][:, :, TOK * t0:TOK * t1].rearrange("p i (c e) -> p c i e", e=4))
 
-        def quantise_x(a, c0, c1, tag):
-            width = c1 - c0
-            codes = keep.tile([P, width], U32, name=f"xq{a}_{c0}", tag=tag, align_bytes=64)[:]
-            scales = keep.tile([P, width], U8, name=f"xs{a}_{c0 // TOK}", align_bytes=64)
-            nc.vector.quantize_mx(out=codes.bitcast(FP8X4), scales=scales[:], in_=xb[a, c0].rearrange("p c i -> p (c i)"))
-            for t in range(width // TOK):
-                xq[a, c0 // TOK + t] = codes[:, TOK * t:TOK * (t + 1)].bitcast(FP8X4)
-                xs[a, c0 // TOK + t] = scales[:, TOK * t:TOK * (t + 1)]
+        def quantise_x(a, t0, t1, tag):
+            width = TOK * (t1 - t0)
+            codes = keep.tile([P, width], U32, name=f"xq{a}_{t0}", tag=tag, align_bytes=64)[:]
+            scales = keep.tile([P, width], U8, name=f"xs{a}_{t0}", align_bytes=64)
+            nc.vector.quantize_mx(out=codes.bitcast(FP8X4), scales=scales[:], in_=xb[a, t0].rearrange("p c i -> p (c i)"))
+            for t in range(t0, t1):
+                xq[a, t] = codes[:, TOK * (t - t0):TOK * (t - t0 + 1)].bitcast(FP8X4)
+                xs[a, t] = scales[:, TOK * (t - t0):TOK * (t - t0 + 1)]
 
         for i in range(PACK):
             gather(0, i, 0, J)
-        weave(0, 0, HALF, "xb00", nc.scalar.copy)
-        weave(0, HALF, J, "xb01", nc.scalar.copy)
+        weave(0, 0, 4, "xb00", nc.scalar.copy)
+        weave(0, 4, 8, "xb01", nc.scalar.copy)
         gather(1, 0, 0, J)
         gather(1, 1, 0, J)
         w_sc = keep.tile([P, R], U8, name="w_sc", align_bytes=64)
         nc.vector.tensor_copy(w_sc[:].rearrange("p (b i q) -> p b q i", i=PACK, q=P),
                               sc_raw[:].rearrange("p (b q i) -> p b q i", i=PACK, q=P))
-        quantise_x(0, 0, HALF, "x11")
-        quantise_x(0, HALF, J, "xq01")
+        quantise_x(0, 0, 4, "x11")
+        quantise_x(0, 4, 8, "xq01")
         deal_weights(0, 0, 0, 2, False)
         gather(1, 2, 0, J)
         deal_weights(1, 0, 0, 2, False)
@@ -188,130 +175,160 @@ def tile_list_gelu_scat_kernel(tc, xT, wgt, wg_words, wg_scales, wu_words, wu_sc
                 first_pass(m, b, t, 0)
 
         gather(1, 3, 0, TOK)
-        weave(1, 0, TOK, "xb10", nc.scalar.copy)
-        gather(1, 3, TOK, HALF)
+        weave(1, 0, 1, "xb10", nc.scalar.copy)
+        gather(1, 3, TOK, EARLY)
         deal_weights(0, 1, 0, 1, False)
         deal_weights(1, 1, 0, 1, True)
-        quantise_x(1, 0, TOK, "xq10")
+        quantise_x(1, 0, 1, "xq10")
         deal_weights(0, 1, 1, 2, True)
-        weave(1, TOK, 2 * TOK, "xb10", nc.vector.tensor_copy)
+        weave(1, 1, 2, "xb10", nc.vector.tensor_copy)
         deal_weights(1, 1, 1, 2, True)
-        quantise_x(1, TOK, 2 * TOK, "xq11")
-        weave(1, 2 * TOK, 3 * TOK, "xb12", nc.scalar.copy)
-        quantise_x(1, 2 * TOK, 3 * TOK, "xq12")
-        weave(1, 3 * TOK, 4 * TOK, "xb10", nc.vector.tensor_copy)
-
-        acts, ups = {}, {}
-
-        def new_set(t):
-            acts[t] = keep.tile([P, R], F32, name=f"act{t}", tag=f"act{t % 5}", align_bytes=64)
-            ups[t] = keep.tile([P, R], F32, name=f"up{t}", tag=UP_TAGS[t], align_bytes=64)
+        quantise_x(1, 1, 2, "xq11")
+        weave(1, 2, 3, "xb12", nc.scalar.copy)
+        quantise_x(1, 2, 3, "xq12")
 
         def by_word(ap):
             return ap.rearrange("p (c i) -> p c i", i=PACK)
 
-        hq, hs = {}, {}
-
-        def quantise_h(t, hb, tag):
-            codes = keep.tile([P, 2 * TOK], U32, name=f"hq{t}", tag=tag, align_bytes=64)
-            scales = keep.tile([P, 2 * TOK], U8, name=f"hs{t}", align_bytes=64)
-            nc.vector.quantize_mx(out=codes[:].bitcast(FP8X4), scales=scales[:], in_=hb[:])
-            for b in range(2):
-                hq[t, b] = codes[:, TOK * b:TOK * (b + 1)].bitcast(FP8X4)
-                hs[t, b] = scales[:, TOK * b:TOK * (b + 1)]
-
-        def second_layer(pieces, tag):
-            units = [(n, t) for n, t0, t1 in pieces for t in range(t0, t1)]
-            acc = psum.tile([P, len(units) * TOK], F32, name=tag)
-            for k, (n, t) in enumerate(units):
-                for b in range(2):
-                    nc.tensor.matmul_mx(
-                        out=acc[:, TOK * k:TOK * (k + 1)],
-                        lhsT=wd_sb[:, b, 2 * P * n:2 * P * (n + 1)].bitcast(FP4X4),
-                        lhsT_scale=wd_sc[:, b, P * n:P * (n + 1)],
-                        rhs=hq[t, b], rhs_scale=hs[t, b],
-                        start=(b == 0), stop=(b == 1))
-            return acc
-
-        accs = []
-
-        def weigh(pieces, ys):
-            accs.append(second_layer(pieces, f"acc{len(accs) % 2}"))
-            acc = accs[-1]
-            k = 0
-            rest = pieces[1:]
-            spans = [(t0, t1) for n, t0, t1 in rest]
-            groups = [pieces[0][1:] + (1,)] + [span + (spans.count(span),) for span in sorted(set(spans), key=spans.index)]
-            for (t0, t1, count), y in zip(groups, ys):
-                width = TOK * (t1 - t0)
-                cols = slice(k, k + count * width)
-                nc.vector.tensor_tensor(
-                    y[:, 0:count * width].rearrange("p (n c) -> p n c", n=count),
-                    wgo_sb[:, TOK * t0:TOK * t1].unsqueeze(1).to_broadcast([P, count, width]),
-                    acc[:, cols].rearrange("p (n c) -> p n c", n=count), MULT)
-                k = k + count * width
-
-        def scatter_weighed(pieces, ys):
-            k = 0
-            for at, (n, t0, t1) in enumerate(pieces):
-                cols = place[:, TOK * t0 // PER_COL:TOK * t1 // PER_COL]
-                nc.vector.tensor_copy(win[n][:].indirect(cols), ys[min(at, 1)][:, k:k + TOK * (t1 - t0)])
-                k = (k + TOK * (t1 - t0)) * min(at, 1)
+        acts, ups = {}, {}
 
         def hidden(t, b):
             if b == 0:
-                new_set(t)
+                acts[t] = keep.tile([P, R], F32, name=f"act{t}", tag=ACT_TAGS[t], align_bytes=64)
+                ups[t] = keep.tile([P, R + 2 * TOK], F32, name=f"up{t}", tag=UP_TAGS[t], align_bytes=64)
             nc.scalar.activation(by_word(acts[t][:, HALF * b:HALF * (b + 1)]), first_layer(0, b, t), GELU)
             nc.scalar.copy(by_word(ups[t][:, HALF * b:HALF * (b + 1)]), first_layer(1, b, t))
 
-        act_first = keep.tile([P, HALF], F32, name="act_first", align_bytes=64)
-        hb = keep.tile([P, R], BF16, name="hb", align_bytes=64)
-        for b in range(2):
-            act = (act_first[:], g1[:, 3, HALF:J])[b]
-            nc.scalar.activation(by_word(act), first_layer(0, b, 0), GELU)
-            nc.vector.tensor_tensor(by_word(hb[:, HALF * b:HALF * (b + 1)]), by_word(act), first_layer(1, b, 0), MULT)
-        new_set(1)
-        for m in range(2):
-            for b in range(2):
-                first_pass(m, b, 1, 1)
-        for b in range(2):
-            nc.scalar.activation(by_word(acts[1][:, HALF * b:HALF * (b + 1)]), banks[0, b, 1][:].rearrange("p i c -> p c i"), GELU)
-        for b in range(2):
-            nc.scalar.copy(by_word(ups[1][:, HALF * b:HALF * (b + 1)]), banks[1, b, 1][:].rearrange("p i c -> p c i"))
-        quantise_x(1, 3 * TOK, 4 * TOK, "act_first")
-        quantise_h(0, hb, "hq0")
-        gather(1, 3, HALF, J)
-        y_new = [keep.tile([P, HALF], F32, name=tag, align_bytes=64)[:] for tag in ("fresh0", "x00")]
-        holds = ["fresh0", "x00"]
-        weigh(NEW[0], y_new)
-        scatter_weighed(NEW[0], y_new)
-        hidden(2, 0)
+        def new_hb(tiles):
+            return keep.tile([P, 2, tiles, HALF], BF16, name="hb", align_bytes=64)
 
-        for t in range(1, TILES):
-            late = t + LEAD
-            if late < TILES:
-                weave(1, TOK * late, TOK * (late + 1), f"xs1_{t}", nc.scalar.copy)
-            if t + 1 < TILES:
-                hidden(t + 1, 1)
-            hb = keep.tile([P, R], BF16, name="hb", align_bytes=64)
-            nc.gpsimd.tensor_tensor(hb[:], ups[t][:], acts[t][:], MULT)
-            if late < TILES:
-                quantise_x(1, TOK * late, TOK * (late + 1), holds.pop(0))
-            quantise_h(t, hb, holds[0])
-            y_old = (keep.tile([P, TOK], F32, name=f"first{t}", tag=f"act{t % 5}", align_bytes=64)[:], ups[t][:])
-            holds = [f"act{t % 5}", UP_TAGS[t]]
-            weigh(OLD[t], y_old)
-            scatter_weighed(OLD[t], y_old)
-            if t + 2 < TILES:
-                hidden(t + 2, 0)
-            if t in NEW:
-                holds = ["fresh1", "fresh2"]
-                y_new = [keep.tile([P, TOK], F32, name=tag, align_bytes=64)[:] for tag in holds]
-                weigh(NEW[t], y_new)
-                scatter_weighed(NEW[t], y_new)
+        def product(t, hb, k):
+            nc.gpsimd.tensor_tensor(hb[:, :, k, :], ups[t][:, 0:R].rearrange("p (b c) -> p b c", b=2),
+                                    acts[t][:].rearrange("p (b c) -> p b c", b=2), MULT)
+
+        hq, hs = {}, {}
+
+        def quantise_h(t0, t1, hb, tag):
+            width = TOK * (t1 - t0)
+            codes = keep.tile([P, 2 * width], U32, name=f"hq{t0}", tag=tag, align_bytes=64)
+            scales = keep.tile([P, 2 * width], U8, name=f"hs{t0}", align_bytes=64)
+            nc.vector.quantize_mx(out=codes[:].bitcast(FP8X4), scales=scales[:], in_=hb[:].rearrange("p b t c -> p (b t c)"))
+            for b in range(2):
+                for u0, u1 in [(t0, t1)] + [(t, t + 1) for t in range(t0, t1)]:
+                    cols = slice(width * b + TOK * (u0 - t0), width * b + TOK * (u1 - t0))
+                    hq[u0, u1, b] = codes[:, cols].bitcast(FP8X4)
+                    hs[u0, u1, b] = scales[:, cols]
+
+        def second_layer(pieces, tag):
+            acc = psum.tile([P, sum(TOK * (t1 - t0) for n, t0, t1 in pieces)], F32, name=tag)
+            k = 0
+            for n, t0, t1 in pieces:
+                t = t0
+                while t < t1:
+                    end = t + 2 if t + 2 <= t1 and (t, t + 2, 0) in hq else t + 1
+                    width = TOK * (end - t)
+                    for b in range(2):
+                        nc.tensor.matmul_mx(
+                            out=acc[:, k:k + width],
+                            lhsT=wd_sb[:, b, 2 * P * n:2 * P * (n + 1)].bitcast(FP4X4),
+                            lhsT_scale=wd_sc[:, b, P * n:P * (n + 1)],
+                            rhs=hq[t, end, b], rhs_scale=hs[t, end, b],
+                            start=(b == 0), stop=(b == 1))
+                    k = k + width
+                    t = end
+            return acc
+
+        def scatter(n, t0, t1, y):
+            nc.vector.tensor_copy(win[n][:].indirect(place[:, TOK * t0 // PER_COL:TOK * t1 // PER_COL]), y)
+
+        def weigh_together(rows, t0, t1, acc, host):
+            width = TOK * (t1 - t0)
+            y = ups[host][:, R + width - 2 * width:R + width - 2 * width + len(rows) * width]
+            nc.vector.tensor_tensor(
+                y.rearrange("p (n c) -> p n c", n=len(rows)),
+                wgo_sb[:, TOK * t0:TOK * t1].unsqueeze(1).to_broadcast([P, len(rows), width]),
+                acc[:].rearrange("p (n c) -> p n c", n=len(rows)), MULT)
+            return y
+
+        def scatter_together(rows, t0, t1, y):
+            width = TOK * (t1 - t0)
+            for k, n in enumerate(rows):
+                scatter(n, t0, t1, y[:, width * k:width * (k + 1)])
+
+        def fresh(rows, t0, t1, host):
+            width = TOK * (t1 - t0)
+            acc = second_layer([(n, t0, t1) for n in rows], "acc0")
+            tag = f"fresh{t0}"
+            ys = [ups[host][:, R:R + width], keep.tile([P, width], F32, name=tag, align_bytes=64)[:]]
+            for k, y in enumerate(ys):
+                nc.vector.tensor_tensor(y, wgo_sb[:, TOK * t0:TOK * t1], acc[:, width * k:width * (k + 1)], MULT)
+            for n, y in zip(rows, ys):
+                scatter(n, t0, t1, y)
+            return tag
+
+        hb = new_hb(2)
+        for t in range(2):
+            for b in range(2):
+                if (t, b) == (1, 1):
+                    act = g1_flat[:, 3 * J + EARLY:3 * J + EARLY + HALF]
+                else:
+                    act = keep.tile([P, HALF], F32, name=f"act_first{t}{b}", align_bytes=64)[:]
+                nc.scalar.activation(by_word(act), first_layer(0, b, t), GELU)
+                nc.vector.tensor_tensor(by_word(hb[:, b, t, :]), by_word(act), first_layer(1, b, t), MULT)
+        weave(1, 3, 5, "xs1_1", nc.scalar.copy)
+        quantise_h(0, 2, hb, "hq0")
+        gather(1, 3, EARLY, J)
+        quantise_x(1, 3, 5, "xq13")
+        hidden(2, 0)
+        hidden(2, 1)
+        hold = fresh((0, 1), 0, 2, 2)
+        acc = second_layer([(n, 0, 2) for n in (2, 3)], "acc1")
+        weave(1, 5, 8, "xs1_2", nc.scalar.copy)
+        hidden(3, 0)
+        hidden(3, 1)
+
+        hb = new_hb(1)
+        product(2, hb, 0)
+        y = weigh_together((2, 3), 0, 2, acc, 2)
+        quantise_h(2, 3, hb, hold)
+        quantise_x(1, 5, 8, ACT_TAGS[2])
+        scatter_together((2, 3), 0, 2, y)
+        hidden(4, 0)
+        hidden(4, 1)
+        hold = fresh((0, 1), 2, 3, 4)
+        acc = second_layer([(n, 2, 3) for n in (2, 3)], "acc1")
+        hidden(5, 0)
+        hidden(5, 1)
+
+        hb = new_hb(2)
+        product(3, hb, 0)
+        product(4, hb, 1)
+        y = weigh_together((2, 3), 2, 3, acc, 4)
+        quantise_h(3, 5, hb, hold)
+        scatter_together((2, 3), 2, 3, y)
+        hidden(6, 0)
+        hidden(6, 1)
+        hold = fresh((0, 1), 3, 5, 6)
+        acc = second_layer([(n, 3, 5) for n in (2, 3)], "acc1")
+        hidden(7, 0)
+        hidden(7, 1)
+
+        hb = new_hb(2)
+        product(5, hb, 0)
+        product(6, hb, 1)
+        y = weigh_together((2, 3), 3, 5, acc, 6)
+        quantise_h(5, 7, hb, hold)
+        scatter_together((2, 3), 3, 5, y)
+        acc = second_layer([(0, 5, 7)], "acc0")
+
+        hb = new_hb(1)
+        product(7, hb, 0)
+        y = weigh_together((0,), 5, 7, acc, 7)
+        quantise_h(7, 8, hb, UP_TAGS[6])
+        scatter_together((0,), 5, 7, y)
 
         for n, t0, t1 in LAST:
-            acc = second_layer([(n, t0, t1)], f"bank{(n + 4) % 6}")
+            acc = second_layer([(n, t0, t1)], f"bank{n}")
             y = g0[:, n, 0:TOK * (t1 - t0)]
             nc.scalar.copy(y, acc[:])
             cols = place[:, TOK * t0 // PER_COL:TOK * t1 // PER_COL]

@@ -1,6 +1,7 @@
 from contextlib import ExitStack
 
 import concourse.mybir as mybir
+from concourse.masks import make_identity
 
 K, R, N, T, J = 1024, 1024, 512, 2048, 1024
 FLOPS = 2 * J * (2 * K * R + R * N)
@@ -43,6 +44,8 @@ def tile_list_gelu_scat_kernel(tc, xT, wgt, wg_words, wg_scales, wu_words, wu_sc
 
         sc_raw = keep.tile([P, R], U8, name="sc_raw", align_bytes=64)
         nc.gpsimd.memset(sc_raw[:].bitcast(I32), 0)
+        ident = keep.tile([P, P], F32, name="ident")
+        make_identity(nc, ident[:])
         wd_sc = keep.tile([P, 2, N], U8, name="wd_sc", align_bytes=64)
         nc.gpsimd.memset(wd_sc[:].rearrange("p a r -> p (a r)").bitcast(I32), 0)
         win = [keep.tile([P, T], F32, name=f"win{n}") for n in range(PACK)]
@@ -67,14 +70,17 @@ def tile_list_gelu_scat_kernel(tc, xT, wgt, wg_words, wg_scales, wu_words, wu_sc
             nc.sync.dma_start(out=piece[:], in_=src.bitcast(I32))
             w_raw[m, a, b0] = piece
 
+        rows = keep.tile([P, TOK], F32, name="rows")
+        for w, src in enumerate((wgt, wgo)):
+            nc.sync.dma_start(out=rows[64 * w:64 * (w + 1), :], in_=src[0:P:PER_COL, :].rearrange("g (c e) -> g c e", e=TOK))
         load_plane(0)
         nc.sync.dma_start(pick[:], offs)
-        nc.sync.dma_start(out=wgt_sb[:], in_=wgt)
-        for plane in range(1, 6):
+        for plane in range(1, 5):
             load_plane(plane)
         load_scales(0)
-        load_weights(0, 0, 0, 2)
+        load_plane(5)
         load_scales(1)
+        load_weights(0, 0, 0, 2)
         load_plane(6)
         load_weights(1, 0, 0, 2)
         load_plane(7)
@@ -86,11 +92,36 @@ def tile_list_gelu_scat_kernel(tc, xT, wgt, wg_words, wg_scales, wu_words, wu_sc
         for q in range(4):
             nc.sync.dma_start(out=wd_sc[32 * q:32 * q + 4, :, :].bitcast(I32),
                               in_=wd_scales[:, 4 * q:4 * q + 4, :].rearrange("a q n -> q a n").bitcast(I32))
-        nc.sync.dma_start(out=wgo_sb[:], in_=wgo)
         nc.sync.dma_start(place[:], offs2)
 
         warm = keep.tile([P, 8], F32, name="warm")
-        nc.scalar.activation(warm[:], wgt_sb[:, 0:8], GELU)
+        nc.scalar.activation(warm[:], ident[:, 0:8], GELU)
+
+        turned = [psum.tile([P, P], F32, name=f"acc{k}") for k in range(2)]
+        for k in range(2):
+            nc.tensor.transpose(turned[k][:], rows[:], ident[:])
+
+        def widen(w, c0, c1, copy, src, tag):
+            wide = keep.tile([P, c1 - c0, 8, PER_COL], F32, name=f"wide{w}{c0}", tag=tag)
+            picked = src[:, 64 * w:64 * (w + 1)].rearrange("e (g c) -> e c g", c=TILES)[:, c0:c1, :]
+            copy(wide[:], picked.unsqueeze(3).to_broadcast([P, c1 - c0, 8, PER_COL]))
+            return wide
+
+        def spread(wide, c0, c1, first, copy, dst, bank):
+            back = psum.tile([P, c1 - c0, TOK], F32, name=bank)
+            for c in range(c0, c1):
+                nc.tensor.transpose(back[:, c - c0, :], wide[:, c - first, :, :].rearrange("e g r -> e (g r)"), ident[:])
+            copy(dst[:, TOK * c0:TOK * c1], back[:].rearrange("p c e -> p (c e)"))
+
+        wide_a = widen(0, 0, 2, nc.vector.tensor_copy, turned[0], "wide_a")
+        wide_b = widen(0, 2, 4, nc.vector.tensor_copy, turned[0], "wide_b")
+        wide_c = widen(0, 4, 8, nc.scalar.copy, turned[1], "wide_c")
+        spread(wide_a, 0, 2, 0, nc.vector.tensor_copy, wgt_sb, "bank0")
+        spread(wide_b, 2, 4, 2, nc.scalar.copy, wgt_sb, "bank1")
+        spread(wide_c, 4, 8, 4, nc.scalar.copy, wgt_sb, "bank2")
+        wide_o = widen(1, 0, 8, nc.scalar.copy, turned[1], "wide_c")
+        spread(wide_o, 0, 4, 0, nc.scalar.copy, wgo_sb, "bank3")
+        spread(wide_o, 4, 8, 0, nc.scalar.copy, wgo_sb, "bank4")
 
         g0 = keep.tile([P, PACK, J], F32, name="g0")
         g1_flat = keep.tile([P, PACK * J + TOK], F32, name="g1", align_bytes=64)
@@ -129,7 +160,10 @@ def tile_list_gelu_scat_kernel(tc, xT, wgt, wg_words, wg_scales, wu_words, wu_sc
                 xq[a, t] = codes[:, TOK * (t - t0):TOK * (t - t0 + 1)].bitcast(FP8X4)
                 xs[a, t] = scales[:, TOK * (t - t0):TOK * (t - t0 + 1)]
 
-        for i in range(PACK):
+        gather(0, 0, 0, 2 * TOK)
+        gather(0, 0, 2 * TOK, HALF)
+        gather(0, 0, HALF, J)
+        for i in range(1, PACK):
             gather(0, i, 0, J)
         weave(0, 0, 4, "xb00", nc.scalar.copy)
         weave(0, 4, 8, "xb01", nc.scalar.copy)

@@ -15,6 +15,7 @@ U8 = mybir.dt.uint8
 FP8X4 = mybir.dt.float8_e4m3fn_x4
 FP4X4 = mybir.dt.float4_e2m1fn_x4
 MULT = mybir.AluOpType.mult
+COPY = mybir.ActivationFunctionType.Copy
 GELU = mybir.ActivationFunctionType.Gelu_apprx_tanh
 
 P = 128
@@ -56,11 +57,11 @@ def tile_list_gelu_scat_kernel(tc, xT, wgt, wg_words, wg_scales, wu_words, wu_sc
             a, i = divmod(plane, PACK)
             nc.sync.dma_start(out=x_sb[a][i][:], in_=x_rows[a, i])
 
-        def load_scales(m):
-            for q in range(4):
-                row = 32 * q + 8 * m
-                nc.sync.dma_start(out=sc_raw[row:row + 8, :].bitcast(I32),
-                                  in_=(wg_scales, wu_scales)[m][:, 4 * q:4 * q + 4, :].bitcast(I32))
+        def load_scales(first, last):
+            for k in range(first, last):
+                m, a, r = k // 8, k // 4 % 2, k % 4
+                nc.sync.dma_start(out=sc_raw[8 * m + 4 * a + r:P:32, :].bitcast(I32),
+                                  in_=(wg_scales, wu_scales)[m][a, r:16:4, :].bitcast(I32))
 
         w_raw, w_sb = {}, {}
 
@@ -75,11 +76,11 @@ def tile_list_gelu_scat_kernel(tc, xT, wgt, wg_words, wg_scales, wu_words, wu_sc
             nc.sync.dma_start(out=rows[64 * w:64 * (w + 1), :], in_=src[0:P:PER_COL, :].rearrange("g (c e) -> g c e", e=TOK))
         load_plane(0)
         nc.sync.dma_start(pick[:], offs)
-        for plane in range(1, 5):
+        load_plane(1)
+        load_plane(2)
+        for plane in range(3, 6):
             load_plane(plane)
-        load_scales(0)
-        load_plane(5)
-        load_scales(1)
+            load_scales(6 * (plane - 3), min(16, 6 * (plane - 2)))
         load_weights(0, 0, 0, 2)
         load_plane(6)
         load_weights(1, 0, 0, 2)
@@ -119,6 +120,8 @@ def tile_list_gelu_scat_kernel(tc, xT, wgt, wg_words, wg_scales, wu_words, wu_sc
         spread(wide_a, 0, 2, 0, nc.vector.tensor_copy, wgt_sb, "bank0")
         spread(wide_b, 2, 4, 2, nc.scalar.copy, wgt_sb, "bank1")
         spread(wide_c, 4, 8, 4, nc.scalar.copy, wgt_sb, "bank2")
+        by_token = keep.tile([P, 8, TILES], F32, name="by_token")
+        nc.scalar.copy(by_token[:].rearrange("e g c -> e (g c)"), turned[1][:, 64:P])
         wide_o = widen(1, 0, 8, nc.scalar.copy, turned[1], "wide_c")
         spread(wide_o, 0, 4, 0, nc.scalar.copy, wgo_sb, "bank3")
         spread(wide_o, 4, 8, 0, nc.scalar.copy, wgo_sb, "bank4")
@@ -173,7 +176,6 @@ def tile_list_gelu_scat_kernel(tc, xT, wgt, wg_words, wg_scales, wu_words, wu_sc
         nc.vector.tensor_copy(w_sc[:].rearrange("p (b i q) -> p b q i", i=PACK, q=P),
                               sc_raw[:].rearrange("p (b q i) -> p b q i", i=PACK, q=P))
         quantise_x(0, 0, 4, "x11")
-        quantise_x(0, 4, 8, "xq01")
         deal_weights(0, 0, 0, 2, False)
         gather(1, 2, 0, J)
         deal_weights(1, 0, 0, 2, False)
@@ -284,16 +286,41 @@ def tile_list_gelu_scat_kernel(tc, xT, wgt, wg_words, wg_scales, wu_words, wu_sc
                 acc[:].rearrange("p (n c) -> p n c", n=len(rows)), MULT)
             return y
 
+        def weigh_on_scalar(t0, t1):
+            tiles = t1 - t0
+            flat = psum.tile([P, tiles, 2, 8, PER_COL], F32, name="acc1")
+            for t in range(t0, t1):
+                for b in range(2):
+                    nc.tensor.matmul_mx(
+                        out=flat[:, t - t0].rearrange("e n g r -> e (n g r)"),
+                        lhsT=hq[t, t + 1, b], lhsT_scale=hs[t, t + 1, b],
+                        rhs=wd_sb[:, b, N:2 * N].bitcast(FP4X4), rhs_scale=wd_sc[:, b, N // 2:N],
+                        start=(b == 0), stop=(b == 1))
+            weighed = keep.tile([P, tiles, 2, 8, PER_COL], F32, name="weighed")
+            for t in range(t0, t1):
+                for g in range(8):
+                    nc.scalar.activation(weighed[:, t - t0, :, g, :], flat[:, t - t0, :, g, :], COPY, scale=by_token[:, g, t:t + 1])
+            return weighed
+
+        def turn_back(weighed, tiles):
+            back = psum.tile([P, 2, tiles, TOK], F32, name="acc0")
+            for n in range(2):
+                for k in range(tiles):
+                    nc.tensor.transpose(back[:, n, k, :], weighed[:, k, n].rearrange("e g r -> e (g r)"), ident[:])
+            return back
+
         def scatter_together(rows, t0, t1, y):
             width = TOK * (t1 - t0)
             for k, n in enumerate(rows):
                 scatter(n, t0, t1, y[:, width * k:width * (k + 1)])
 
-        def fresh(rows, t0, t1, host):
+        def fresh(rows, t0, t1, host, hold_first=False):
             width = TOK * (t1 - t0)
             acc = second_layer([(n, t0, t1) for n in rows], "acc0")
             tag = f"fresh{t0}"
             ys = [ups[host][:, R:R + width], keep.tile([P, width], F32, name=tag, align_bytes=64)[:]]
+            if hold_first:
+                ys = [ys[1], ys[0]]
             for k, y in enumerate(ys):
                 nc.vector.tensor_tensor(y, wgo_sb[:, TOK * t0:TOK * t1], acc[:, width * k:width * (k + 1)], MULT)
             for n, y in zip(rows, ys):
@@ -310,6 +337,7 @@ def tile_list_gelu_scat_kernel(tc, xT, wgt, wg_words, wg_scales, wu_words, wu_sc
                 nc.scalar.activation(by_word(act), first_layer(0, b, t), GELU)
                 nc.vector.tensor_tensor(by_word(hb[:, b, t, :]), by_word(act), first_layer(1, b, t), MULT)
         weave(1, 3, 5, "xs1_1", nc.scalar.copy)
+        quantise_x(0, 4, 8, "xq11")
         quantise_h(0, 2, hb, "hq0")
         gather(1, 3, EARLY, J)
         quantise_x(1, 3, 5, "xq13")
@@ -342,24 +370,28 @@ def tile_list_gelu_scat_kernel(tc, xT, wgt, wg_words, wg_scales, wu_words, wu_sc
         scatter_together((2, 3), 2, 3, y)
         hidden(6, 0)
         hidden(6, 1)
-        hold = fresh((0, 1), 3, 5, 6)
-        acc = second_layer([(n, 3, 5) for n in (2, 3)], "acc1")
+        hold = fresh((0, 1), 3, 5, 6, True)
+        weighed = weigh_on_scalar(3, 5)
         hidden(7, 0)
         hidden(7, 1)
+        back = turn_back(weighed, 2)
 
         hb = new_hb(2)
         product(5, hb, 0)
         product(6, hb, 1)
-        y = weigh_together((2, 3), 3, 5, acc, 6)
+        y = ups[6][:, 0:HALF]
+        nc.scalar.copy(y, back[:].rearrange("p n k c -> p (n k c)"))
         quantise_h(5, 7, hb, hold)
         scatter_together((2, 3), 3, 5, y)
         acc = second_layer([(0, 5, 7)], "acc0")
 
         hb = new_hb(1)
         product(7, hb, 0)
-        y = weigh_together((0,), 5, 7, acc, 7)
-        quantise_h(7, 8, hb, UP_TAGS[6])
-        scatter_together((0,), 5, 7, y)
+        quantise_h(7, 8, hb, "hq7")
+        y = ups[7][:, 0:2 * TOK]
+        nc.scalar.copy(y, acc[:])
+        cols = place[:, 5 * TOK // PER_COL:7 * TOK // PER_COL]
+        nc.vector.tensor_tensor(win[0][:].indirect(cols), y, wgo_sb[:, 5 * TOK:7 * TOK], MULT)
 
         for n, t0, t1 in LAST:
             acc = second_layer([(n, t0, t1)], f"bank{n}")

@@ -302,8 +302,8 @@ def tile_list_gelu_scat_kernel(tc, xT, wgt, wg_words, wg_scales, wu_words, wu_sc
                     nc.scalar.activation(weighed[:, t - t0, :, g, :], flat[:, t - t0, :, g, :], COPY, scale=by_token[:, g, t:t + 1])
             return weighed
 
-        def turn_back(weighed, tiles):
-            back = psum.tile([P, 2, tiles, TOK], F32, name="acc0")
+        def turn_back(weighed, tiles, bank):
+            back = psum.tile([P, 2, tiles, TOK], F32, name=bank)
             for n in range(2):
                 for k in range(tiles):
                     nc.tensor.transpose(back[:, n, k, :], weighed[:, k, n].rearrange("e g r -> e (g r)"), ident[:])
@@ -357,24 +357,26 @@ def tile_list_gelu_scat_kernel(tc, xT, wgt, wg_words, wg_scales, wu_words, wu_sc
         scatter_together((2, 3), 0, 2, y)
         hidden(4, 0)
         hidden(4, 1)
-        hold = fresh((0, 1), 2, 3, 4)
-        acc = second_layer([(n, 2, 3) for n in (2, 3)], "acc1")
+        hold = fresh((0, 1), 2, 3, 4, True)
+        weighed = weigh_on_scalar(2, 3)
         hidden(5, 0)
         hidden(5, 1)
 
         hb = new_hb(2)
         product(3, hb, 0)
         product(4, hb, 1)
-        y = weigh_together((2, 3), 2, 3, acc, 4)
+        hidden(6, 0)
+        back = turn_back(weighed, 1, "acc1")
+        y = ups[4][:, 0:2 * TOK]
+        nc.scalar.copy(y, back[:].rearrange("p n k c -> p (n k c)"))
         quantise_h(3, 5, hb, hold)
         scatter_together((2, 3), 2, 3, y)
-        hidden(6, 0)
         hidden(6, 1)
         hold = fresh((0, 1), 3, 5, 6, True)
         weighed = weigh_on_scalar(3, 5)
         hidden(7, 0)
         hidden(7, 1)
-        back = turn_back(weighed, 2)
+        back = turn_back(weighed, 2, "acc1")
 
         hb = new_hb(2)
         product(5, hb, 0)

from contextlib import ExitStack

import concourse.mybir as mybir
from concourse.masks import make_identity

K, R, N, T, J = 1024, 1024, 512, 2048, 1024
FLOPS = 2 * J * (2 * K * R + R * N)

F32 = mybir.dt.float32
BF16 = mybir.dt.bfloat16
I32 = mybir.dt.int32
U32 = mybir.dt.uint32
U16 = mybir.dt.uint16
U8 = mybir.dt.uint8
FP8X4 = mybir.dt.float8_e4m3fn_x4
FP4X4 = mybir.dt.float4_e2m1fn_x4
MULT = mybir.AluOpType.mult
COPY = mybir.ActivationFunctionType.Copy
GELU = mybir.ActivationFunctionType.Gelu_apprx_tanh

P = 128
PACK = 4
HALF = 512
TOK = 128
TILES = J // TOK
PER_COL = 16
EARLY = 5 * TOK
ACT_TAGS = {2: "act0", 3: "act1", 4: "act2", 5: "x13", 6: "act1", 7: "act2"}
UP_TAGS = {2: "x00", 3: "x01", 4: "x02", 5: "x03", 6: "x10", 7: "x12"}
LAST = [(0, 7, 8), (1, 5, 8), (2, 5, 8), (3, 5, 8)]


def tile_list_gelu_scat_kernel(tc, xT, wgt, wg_words, wg_scales, wu_words, wu_scales, wd_words, wd_scales, wgo, offs, offs2, out):
    nc = tc.nc
    with ExitStack() as ctx:
        keep = ctx.enter_context(tc.tile_pool(name="keep", bufs=1))
        psum = ctx.enter_context(tc.psum_pool(name="psum", bufs=1))

        pick = keep.tile([P, J // PER_COL], U16, name="pick")
        place = keep.tile([P, J // PER_COL], U16, name="place")
        wgt_sb = keep.tile([P, J], F32, name="wgt_sb")
        wgo_sb = keep.tile([P, J], F32, name="wgo_sb")
        x_sb = [[keep.tile([P, T], F32, name=f"x{a}{i}", align_bytes=64) for i in range(PACK)] for a in range(2)]
        x_rows = xT.rearrange("(a p i) t -> a i p t", a=2, i=PACK)

        sc_raw = keep.tile([P, R], U8, name="sc_raw", align_bytes=64)
        nc.gpsimd.memset(sc_raw[:].bitcast(I32), 0)
        ident = keep.tile([P, P], F32, name="ident")
        make_identity(nc, ident[:])
        wd_sc = keep.tile([P, 2, N], U8, name="wd_sc", align_bytes=64)
        nc.gpsimd.memset(wd_sc[:].rearrange("p a r -> p (a r)").bitcast(I32), 0)
        win = [keep.tile([P, T], F32, name=f"win{n}") for n in range(PACK)]
        for n in range(PACK):
            nc.gpsimd.memset(win[n][:], 0.0)

        def load_plane(plane):
            a, i = divmod(plane, PACK)
            nc.sync.dma_start(out=x_sb[a][i][:], in_=x_rows[a, i])

        def load_scales(first, last):
            for k in range(first, last):
                m, a, r = k // 8, k // 4 % 2, k % 4
                nc.sync.dma_start(out=sc_raw[8 * m + 4 * a + r:P:32, :].bitcast(I32),
                                  in_=(wg_scales, wu_scales)[m][a, r:16:4, :].bitcast(I32))

        w_raw, w_sb = {}, {}

        def load_weights(m, a, b0, b1):
            piece = keep.tile([P, (b1 - b0) * HALF], I32, name=f"w_raw{m}{a}{b0}", align_bytes=64)
            src = (wg_words, wu_words)[m][a].rearrange("p r i -> p (r i)")[:, 2048 * b0:2048 * b1]
            nc.sync.dma_start(out=piece[:], in_=src.bitcast(I32))
            w_raw[m, a, b0] = piece

        rows = keep.tile([P, TOK], F32, name="rows")
        for w, src in enumerate((wgt, wgo)):
            nc.sync.dma_start(out=rows[64 * w:64 * (w + 1), :], in_=src[0:P:PER_COL, :].rearrange("g (c e) -> g c e", e=TOK))
        load_plane(0)
        nc.sync.dma_start(pick[:], offs)
        load_plane(1)
        load_plane(2)
        for plane in range(3, 6):
            load_plane(plane)
            load_scales(6 * (plane - 3), min(16, 6 * (plane - 2)))
        load_weights(0, 0, 0, 2)
        load_plane(6)
        load_weights(1, 0, 0, 2)
        load_plane(7)
        for b in range(2):
            for m in range(2):
                load_weights(m, 1, b, b + 1)
        wd_sb = keep.tile([P, 2, 2 * N], U8, name="wd_sb", align_bytes=64)
        nc.sync.dma_start(out=wd_sb[:].bitcast(I32), in_=wd_words.rearrange("a p c -> p a c").bitcast(I32))
        for q in range(4):
            nc.sync.dma_start(out=wd_sc[32 * q:32 * q + 4, :, :].bitcast(I32),
                              in_=wd_scales[:, 4 * q:4 * q + 4, :].rearrange("a q n -> q a n").bitcast(I32))
        nc.sync.dma_start(place[:], offs2)

        warm = keep.tile([P, 8], F32, name="warm")
        nc.scalar.activation(warm[:], ident[:, 0:8], GELU)

        turned = [psum.tile([P, P], F32, name=f"acc{k}") for k in range(2)]
        for k in range(2):
            nc.tensor.transpose(turned[k][:], rows[:], ident[:])

        def widen(w, c0, c1, copy, src, tag):
            wide = keep.tile([P, c1 - c0, 8, PER_COL], F32, name=f"wide{w}{c0}", tag=tag)
            picked = src[:, 64 * w:64 * (w + 1)].rearrange("e (g c) -> e c g", c=TILES)[:, c0:c1, :]
            copy(wide[:], picked.unsqueeze(3).to_broadcast([P, c1 - c0, 8, PER_COL]))
            return wide

        def spread(wide, c0, c1, first, copy, dst, bank):
            back = psum.tile([P, c1 - c0, TOK], F32, name=bank)
            for c in range(c0, c1):
                nc.tensor.transpose(back[:, c - c0, :], wide[:, c - first, :, :].rearrange("e g r -> e (g r)"), ident[:])
            copy(dst[:, TOK * c0:TOK * c1], back[:].rearrange("p c e -> p (c e)"))

        wide_a = widen(0, 0, 2, nc.vector.tensor_copy, turned[0], "wide_a")
        wide_b = widen(0, 2, 4, nc.vector.tensor_copy, turned[0], "wide_b")
        wide_c = widen(0, 4, 8, nc.scalar.copy, turned[1], "wide_c")
        spread(wide_a, 0, 2, 0, nc.vector.tensor_copy, wgt_sb, "bank0")
        spread(wide_b, 2, 4, 2, nc.scalar.copy, wgt_sb, "bank1")
        spread(wide_c, 4, 8, 4, nc.scalar.copy, wgt_sb, "bank2")
        by_token = keep.tile([P, 8, TILES], F32, name="by_token")
        nc.scalar.copy(by_token[:].rearrange("e g c -> e (g c)"), turned[1][:, 64:P])
        wide_o = widen(1, 0, 8, nc.scalar.copy, turned[1], "wide_c")
        spread(wide_o, 0, 4, 0, nc.scalar.copy, wgo_sb, "bank3")
        spread(wide_o, 4, 8, 0, nc.scalar.copy, wgo_sb, "bank4")

        g0 = keep.tile([P, PACK, J], F32, name="g0")
        g1_flat = keep.tile([P, PACK * J + TOK], F32, name="g1", align_bytes=64)
        g1 = g1_flat[:, 0:PACK * J].rearrange("p (i j) -> p i j", i=PACK)

        def gather(a, i, c0, c1):
            cols = pick[:, c0 // PER_COL:c1 // PER_COL]
            nc.vector.tensor_tensor((g0, g1)[a][:, i, c0:c1], x_sb[a][i][:].indirect(cols), wgt_sb[:, c0:c1], MULT)

        def deal_weights(m, a, b0, b1, on_vector):
            dealt = keep.tile([P, (b1 - b0) * HALF], I32, name=f"w_sb{m}{a}{b0}", align_bytes=64)
            dst = dealt[:].rearrange("p (b i q) -> p b q i", i=PACK, q=P)
            src = w_raw[m, a, b0][:].rearrange("p (b q i) -> p b q i", i=PACK, q=P)
            if on_vector:
                nc.vector.tensor_copy(dst, src)
            else:
                nc.scalar.copy(dst.bitcast(U32), src.bitcast(U32))
            for b in range(b0, b1):
                for i in range(PACK):
                    c = HALF * (b - b0) + P * i
                    w_sb[m, a, b, i] = dealt[:, c:c + P].bitcast(FP8X4)

        xb, xq, xs = {}, {}, {}

        def weave(a, t0, t1, tag, copy):
            xb[a, t0] = keep.tile([P, TOK * (t1 - t0), PACK], BF16, name=f"xb{a}_{t0}", tag=tag, align_bytes=64)[:]
            copy(xb[a, t0].rearrange("p (c e) i -> p c i e", e=4),
                 (g0, g1)[a][:, :, TOK * t0:TOK * t1].rearrange("p i (c e) -> p c i e", e=4))

        def quantise_x(a, t0, t1, tag):
            width = TOK * (t1 - t0)
            codes = keep.tile([P, width], U32, name=f"xq{a}_{t0}", tag=tag, align_bytes=64)[:]
            scales = keep.tile([P, width], U8, name=f"xs{a}_{t0}", align_bytes=64)
            nc.vector.quantize_mx(out=codes.bitcast(FP8X4), scales=scales[:], in_=xb[a, t0].rearrange("p c i -> p (c i)"))
            for t in range(t0, t1):
                xq[a, t] = codes[:, TOK * (t - t0):TOK * (t - t0 + 1)].bitcast(FP8X4)
                xs[a, t] = scales[:, TOK * (t - t0):TOK * (t - t0 + 1)]

        gather(0, 0, 0, 2 * TOK)
        gather(0, 0, 2 * TOK, HALF)
        gather(0, 0, HALF, J)
        for i in range(1, PACK):
            gather(0, i, 0, J)
        weave(0, 0, 4, "xb00", nc.scalar.copy)
        weave(0, 4, 8, "xb01", nc.scalar.copy)
        gather(1, 0, 0, J)
        gather(1, 1, 0, J)
        w_sc = keep.tile([P, R], U8, name="w_sc", align_bytes=64)
        nc.vector.tensor_copy(w_sc[:].rearrange("p (b i q) -> p b q i", i=PACK, q=P),
                              sc_raw[:].rearrange("p (b q i) -> p b q i", i=PACK, q=P))
        quantise_x(0, 0, 4, "x11")
        deal_weights(0, 0, 0, 2, False)
        gather(1, 2, 0, J)
        deal_weights(1, 0, 0, 2, False)

        banks = {}
        ring = []

        def first_pass(m, b, t, a):
            if a == 0:
                if (b, t) == (1, 1):
                    tag = f"acc{m}"
                else:
                    tag = f"bank{len(ring) % 6}"
                    ring.append(tag)
                banks[m, b, t] = psum.tile([P, PACK, TOK], F32, name=tag)
            row = 8 * m + 4 * a
            for i in range(PACK):
                c = HALF * b + P * i
                nc.tensor.matmul_mx(
                    out=banks[m, b, t][:, i, :],
                    lhsT=w_sb[m, a, b, i], lhsT_scale=w_sc[row:, c:c + P],
                    rhs=xq[a, t], rhs_scale=xs[a, t],
                    start=(a == 0 and i == 0), stop=(a == 1 and i == PACK - 1))

        def first_layer(m, b, t):
            if (m, b, t) not in banks:
                first_pass(m, b, t, 0)
            first_pass(m, b, t, 1)
            return banks[m, b, t][:].rearrange("p i c -> p c i")

        for t, b in ((0, 0), (0, 1), (1, 0), (1, 1)):
            for m in range(2):
                first_pass(m, b, t, 0)

        gather(1, 3, 0, TOK)
        weave(1, 0, 1, "xb10", nc.scalar.copy)
        gather(1, 3, TOK, EARLY)
        deal_weights(0, 1, 0, 1, False)
        deal_weights(1, 1, 0, 1, True)
        quantise_x(1, 0, 1, "xq10")
        deal_weights(0, 1, 1, 2, True)
        weave(1, 1, 2, "xb10", nc.vector.tensor_copy)
        deal_weights(1, 1, 1, 2, True)
        quantise_x(1, 1, 2, "xq11")
        weave(1, 2, 3, "xb12", nc.scalar.copy)
        quantise_x(1, 2, 3, "xq12")

        def by_word(ap):
            return ap.rearrange("p (c i) -> p c i", i=PACK)

        acts, ups = {}, {}

        def hidden(t, b):
            if b == 0:
                acts[t] = keep.tile([P, R], F32, name=f"act{t}", tag=ACT_TAGS[t], align_bytes=64)
                ups[t] = keep.tile([P, R + 2 * TOK], F32, name=f"up{t}", tag=UP_TAGS[t], align_bytes=64)
            nc.scalar.activation(by_word(acts[t][:, HALF * b:HALF * (b + 1)]), first_layer(0, b, t), GELU)
            nc.scalar.copy(by_word(ups[t][:, HALF * b:HALF * (b + 1)]), first_layer(1, b, t))

        def new_hb(tiles):
            return keep.tile([P, 2, tiles, HALF], BF16, name="hb", align_bytes=64)

        def product(t, hb, k):
            nc.gpsimd.tensor_tensor(hb[:, :, k, :], ups[t][:, 0:R].rearrange("p (b c) -> p b c", b=2),
                                    acts[t][:].rearrange("p (b c) -> p b c", b=2), MULT)

        hq, hs = {}, {}

        def quantise_h(t0, t1, hb, tag):
            width = TOK * (t1 - t0)
            codes = keep.tile([P, 2 * width], U32, name=f"hq{t0}", tag=tag, align_bytes=64)
            scales = keep.tile([P, 2 * width], U8, name=f"hs{t0}", align_bytes=64)
            nc.vector.quantize_mx(out=codes[:].bitcast(FP8X4), scales=scales[:], in_=hb[:].rearrange("p b t c -> p (b t c)"))
            for b in range(2):
                for u0, u1 in [(t0, t1)] + [(t, t + 1) for t in range(t0, t1)]:
                    cols = slice(width * b + TOK * (u0 - t0), width * b + TOK * (u1 - t0))
                    hq[u0, u1, b] = codes[:, cols].bitcast(FP8X4)
                    hs[u0, u1, b] = scales[:, cols]

        def second_layer(pieces, tag):
            acc = psum.tile([P, sum(TOK * (t1 - t0) for n, t0, t1 in pieces)], F32, name=tag)
            k = 0
            for n, t0, t1 in pieces:
                t = t0
                while t < t1:
                    end = t + 2 if t + 2 <= t1 and (t, t + 2, 0) in hq else t + 1
                    width = TOK * (end - t)
                    for b in range(2):
                        nc.tensor.matmul_mx(
                            out=acc[:, k:k + width],
                            lhsT=wd_sb[:, b, 2 * P * n:2 * P * (n + 1)].bitcast(FP4X4),
                            lhsT_scale=wd_sc[:, b, P * n:P * (n + 1)],
                            rhs=hq[t, end, b], rhs_scale=hs[t, end, b],
                            start=(b == 0), stop=(b == 1))
                    k = k + width
                    t = end
            return acc

        def scatter(n, t0, t1, y):
            nc.vector.tensor_copy(win[n][:].indirect(place[:, TOK * t0 // PER_COL:TOK * t1 // PER_COL]), y)

        def weigh_together(rows, t0, t1, acc, host):
            width = TOK * (t1 - t0)
            y = ups[host][:, R + width - 2 * width:R + width - 2 * width + len(rows) * width]
            nc.vector.tensor_tensor(
                y.rearrange("p (n c) -> p n c", n=len(rows)),
                wgo_sb[:, TOK * t0:TOK * t1].unsqueeze(1).to_broadcast([P, len(rows), width]),
                acc[:].rearrange("p (n c) -> p n c", n=len(rows)), MULT)
            return y

        def weigh_on_scalar(t0, t1):
            tiles = t1 - t0
            flat = psum.tile([P, tiles, 2, 8, PER_COL], F32, name="acc1")
            for t in range(t0, t1):
                for b in range(2):
                    nc.tensor.matmul_mx(
                        out=flat[:, t - t0].rearrange("e n g r -> e (n g r)"),
                        lhsT=hq[t, t + 1, b], lhsT_scale=hs[t, t + 1, b],
                        rhs=wd_sb[:, b, N:2 * N].bitcast(FP4X4), rhs_scale=wd_sc[:, b, N // 2:N],
                        start=(b == 0), stop=(b == 1))
            weighed = keep.tile([P, tiles, 2, 8, PER_COL], F32, name="weighed")
            for t in range(t0, t1):
                for g in range(8):
                    nc.scalar.activation(weighed[:, t - t0, :, g, :], flat[:, t - t0, :, g, :], COPY, scale=by_token[:, g, t:t + 1])
            return weighed

        def turn_back(weighed, tiles, bank):
            back = psum.tile([P, 2, tiles, TOK], F32, name=bank)
            for n in range(2):
                for k in range(tiles):
                    nc.tensor.transpose(back[:, n, k, :], weighed[:, k, n].rearrange("e g r -> e (g r)"), ident[:])
            return back

        def scatter_together(rows, t0, t1, y):
            width = TOK * (t1 - t0)
            for k, n in enumerate(rows):
                scatter(n, t0, t1, y[:, width * k:width * (k + 1)])

        def fresh(rows, t0, t1, host, hold_first=False):
            width = TOK * (t1 - t0)
            acc = second_layer([(n, t0, t1) for n in rows], "acc0")
            tag = f"fresh{t0}"
            ys = [ups[host][:, R:R + width], keep.tile([P, width], F32, name=tag, align_bytes=64)[:]]
            if hold_first:
                ys = [ys[1], ys[0]]
            for k, y in enumerate(ys):
                nc.vector.tensor_tensor(y, wgo_sb[:, TOK * t0:TOK * t1], acc[:, width * k:width * (k + 1)], MULT)
            for n, y in zip(rows, ys):
                scatter(n, t0, t1, y)
            return tag

        hb = new_hb(2)
        for t in range(2):
            for b in range(2):
                if (t, b) == (1, 1):
                    act = g1_flat[:, 3 * J + EARLY:3 * J + EARLY + HALF]
                else:
                    act = keep.tile([P, HALF], F32, name=f"act_first{t}{b}", align_bytes=64)[:]
                nc.scalar.activation(by_word(act), first_layer(0, b, t), GELU)
                nc.vector.tensor_tensor(by_word(hb[:, b, t, :]), by_word(act), first_layer(1, b, t), MULT)
        weave(1, 3, 5, "xs1_1", nc.scalar.copy)
        quantise_x(0, 4, 8, "xq11")
        quantise_h(0, 2, hb, "hq0")
        gather(1, 3, EARLY, J)
        quantise_x(1, 3, 5, "xq13")
        hidden(2, 0)
        hidden(2, 1)
        hold = fresh((0, 1), 0, 2, 2)
        acc = second_layer([(n, 0, 2) for n in (2, 3)], "acc1")
        weave(1, 5, 8, "xs1_2", nc.scalar.copy)
        hidden(3, 0)
        hidden(3, 1)

        hb = new_hb(1)
        product(2, hb, 0)
        y = weigh_together((2, 3), 0, 2, acc, 2)
        quantise_h(2, 3, hb, hold)
        quantise_x(1, 5, 8, ACT_TAGS[2])
        scatter_together((2, 3), 0, 2, y)
        hidden(4, 0)
        hidden(4, 1)
        hold = fresh((0, 1), 2, 3, 4, True)
        weighed = weigh_on_scalar(2, 3)
        hidden(5, 0)
        hidden(5, 1)

        hb = new_hb(2)
        product(3, hb, 0)
        product(4, hb, 1)
        hidden(6, 0)
        back = turn_back(weighed, 1, "acc1")
        y = ups[4][:, 0:2 * TOK]
        nc.scalar.copy(y, back[:].rearrange("p n k c -> p (n k c)"))
        quantise_h(3, 5, hb, hold)
        scatter_together((2, 3), 2, 3, y)
        hidden(6, 1)
        hold = fresh((0, 1), 3, 5, 6, True)
        weighed = weigh_on_scalar(3, 5)
        hidden(7, 0)
        hidden(7, 1)
        back = turn_back(weighed, 2, "acc1")

        hb = new_hb(2)
        product(5, hb, 0)
        product(6, hb, 1)
        y = ups[6][:, 0:HALF]
        nc.scalar.copy(y, back[:].rearrange("p n k c -> p (n k c)"))
        quantise_h(5, 7, hb, hold)
        scatter_together((2, 3), 3, 5, y)
        acc = second_layer([(0, 5, 7)], "acc0")

        hb = new_hb(1)
        product(7, hb, 0)
        quantise_h(7, 8, hb, "hq7")
        y = ups[7][:, 0:2 * TOK]
        nc.scalar.copy(y, acc[:])
        cols = place[:, 5 * TOK // PER_COL:7 * TOK // PER_COL]
        nc.vector.tensor_tensor(win[0][:].indirect(cols), y, wgo_sb[:, 5 * TOK:7 * TOK], MULT)

        for n, t0, t1 in LAST:
            acc = second_layer([(n, t0, t1)], f"bank{n}")
            y = g0[:, n, 0:TOK * (t1 - t0)]
            nc.scalar.copy(y, acc[:])
            cols = place[:, TOK * t0 // PER_COL:TOK * t1 // PER_COL]
            nc.vector.tensor_tensor(win[n][:].indirect(cols), y, wgo_sb[:, TOK * t0:TOK * t1], MULT)
            nc.sync.dma_start(out=out[P * n:P * (n + 1), :], in_=win[n][:])
